import numpy as np
import ml_dtypes


def mxq(x, axis, fmt="e4m3"):
    dtype, down = {"e4m3": (ml_dtypes.float8_e4m3fn, 7), "e5m2": (ml_dtypes.float8_e5m2, 14)}[fmt]
    v = np.moveaxis(np.asarray(x, np.float32).astype(ml_dtypes.bfloat16).astype(np.float64), axis, -1)
    blocks = v.reshape(v.shape[:-1] + (-1, 32))
    amax = np.abs(blocks).max(-1, keepdims=True)
    byte = np.maximum(np.where(amax > 0, np.frexp(amax)[1] - 1 + 127, 0) - down, 1)
    scale = np.exp2(byte - 127.0)
    codes = (blocks / scale).astype(np.float32).astype(dtype).astype(np.float64)
    return np.moveaxis((codes * scale).reshape(v.shape), -1, axis)


WIDE = False


def mx_kscale(k):
    if not WIDE:
        return np.ones(k)
    levels = np.array([24, -24, 12, -12, 0])
    if k % 512:
        return np.exp2(np.random.permutation(np.resize(levels, k // 32))).repeat(32)
    a = np.empty((k // 512, 16))
    for p in range(k // 512):
        a[p, :8] = np.random.permutation(np.resize(levels, 8))
        for g in range(8):
            far = levels[np.abs(levels - a[p, g]) >= 10]
            a[p, g + 8] = far[np.random.randint(len(far))]
    return np.exp2(a.ravel()).repeat(32)


def f64(x):
    return np.asarray(x).astype(np.float64)


def striped(idx):
    return np.tile(idx.reshape(-1, 16).T, (8, 1)).astype(np.uint16)


def unstriped(offs):
    return offs[:16].T.reshape(-1).astype(np.int64)


E2M1 = np.array([0.0, 0.5, 1.0, 1.5, 2.0, 3.0, 4.0, 6.0, -0.0, -0.5, -1.0, -1.5, -2.0, -3.0, -4.0, -6.0])


def pack_weight(w, fmt):
    k, n = w.shape
    w = f64(np.asarray(w, np.float32).astype(ml_dtypes.bfloat16)).reshape(k // 32, 32, n)
    amax = np.abs(w).max(1)
    if fmt == "e4m3":
        byte = np.frexp(amax)[1] - 1 + 127 - 7
    else:
        mant, ex = np.frexp(amax / 6.0)
        byte = np.where(mant > 0.5, ex, ex - 1) + 127
    byte = np.clip(np.where(amax > 0, byte, 1), 1, 254)
    scaled = (w * np.exp2(127.0 - byte)[:, None, :]).reshape(k, n).astype(np.float32)
    by_word = np.ascontiguousarray(scaled.reshape(k // 512, 128, 4, n).transpose(0, 1, 3, 2))
    if fmt == "e4m3":
        words = by_word.astype(ml_dtypes.float8_e4m3fn).view(np.uint8)
    else:
        c = by_word.astype(ml_dtypes.float4_e2m1fn).view(np.uint8) & 0xF
        words = (c[..., 0::2] | (c[..., 1::2] << 4)).reshape(k // 512, 128, 2 * n)
    return np.ascontiguousarray(words), np.ascontiguousarray(byte.astype(np.uint8).reshape(k // 512, 16, n))


def unpack_weight(words, scales, fmt):
    g, _, n = scales.shape
    words = np.ascontiguousarray(words).reshape(g, 128, n, -1)
    if fmt == "e4m3":
        vals = words.view(ml_dtypes.float8_e4m3fn).astype(np.float64)
    else:
        nib = np.empty((g, 128, n, 4), np.uint8)
        nib[..., 0::2] = words & 0xF
        nib[..., 1::2] = words >> 4
        vals = E2M1[nib]
    vals = vals * np.repeat(np.exp2(scales.astype(np.float64) - 127.0), 8, axis=1)[..., None]
    return vals.transpose(0, 1, 3, 2).reshape(g * 512, n)


def gelu(f):
    return 0.5 * f * (1.0 + np.tanh(np.sqrt(2.0 / np.pi) * (f + 0.044715 * f**3)))


K, R, N, T, J = 512, 1024, 256, 4096, 1024


def setup_inputs():
    n = np.random.standard_normal
    s = mx_kscale(K)[:, None]
    u = mx_kscale(R)[:, None]
    p_tab = pack_weight(n((K, T)) * s, "e4m3")
    p_w0 = pack_weight(n((K, R)) / np.sqrt(3 * K) / s, "e4m3")
    p_w1 = pack_weight(n((K, R)) / np.sqrt(3 * K) / s, "e4m3")
    p_w2 = pack_weight(n((K, R)) / np.sqrt(3 * K) / s, "e4m3")
    p_wd = pack_weight(n((R, N)) / np.sqrt(R) / u, "e2m1")
    return {
        "tab_words": p_tab[0],
        "tab_scales": p_tab[1],
        "w0_words": p_w0[0],
        "w0_scales": p_w0[1],
        "w1_words": p_w1[0],
        "w1_scales": p_w1[1],
        "w2_words": p_w2[0],
        "w2_scales": p_w2[1],
        "sm": (np.random.uniform(0.5, 2.0, R) * u[:, 0]).astype(np.float32),
        "wd_words": p_wd[0],
        "wd_scales": p_wd[1],
        "offs": striped(np.concatenate([np.random.permutation(T)[:J] for _ in range(3)])),
    }


def reference(tab_words, tab_scales, w0_words, w0_scales, w1_words, w1_scales, w2_words, w2_scales, sm, wd_words, wd_scales, offs):
    idx = unstriped(offs).reshape(3, J)
    tab_ = unpack_weight(tab_words, tab_scales, "e4m3")[:, idx]
    w0_ = unpack_weight(w0_words, w0_scales, "e4m3")
    w1_ = unpack_weight(w1_words, w1_scales, "e4m3")
    w2_ = unpack_weight(w2_words, w2_scales, "e4m3")
    a = w0_.T @ tab_[:, 0] + w1_.T @ tab_[:, 1] + w2_.T @ tab_[:, 2]
    h = f64(sm)[:, None] * gelu(a)
    h_ = mxq(h, 0, "e4m3")
    wd_ = unpack_weight(wd_words, wd_scales, "e2m1")
    y = wd_.T @ h_
    return y

@@ -1,0 +1,212 @@
+from contextlib import ExitStack
+
+import concourse.mybir as mybir
+
+K, R, N, T, J = 512, 1024, 256, 4096, 1024
+FLOPS = 2 * 3 * K * R * J + 2 * R * N * J
+
+F32 = mybir.dt.float32
+BF16 = mybir.dt.bfloat16
+I32 = mybir.dt.int32
+U32 = mybir.dt.uint32
+U16 = mybir.dt.uint16
+U8 = mybir.dt.uint8
+FP8X4 = mybir.dt.float8_e4m3fn_x4
+FP4X4 = mybir.dt.float4_e2m1fn_x4
+GELU = mybir.ActivationFunctionType.Gelu_apprx_tanh
+MULT = mybir.AluOpType.mult
+
+P = 128
+HALF = 512
+CHUNK = 256
+WS_ON_SYNC = 3
+WS_ON_SCALAR = 4
+
+
+def tile_list_rvq_gelu_none_kernel(tc, tab_words, tab_scales, w0_words, w0_scales, w1_words, w1_scales,
+        w2_words, w2_scales, sm, wd_words, wd_scales, offs, out):
+    nc = tc.nc
+    w_words = (w0_words, w1_words, w2_words)
+    w_scales = (w0_scales, w1_scales, w2_scales)
+    with ExitStack() as ctx:
+        keep = ctx.enter_context(tc.tile_pool(name="keep", bufs=1))
+        lay = ctx.enter_context(tc.tile_pool(name="lay", bufs=1))
+        psum = ctx.enter_context(tc.psum_pool(name="psum", bufs=1))
+
+        offsets = keep.tile([P, 3 * J // 16], U16, name="offsets")
+        nc.sync.dma_start(offsets[:], offs)
+
+        tab_plane = keep.tile([P, T], U8, name="tab_plane", align_bytes=256)
+        at_tab, at_wd, at_wds, at_sm = 0, 16384, 17408, 17920
+        at_w = (33536, 18176, 22272)
+        at_ws = at_w[0] + 4096
+        ws_raw = lay.tile([P, R], U8, name="ws_raw", offset=at_ws, align_bytes=256)
+        nc.vector.memset(tab_plane[:].bitcast(I32), 0)
+        nc.vector.memset(ws_raw[:].bitcast(I32), 0)
+
+        warm = lay.tile([P, at_ws // 4], F32, name="warm", offset=0, align_bytes=256)
+        nc.gpsimd.memset(warm[:, 0:8], 0.0)
+        nc.scalar.activation(warm[:, 8:16], warm[:, 0:8], GELU)
+
+        for q in range(4):
+            nc.sync.dma_start(tab_plane[32 * q : 32 * q + 4, :].bitcast(I32), tab_scales[0, 4 * q : 4 * q + 4, :].bitcast(I32))
+        for g in range(3):
+            for q in range(4):
+                eng = nc.sync if 4 * g + q < WS_ON_SYNC else (nc.scalar if 4 * g + q < WS_ON_SYNC + WS_ON_SCALAR else nc.gpsimd)
+                row = 32 * q + 4 * (g + 1)
+                eng.dma_start(ws_raw[row : row + 4, :].bitcast(I32), w_scales[g][0, 4 * q : 4 * q + 4, :].bitcast(I32))
+
+        tab = lay.tile([P, T], I32, name="tab", offset=at_tab, align_bytes=256)
+        nc.sync.dma_start(tab[:], tab_words[0].rearrange("p t i -> p (t i)").bitcast(I32))
+        w_raw = []
+        for g in range(3):
+            raw = lay.tile([P, R], I32, name="w_raw%d" % g, offset=at_w[g], align_bytes=256)
+            nc.sync.dma_start(raw[:], w_words[g][0].rearrange("p r i -> p (r i)").bitcast(I32))
+            w_raw.append(raw)
+        sm_t = lay.tile([P, 2, 4], F32, name="sm_t", offset=at_sm, align_bytes=256)
+        nc.sync.dma_start(sm_t[:], sm.rearrange("(b p t) -> p b t", b=2, t=4))
+        wd = lay.tile([P, 2 * 2 * N], U8, name="wd", offset=at_wd, align_bytes=256)
+        nc.sync.dma_start(wd[:].bitcast(I32).rearrange("p (a c) -> p a c", a=2), wd_words.bitcast(I32).rearrange("a p c -> p a c"))
+        wd_plane = lay.tile([P, 2 * N], U8, name="wd_plane", offset=at_wds, align_bytes=256)
+        nc.gpsimd.memset(wd_plane[:].bitcast(I32), 0)
+        for q in range(4):
+            nc.sync.dma_start(
+                wd_plane[32 * q : 32 * q + 4, :].bitcast(I32).rearrange("p (a c) -> p a c", a=2),
+                wd_scales[:, 4 * q : 4 * q + 4, :].bitcast(I32).rearrange("a r c -> r a c"),
+            )
+
+        def entries(half, g):
+            c0 = (J * g + HALF * half) // 16
+            return offsets[:, c0 : c0 + HALF // 16]
+
+        def gather_plane(dst, half, g):
+            nc.vector.tensor_copy(dst, tab_plane[:].indirect(entries(half, g)))
+
+        def gather_words(dst, half, g):
+            nc.vector.tensor_copy(dst, tab[:].bitcast(U32).indirect(entries(half, g)))
+
+        def sort_columns(dst, src):
+            nc.vector.tensor_copy(dst.rearrange("p (b t m) -> p b m t", b=2, t=4), src.rearrange("p (b m t) -> p b m t", b=2, t=4))
+
+        gs = {}
+        gw = {}
+        for half, g in ((0, 0), (0, 1), (0, 2), (1, 0)):
+            t_ = keep.tile([P, HALF], U8, name="gs%d%d" % (half, g), align_bytes=256)
+            gs[half, g] = t_[:]
+            gather_plane(gs[half, g], half, g)
+        ws = keep.tile([P, R], U8, name="ws", align_bytes=256)
+        w = []
+        for g in range(3):
+            if g == 0:
+                t_ = keep.tile([P, HALF], U32, name="gw00", align_bytes=256)
+            else:
+                t_ = lay.tile([P, HALF], U32, name="gw0%d" % g, offset=(at_ws - 1536 if g == 1 else at_w[1]), align_bytes=256)
+            gw[0, g] = t_[:]
+            gather_words(gw[0, g], 0, g)
+            if g == 0:
+                sort_columns(ws[:], ws_raw[:])
+            if g == 1:
+                wg = lay.tile([P, R], I32, name="w1", offset=at_ws + 512, align_bytes=256)
+            else:
+                wg = keep.tile([P, R], I32, name="w%d" % g, align_bytes=256)
+            sort_columns(wg[:], w_raw[g][:])
+            w.append(wg)
+        gs_late = lay.tile([P, 2 * HALF], U8, name="gs_late", offset=at_w[2], align_bytes=256)
+        gw_late = lay.tile([P, 3 * HALF], U32, name="gw_late", offset=at_w[2] + 1024, align_bytes=256)
+        for g in range(3):
+            if g > 0:
+                gs[1, g] = gs_late[:, (g - 1) * HALF : g * HALF]
+                gather_plane(gs[1, g], 1, g)
+            gw[1, g] = gw_late[:, g * HALF : (g + 1) * HALF]
+            gather_words(gw[1, g], 1, g)
+
+        banks = {}
+        acts = {}
+        codes = {}
+        planes = {}
+
+        def place(unit):
+            return unit // 8, (unit // 4) % 2, (unit // 2) % 2, unit % 2
+
+        def passes(unit, g):
+            half, jq, b, u = place(unit)
+            if g == 0:
+                banks[unit] = psum.tile([P, 2 * CHUNK], F32, name="a%d" % unit, tag="bank%d" % (unit % 8))
+            cols = slice(jq * CHUNK, (jq + 1) * CHUNK)
+            for e in range(2):
+                r0 = 512 * b + 128 * (2 * u + e)
+                nc.tensor.matmul_mx(
+                    out=banks[unit][:, e * CHUNK : (e + 1) * CHUNK],
+                    lhsT=w[g][:, r0 : r0 + 128].bitcast(FP8X4),
+                    lhsT_scale=ws[4 * (g + 1) : P, r0 : r0 + 128],
+                    rhs=gw[half, g][:, cols].bitcast(FP8X4),
+                    rhs_scale=gs[half, g][:, cols],
+                    start=(g == 0 and e == 0),
+                    stop=(g == 2 and e == 1),
+                )
+
+        def activate(unit):
+            pair = unit // 2
+            if unit % 2 == 0:
+                acts[pair] = keep.tile([P, 2, CHUNK, 2], F32, name="act%d" % pair, align_bytes=256)
+            nc.scalar.activation(acts[pair][:, unit % 2, :, :], banks[unit][:].rearrange("p (e j) -> p j e", e=2), GELU)
+
+        hbs = {}
+
+        def smooth(pair, j0, j1):
+            if j0 == 0:
+                hbs[pair] = keep.tile([P, 4 * CHUNK], BF16, name="hb%d" % pair, align_bytes=256)
+            nc.vector.tensor_tensor(
+                hbs[pair][:, 4 * j0 : 4 * j1].rearrange("p (j u e) -> p j u e", u=2, e=2),
+                acts[pair][:, :, j0:j1, :].rearrange("p u j e -> p j u e"),
+                sm_t[:, pair % 2, :].rearrange("p (u e) -> p u e", u=2).unsqueeze(1).to_broadcast([P, j1 - j0, 2, 2]),
+                MULT,
+            )
+
+        def quantise(pair, j0, j1):
+            if j0 == 0:
+                codes[pair] = keep.tile([P, CHUNK], U32, name="codes%d" % pair, align_bytes=256)
+                planes[pair] = keep.tile([P, CHUNK], U8, name="plane%d" % pair, align_bytes=256)
+            nc.vector.quantize_mx(out=codes[pair][:, j0:j1].bitcast(FP8X4), scales=planes[pair][:, j0:j1], in_=hbs[pair][:, 4 * j0 : 4 * j1])
+
+        out_v = out.rearrange("(nt p) j -> p nt j", p=P)
+
+        def second_layer(chunk, j0, j1, bank):
+            width = j1 - j0
+            y = psum.tile([P, 2 * width], F32, name="y%d_%d" % (chunk, j0), tag="bank%d" % bank)
+            blocks = [(b, nt, j) for b in range(2) for nt in range(2) for j in range(j0, j1, 128)]
+            for b, nt, j in blocks:
+                pair = 2 * chunk + b
+                nc.tensor.matmul_mx(
+                    out=y[:, nt * width + j - j0 : nt * width + j - j0 + 128],
+                    lhsT=wd[:, 512 * b + 256 * nt : 512 * b + 256 * (nt + 1)].bitcast(FP4X4),
+                    lhsT_scale=wd_plane[:, 256 * b + 128 * nt : 256 * b + 128 * (nt + 1)],
+                    rhs=codes[pair][:, j : j + 128].bitcast(FP8X4),
+                    rhs_scale=planes[pair][:, j : j + 128],
+                    start=((b, nt, j) == blocks[0]),
+                    stop=((b, nt, j) == blocks[-1]),
+                )
+            res = keep.tile([P, 2, width], F32, name="res%d_%d" % (chunk, j0), align_bytes=256)
+            nc.scalar.copy(res[:], y[:].rearrange("p (nt j) -> p nt j", nt=2))
+            nc.sync.dma_start(out_v[:, :, chunk * CHUNK + j0 : chunk * CHUNK + j1], res[:])
+
+        for unit in range(8):
+            passes(unit, 0)
+        for unit in range(16):
+            for g in range(0 if unit >= 8 else 1, 3):
+                passes(unit, g)
+            activate(unit)
+            if unit % 2 == 1 and unit < 15:
+                smooth(unit // 2, 0, CHUNK)
+                if unit > 1:
+                    quantise(unit // 2 - 1, 0, CHUNK)
+            if unit in (11, 13):
+                second_layer((unit - 11) // 2, 0, CHUNK, (unit - 11) // 2)
+        smooth(7, 0, 128)
+        quantise(6, 0, CHUNK)
+        second_layer(2, 0, CHUNK, 2)
+        smooth(7, 128, CHUNK)
+        quantise(7, 0, 128)
+        second_layer(3, 0, 128, 3)
+        quantise(7, 128, CHUNK)
+        second_layer(3, 128, CHUNK, 4)

@@ -85,8 +85,14 @@ def tile_list_rvq_gelu_none_kernel(tc, tab_words, tab_scales, w0_words, w0_scale
         def gather_words(dst, half, g):
             nc.vector.tensor_copy(dst, tab[:].bitcast(U32).indirect(entries(half, g)))
 
-        def sort_columns(dst, src):
-            nc.vector.tensor_copy(dst.rearrange("p (b t m) -> p b m t", b=2, t=4), src.rearrange("p (b m t) -> p b m t", b=2, t=4))
+        def sort_words(dst, src):
+            nc.vector.tensor_copy(
+                dst.rearrange("p (b t c i) -> p b c t i", b=2, t=4, i=4),
+                src.rearrange("p (b c i t) -> p b c t i", b=2, t=4, i=4),
+            )
+
+        def sort_bytes(dst, src):
+            nc.vector.tensor_copy(dst.rearrange("p (b t m) -> p b t m", b=2, t=4), src.rearrange("p (b m t) -> p b t m", b=2, t=4))
 
         gs = {}
         gw = {}
@@ -104,12 +110,12 @@ def tile_list_rvq_gelu_none_kernel(tc, tab_words, tab_scales, w0_words, w0_scale
             gw[0, g] = t_[:]
             gather_words(gw[0, g], 0, g)
             if g == 0:
-                sort_columns(ws[:], ws_raw[:])
+                sort_bytes(ws[:], ws_raw[:])
             if g == 1:
                 wg = lay.tile([P, R], I32, name="w1", offset=at_ws + 512, align_bytes=256)
             else:
                 wg = keep.tile([P, R], I32, name="w%d" % g, align_bytes=256)
-            sort_columns(wg[:], w_raw[g][:])
+            sort_words(wg[:], w_raw[g][:])
             w.append(wg)
         gs_late = lay.tile([P, 2 * HALF], U8, name="gs_late", offset=at_w[2], align_bytes=256)
         gw_late = lay.tile([P, 3 * HALF], U32, name="gw_late", offset=at_w[2] + 1024, align_bytes=256)

@@ -14,13 +14,12 @@ U8 = mybir.dt.uint8
 FP8X4 = mybir.dt.float8_e4m3fn_x4
 FP4X4 = mybir.dt.float4_e2m1fn_x4
 GELU = mybir.ActivationFunctionType.Gelu_apprx_tanh
+COPY = mybir.ActivationFunctionType.Copy
 MULT = mybir.AluOpType.mult
 
 P = 128
 HALF = 512
 CHUNK = 256
-WS_ON_SYNC = 3
-WS_ON_SCALAR = 4
 
 
 def tile_list_rvq_gelu_none_kernel(tc, tab_words, tab_scales, w0_words, w0_scales, w1_words, w1_scales,
@@ -38,37 +37,47 @@ def tile_list_rvq_gelu_none_kernel(tc, tab_words, tab_scales, w0_words, w0_scale
 
         tab_plane = keep.tile([P, T], U8, name="tab_plane", align_bytes=256)
         at_tab, at_wd, at_wds, at_sm = 0, 16384, 17408, 17920
-        at_w = (33536, 18176, 22272)
-        at_ws = at_w[0] + 4096
-        ws_raw = lay.tile([P, R], U8, name="ws_raw", offset=at_ws, align_bytes=256)
-        nc.vector.memset(tab_plane[:].bitcast(I32), 0)
-        nc.vector.memset(ws_raw[:].bitcast(I32), 0)
+        at_w = {(1, 0): 19200, (2, 0): 22272, (0, 1): 24832, (1, 1): 26880, (2, 1): 28928, (0, 0): 36096}
+        raw_cols = {(2, 0): 640, (0, 0): 1024}
+        at_ws = at_w[0, 0] + 4096
+        wsx = lay.tile([P, 1536 + R], U8, name="wsx", offset=at_ws, align_bytes=256)
 
         warm = lay.tile([P, at_ws // 4], F32, name="warm", offset=0, align_bytes=256)
+        nc.gpsimd.memset(tab_plane[:, 0 : T // 2].bitcast(I32), 0)
         nc.gpsimd.memset(warm[:, 0:8], 0.0)
         nc.scalar.activation(warm[:, 8:16], warm[:, 0:8], GELU)
+        nc.gpsimd.memset(wsx[32:64, 1536:].bitcast(I32), 0)
+        nc.vector.memset(tab_plane[:, T // 2 : T].bitcast(I32), 0)
+        nc.vector.memset(wsx[0:32, 1536:].bitcast(I32), 0)
+        nc.vector.memset(wsx[64:128, 1536:].bitcast(I32), 0)
+
+        def load_w_scales(eng, q):
+            for g in range(3):
+                row = 32 * q + 4 * (g + 1)
+                eng.dma_start(wsx[row : row + 4, 1536:].bitcast(I32), w_scales[g][0, 4 * q : 4 * q + 4, :].bitcast(I32))
+
+        def load_w(g, b):
+            raw = lay.tile([P, raw_cols.get((g, b), 512)], I32, name="w_raw%d%d" % (g, b), offset=at_w[g, b], align_bytes=256)
+            nc.sync.dma_start(raw[:, 0:512], w_words[g][0].rearrange("p r i -> p (r i)")[:, 2048 * b : 2048 * (b + 1)].bitcast(I32))
+            return raw
 
         for q in range(4):
             nc.sync.dma_start(tab_plane[32 * q : 32 * q + 4, :].bitcast(I32), tab_scales[0, 4 * q : 4 * q + 4, :].bitcast(I32))
-        for g in range(3):
-            for q in range(4):
-                eng = nc.sync if 4 * g + q < WS_ON_SYNC else (nc.scalar if 4 * g + q < WS_ON_SYNC + WS_ON_SCALAR else nc.gpsimd)
-                row = 32 * q + 4 * (g + 1)
-                eng.dma_start(ws_raw[row : row + 4, :].bitcast(I32), w_scales[g][0, 4 * q : 4 * q + 4, :].bitcast(I32))
-
+        load_w_scales(nc.sync, 0)
+        load_w_scales(nc.gpsimd, 1)
         tab = lay.tile([P, T], I32, name="tab", offset=at_tab, align_bytes=256)
         nc.sync.dma_start(tab[:], tab_words[0].rearrange("p t i -> p (t i)").bitcast(I32))
-        w_raw = []
-        for g in range(3):
-            raw = lay.tile([P, R], I32, name="w_raw%d" % g, offset=at_w[g], align_bytes=256)
-            nc.sync.dma_start(raw[:], w_words[g][0].rearrange("p r i -> p (r i)").bitcast(I32))
-            w_raw.append(raw)
+        load_w_scales(nc.sync, 2)
+        load_w_scales(nc.sync, 3)
+        w_raw = {(g, 0): load_w(g, 0) for g in range(3)}
         sm_t = lay.tile([P, 2, 4], F32, name="sm_t", offset=at_sm, align_bytes=256)
         nc.sync.dma_start(sm_t[:], sm.rearrange("(b p t) -> p b t", b=2, t=4))
+        for g in range(3):
+            w_raw[g, 1] = load_w(g, 1)
         wd = lay.tile([P, 2 * 2 * N], U8, name="wd", offset=at_wd, align_bytes=256)
         nc.sync.dma_start(wd[:].bitcast(I32).rearrange("p (a c) -> p a c", a=2), wd_words.bitcast(I32).rearrange("a p c -> p a c"))
         wd_plane = lay.tile([P, 2 * N], U8, name="wd_plane", offset=at_wds, align_bytes=256)
-        nc.gpsimd.memset(wd_plane[:].bitcast(I32), 0)
+        nc.vector.memset(wd_plane[:].bitcast(I32), 0)
         for q in range(4):
             nc.sync.dma_start(
                 wd_plane[32 * q : 32 * q + 4, :].bitcast(I32).rearrange("p (a c) -> p a c", a=2),
@@ -87,12 +96,12 @@ def tile_list_rvq_gelu_none_kernel(tc, tab_words, tab_scales, w0_words, w0_scale
 
         def sort_words(dst, src):
             nc.vector.tensor_copy(
-                dst.rearrange("p (b t c i) -> p b c t i", b=2, t=4, i=4),
-                src.rearrange("p (b c i t) -> p b c t i", b=2, t=4, i=4),
+                dst.rearrange("p (t c i) -> p c t i", t=4, i=4),
+                src.rearrange("p (c i t) -> p c t i", t=4, i=4),
             )
 
         def sort_bytes(dst, src):
-            nc.vector.tensor_copy(dst.rearrange("p (b t m) -> p b t m", b=2, t=4), src.rearrange("p (b m t) -> p b t m", b=2, t=4))
+            nc.vector.tensor_copy(dst.rearrange("p (t m) -> p t m", t=4), src.rearrange("p (m t) -> p t m", t=4))
 
         gs = {}
         gw = {}
@@ -100,25 +109,37 @@ def tile_list_rvq_gelu_none_kernel(tc, tab_words, tab_scales, w0_words, w0_scale
             t_ = keep.tile([P, HALF], U8, name="gs%d%d" % (half, g), align_bytes=256)
             gs[half, g] = t_[:]
             gather_plane(gs[half, g], half, g)
-        ws = keep.tile([P, R], U8, name="ws", align_bytes=256)
-        w = []
+        ws = [
+            keep.tile([P, 512], U8, name="ws0", align_bytes=256),
+            lay.tile([P, 512], U8, name="ws1", offset=at_w[2, 0] + 2048, align_bytes=256),
+        ]
+        w = {}
+        at_gw = (None, at_w[0, 0], at_w[1, 0] - 1024)
+        at_sorted = {(1, 0): at_w[0, 0] + 2048, (2, 0): at_w[1, 0] + 1024, (0, 1): at_w[2, 0], (1, 1): at_w[0, 1], (2, 1): at_w[1, 1]}
+
+        def sort_w(g, b):
+            if (g, b) == (0, 0):
+                w[g, b] = wsx[:, 0:2048].bitcast(I32)
+            else:
+                t_ = lay.tile([P, 512], I32, name="w%d%d" % (g, b), offset=at_sorted[g, b], align_bytes=256)
+                w[g, b] = t_[:]
+            sort_words(w[g, b], w_raw[g, b][:, 0:512])
+
         for g in range(3):
             if g == 0:
                 t_ = keep.tile([P, HALF], U32, name="gw00", align_bytes=256)
             else:
-                t_ = lay.tile([P, HALF], U32, name="gw0%d" % g, offset=(at_ws - 1536 if g == 1 else at_w[1]), align_bytes=256)
+                t_ = lay.tile([P, HALF], U32, name="gw0%d" % g, offset=at_gw[g], align_bytes=256)
             gw[0, g] = t_[:]
             gather_words(gw[0, g], 0, g)
             if g == 0:
-                sort_bytes(ws[:], ws_raw[:])
-            if g == 1:
-                wg = lay.tile([P, R], I32, name="w1", offset=at_ws + 512, align_bytes=256)
-            else:
-                wg = keep.tile([P, R], I32, name="w%d" % g, align_bytes=256)
-            sort_words(wg[:], w_raw[g][:])
-            w.append(wg)
-        gs_late = lay.tile([P, 2 * HALF], U8, name="gs_late", offset=at_w[2], align_bytes=256)
-        gw_late = lay.tile([P, 3 * HALF], U32, name="gw_late", offset=at_w[2] + 1024, align_bytes=256)
+                sort_bytes(ws[0][:], wsx[:, 1536:2048])
+            sort_w(g, 0)
+        sort_bytes(ws[1][:], wsx[:, 2048:2560])
+        for g in range(3):
+            sort_w(g, 1)
+        gs_late = lay.tile([P, 2 * HALF], U8, name="gs_late", offset=at_w[2, 1], align_bytes=256)
+        gw_late = lay.tile([P, 3 * HALF], U32, name="gw_late", offset=at_w[2, 1] + 1024, align_bytes=256)
         for g in range(3):
             if g > 0:
                 gs[1, g] = gs_late[:, (g - 1) * HALF : g * HALF]
@@ -134,17 +155,19 @@ def tile_list_rvq_gelu_none_kernel(tc, tab_words, tab_scales, w0_words, w0_scale
         def place(unit):
             return unit // 8, (unit // 4) % 2, (unit // 2) % 2, unit % 2
 
+        bank_of = {2: 4, 3: 5, 6: 6, 7: 7}
+
         def passes(unit, g):
             half, jq, b, u = place(unit)
             if g == 0:
-                banks[unit] = psum.tile([P, 2 * CHUNK], F32, name="a%d" % unit, tag="bank%d" % (unit % 8))
+                banks[unit] = psum.tile([P, 2 * CHUNK], F32, name="a%d" % unit, tag="bank%d" % bank_of.get(unit, unit % 8))
             cols = slice(jq * CHUNK, (jq + 1) * CHUNK)
             for e in range(2):
-                r0 = 512 * b + 128 * (2 * u + e)
+                r0 = 128 * (2 * u + e)
                 nc.tensor.matmul_mx(
                     out=banks[unit][:, e * CHUNK : (e + 1) * CHUNK],
-                    lhsT=w[g][:, r0 : r0 + 128].bitcast(FP8X4),
-                    lhsT_scale=ws[4 * (g + 1) : P, r0 : r0 + 128],
+                    lhsT=w[g, b][:, r0 : r0 + 128].bitcast(FP8X4),
+                    lhsT_scale=ws[b][4 * (g + 1) : P, r0 : r0 + 128],
                     rhs=gw[half, g][:, cols].bitcast(FP8X4),
                     rhs_scale=gs[half, g][:, cols],
                     start=(g == 0 and e == 0),
@@ -169,10 +192,73 @@ def tile_list_rvq_gelu_none_kernel(tc, tab_words, tab_scales, w0_words, w0_scale
                 MULT,
             )
 
-        def quantise(pair, j0, j1):
+        narrow = {}
+
+        def narrow_passes(half, b, q, g, bank):
+            if g == 0:
+                narrow[half, q] = psum.tile([P, 4 * 128], F32, name="n%d%d" % (half, q), tag="bank%d" % bank)
+            cols = slice(q * 128, (q + 1) * 128)
+            for t in range(4):
+                nc.tensor.matmul_mx(
+                    out=narrow[half, q][:, t * 128 : (t + 1) * 128],
+                    lhsT=w[g, b][:, 128 * t : 128 * (t + 1)].bitcast(FP8X4),
+                    lhsT_scale=ws[b][4 * (g + 1) : P, 128 * t : 128 * (t + 1)],
+                    rhs=gw[half, g][:, cols].bitcast(FP8X4),
+                    rhs_scale=gs[half, g][:, cols],
+                    start=(g == 0 and t == 0),
+                    stop=(g == 2 and t == 3),
+                )
+
+        sm_wide = keep.tile([P, 128, 4], F32, name="sm_wide", align_bytes=256)
+        nc.scalar.copy(sm_wide[:], sm_t[:, 0, :].unsqueeze(1).to_broadcast([P, 128, 4]))
+
+        def narrow_activate(half, q):
+            act = keep.tile([P, 128, 4], F32, name="nact%d%d" % (half, q), align_bytes=256)
+            nc.scalar.activation(act[:], narrow[half, q][:].rearrange("p (t j) -> p j t", t=4), GELU)
+            return act
+
+        def narrow_finish(q):
+            pair = 2 * (q // 2)
+            act = narrow_activate(0, q)
+            if q % 2 == 0:
+                hbs[pair] = keep.tile([P, 4 * CHUNK], BF16, name="hb%d" % pair, align_bytes=256)
+            nc.gpsimd.tensor_tensor(
+                hbs[pair][:, 512 * (q % 2) : 512 * (q % 2 + 1)], act[:].rearrange("p j t -> p (j t)"), sm_wide[:].rearrange("p j t -> p (j t)"), MULT
+            )
+
+        def narrow_smooth(act, j0):
             if j0 == 0:
-                codes[pair] = keep.tile([P, CHUNK], U32, name="codes%d" % pair, align_bytes=256)
-                planes[pair] = keep.tile([P, CHUNK], U8, name="plane%d" % pair, align_bytes=256)
+                hbs[7] = keep.tile([P, 4 * CHUNK], BF16, name="hb7", align_bytes=256)
+            nc.vector.tensor_tensor(
+                hbs[7][:, 4 * j0 : 4 * j0 + 512].rearrange("p (j t) -> p j t", t=4),
+                act[:],
+                sm_t[:, 1, :].unsqueeze(1).to_broadcast([P, 128, 4]),
+                MULT,
+            )
+
+        def smooth_on_scalar(pair):
+            hp = keep.tile([P, 4, CHUNK], BF16, name="hp%d" % pair, align_bytes=256)
+            for t in range(4):
+                nc.scalar.activation(hp[:, t, :], acts[pair][:, t // 2, :, t % 2], COPY, scale=sm_t[:, pair % 2, t : t + 1])
+            hbs[pair] = keep.tile([P, 4 * CHUNK], BF16, name="hb%d" % pair, align_bytes=256)
+            nc.scalar.copy(
+                hbs[pair][:].rearrange("p (c i t) -> p c t i", i=4, t=4),
+                hp[:].rearrange("p t (c i) -> p c t i", i=4),
+            )
+
+        wide_codes = [keep.tile([P, HALF], U32, name="wcodes%d" % b, align_bytes=256) for b in range(2)]
+        wide_planes = [keep.tile([P, HALF], U8, name="wplane%d" % b, align_bytes=256) for b in range(2)]
+
+        def quantise(pair, j0, j1):
+            if pair < 4:
+                c0 = CHUNK * (pair // 2)
+                codes[pair] = wide_codes[pair % 2][:, c0 : c0 + CHUNK]
+                planes[pair] = wide_planes[pair % 2][:, c0 : c0 + CHUNK]
+            elif j0 == 0:
+                ct = keep.tile([P, CHUNK], U32, name="codes%d" % pair, align_bytes=256)
+                pt = keep.tile([P, CHUNK], U8, name="plane%d" % pair, align_bytes=256)
+                codes[pair] = ct[:]
+                planes[pair] = pt[:]
             nc.vector.quantize_mx(out=codes[pair][:, j0:j1].bitcast(FP8X4), scales=planes[pair][:, j0:j1], in_=hbs[pair][:, 4 * j0 : 4 * j1])
 
         out_v = out.rearrange("(nt p) j -> p nt j", p=P)
@@ -196,22 +282,62 @@ def tile_list_rvq_gelu_none_kernel(tc, tab_words, tab_scales, w0_words, w0_scale
             nc.scalar.copy(res[:], y[:].rearrange("p (nt j) -> p nt j", nt=2))
             nc.sync.dma_start(out_v[:, :, chunk * CHUNK + j0 : chunk * CHUNK + j1], res[:])
 
-        for unit in range(8):
-            passes(unit, 0)
-        for unit in range(16):
-            for g in range(0 if unit >= 8 else 1, 3):
+        def second_layer_wide(nt):
+            y = psum.tile([P, HALF], F32, name="yw%d" % nt, tag="bank%d" % nt)
+            for b in range(2):
+                nc.tensor.matmul_mx(
+                    out=y[:],
+                    lhsT=wd[:, 512 * b + 256 * nt : 512 * b + 256 * (nt + 1)].bitcast(FP4X4),
+                    lhsT_scale=wd_plane[:, 256 * b + 128 * nt : 256 * b + 128 * (nt + 1)],
+                    rhs=wide_codes[b][:].bitcast(FP8X4),
+                    rhs_scale=wide_planes[b][:],
+                    start=(b == 0),
+                    stop=(b == 1),
+                )
+            res = keep.tile([P, HALF], F32, name="resw%d" % nt, align_bytes=256)
+            nc.scalar.copy(res[:], y[:])
+            nc.sync.dma_start(out[P * nt : P * (nt + 1), 0:HALF], res[:])
+
+        for g in range(2):
+            for q in range(4):
+                narrow_passes(0, 0, q, g, q)
+        for q in range(4):
+            narrow_passes(0, 0, q, 2, q)
+            narrow_finish(q)
+        for unit in (2, 3, 6, 7):
+            for g in range(3):
                 passes(unit, g)
             activate(unit)
-            if unit % 2 == 1 and unit < 15:
+        quantise(0, 0, CHUNK)
+        quantise(2, 0, CHUNK)
+        smooth(1, 0, CHUNK)
+        smooth_on_scalar(3)
+        early = (8, 9, 10, 11)
+        for g in range(2):
+            for unit in early:
+                passes(unit, g)
+        for unit in range(8, 14):
+            for g in range(2 if unit in early else 0, 3):
+                passes(unit, g)
+            activate(unit)
+            if unit == 9:
+                quantise(3, 0, CHUNK)
+                quantise(1, 0, CHUNK)
+            if unit % 2 == 1:
                 smooth(unit // 2, 0, CHUNK)
-                if unit > 1:
+                if unit > 9:
                     quantise(unit // 2 - 1, 0, CHUNK)
-            if unit in (11, 13):
-                second_layer((unit - 11) // 2, 0, CHUNK, (unit - 11) // 2)
-        smooth(7, 0, 128)
+        last = []
+        for q in (2, 3):
+            for g in range(3):
+                narrow_passes(1, 1, q, g, 4 + q)
+            last.append(narrow_activate(1, q))
+        second_layer_wide(0)
+        second_layer_wide(1)
+        narrow_smooth(last[0], 0)
         quantise(6, 0, CHUNK)
         second_layer(2, 0, CHUNK, 2)
-        smooth(7, 128, CHUNK)
+        narrow_smooth(last[1], 128)
         quantise(7, 0, 128)
         second_layer(3, 0, 128, 3)
         quantise(7, 128, CHUNK)

@@ -14,12 +14,12 @@ U8 = mybir.dt.uint8
 FP8X4 = mybir.dt.float8_e4m3fn_x4
 FP4X4 = mybir.dt.float4_e2m1fn_x4
 GELU = mybir.ActivationFunctionType.Gelu_apprx_tanh
-COPY = mybir.ActivationFunctionType.Copy
 MULT = mybir.AluOpType.mult
 
 P = 128
 HALF = 512
-CHUNK = 256
+QUARTER = 256
+ON_GPSIMD = 2
 
 
 def tile_list_rvq_gelu_none_kernel(tc, tab_words, tab_scales, w0_words, w0_scales, w1_words, w1_scales,
@@ -32,313 +32,205 @@ def tile_list_rvq_gelu_none_kernel(tc, tab_words, tab_scales, w0_words, w0_scale
         lay = ctx.enter_context(tc.tile_pool(name="lay", bufs=1))
         psum = ctx.enter_context(tc.psum_pool(name="psum", bufs=1))
 
+        def tile(shape, dtype, name, tag=None):
+            return keep.tile(shape, dtype, name=name, tag=tag or name, align_bytes=256)
+
+        def placed(shape, dtype, name, offset):
+            return lay.tile(shape, dtype, name=name, offset=offset, align_bytes=256)
+
+        at_tab = 0
+        at_w = [4 * T + 2048 * g for g in range(3)]
+        at_ws = at_w[2] + 2048 + 256
+
         offsets = keep.tile([P, 3 * J // 16], U16, name="offsets")
         nc.sync.dma_start(offsets[:], offs)
 
-        tab_plane = keep.tile([P, T], U8, name="tab_plane", align_bytes=256)
-        at_tab, at_wd, at_wds, at_sm = 0, 16384, 17408, 17920
-        at_w = {(1, 0): 19200, (2, 0): 22272, (0, 1): 24832, (1, 1): 26880, (2, 1): 28928, (0, 0): 36096}
-        raw_cols = {(2, 0): 640, (0, 0): 1024}
-        at_ws = at_w[0, 0] + 4096
-        wsx = lay.tile([P, 1536 + R], U8, name="wsx", offset=at_ws, align_bytes=256)
-
-        warm = lay.tile([P, at_ws // 4], F32, name="warm", offset=0, align_bytes=256)
+        tab_plane = tile([P, T], U8, "tab_plane")
+        ws_raw = placed([P, R], U8, "ws_raw", at_ws)
+        zeros = placed([P, 9, 128], I32, "zeros", at_w[0] - 256)
+        nc.gpsimd.memset(ws_raw[0:96, :].bitcast(I32), 0)
         nc.gpsimd.memset(tab_plane[:, 0 : T // 2].bitcast(I32), 0)
-        nc.gpsimd.memset(warm[:, 0:8], 0.0)
-        nc.scalar.activation(warm[:, 8:16], warm[:, 0:8], GELU)
-        nc.gpsimd.memset(wsx[32:64, 1536:].bitcast(I32), 0)
         nc.vector.memset(tab_plane[:, T // 2 : T].bitcast(I32), 0)
-        nc.vector.memset(wsx[0:32, 1536:].bitcast(I32), 0)
-        nc.vector.memset(wsx[64:128, 1536:].bitcast(I32), 0)
+        nc.vector.memset(zeros[96:128, 0:9:8, :], 0)
+        nc.vector.tensor_copy(ws_raw[96:128, :].bitcast(I32).rearrange("p (a c) -> p a c", a=2), zeros[96:128, 0:9:8, :])
+
+        w_raw = {}
+
+        def load_w(g, b):
+            w_raw[g, b] = placed([P, 512], I32, "w_raw%d%d" % (g, b), at_w[g])
+            nc.sync.dma_start(w_raw[g, b][:], w_words[g][0].rearrange("p r i -> p (r i)")[:, 2048 * b : 2048 * (b + 1)].bitcast(I32))
 
         def load_w_scales(eng, q):
             for g in range(3):
                 row = 32 * q + 4 * (g + 1)
-                eng.dma_start(wsx[row : row + 4, 1536:].bitcast(I32), w_scales[g][0, 4 * q : 4 * q + 4, :].bitcast(I32))
-
-        def load_w(g, b):
-            raw = lay.tile([P, raw_cols.get((g, b), 512)], I32, name="w_raw%d%d" % (g, b), offset=at_w[g, b], align_bytes=256)
-            nc.sync.dma_start(raw[:, 0:512], w_words[g][0].rearrange("p r i -> p (r i)")[:, 2048 * b : 2048 * (b + 1)].bitcast(I32))
-            return raw
+                eng.dma_start(ws_raw[row : row + 4, :].bitcast(I32), w_scales[g][0, 4 * q : 4 * q + 4, :].bitcast(I32))
 
         for q in range(4):
             nc.sync.dma_start(tab_plane[32 * q : 32 * q + 4, :].bitcast(I32), tab_scales[0, 4 * q : 4 * q + 4, :].bitcast(I32))
-        load_w_scales(nc.sync, 0)
+        load_w_scales(nc.gpsimd, 0)
         load_w_scales(nc.gpsimd, 1)
-        tab = lay.tile([P, T], I32, name="tab", offset=at_tab, align_bytes=256)
-        nc.sync.dma_start(tab[:], tab_words[0].rearrange("p t i -> p (t i)").bitcast(I32))
         load_w_scales(nc.sync, 2)
         load_w_scales(nc.sync, 3)
-        w_raw = {(g, 0): load_w(g, 0) for g in range(3)}
-        sm_t = lay.tile([P, 2, 4], F32, name="sm_t", offset=at_sm, align_bytes=256)
-        nc.sync.dma_start(sm_t[:], sm.rearrange("(b p t) -> p b t", b=2, t=4))
+        tab = placed([P, T], I32, "tab", at_tab)
+        nc.sync.dma_start(tab[:], tab_words[0].rearrange("p t i -> p (t i)").bitcast(I32))
         for g in range(3):
-            w_raw[g, 1] = load_w(g, 1)
-        wd = lay.tile([P, 2 * 2 * N], U8, name="wd", offset=at_wd, align_bytes=256)
+            load_w(g, 0)
+
+        def entries(half, g):
+            c0 = (J * g + HALF * half) // 16
+            return offsets[:, c0 : c0 + HALF // 16]
+
+        gs = {}
+        gw = {}
+
+        def gather_plane(half, g, offset=None):
+            name = "gs%d%d" % (half, g)
+            gs[half, g] = tile([P, HALF], U8, name) if offset is None else placed([P, HALF], U8, name, offset)
+            nc.vector.tensor_copy(gs[half, g][:], tab_plane[:].indirect(entries(half, g)))
+
+        def gather_words(half, g):
+            gw[half, g] = tile([P, HALF], U32, "gw%d%d" % (half, g))
+            nc.vector.tensor_copy(gw[half, g][:], tab[:].bitcast(U32).indirect(entries(half, g)))
+
+        ws = {}
+        w = {}
+
+        def sort_bytes(b):
+            ws[b] = tile([P, 512], U8, "ws%d" % b)
+            nc.gpsimd.tensor_copy(
+                ws[b][:].rearrange("p (t m) -> p t m", t=4), ws_raw[:, 512 * b : 512 * (b + 1)].rearrange("p (m t) -> p t m", t=4)
+            )
+
+        def sort_words(g, b):
+            w[g, b] = tile([P, 512], I32, "w%d%d" % (g, b))
+            nc.gpsimd.tensor_copy(
+                w[g, b][:].rearrange("p (t m) -> p t m", t=4), w_raw[g, b][:].rearrange("p (m t) -> p t m", t=4)
+            )
+
+        for b in range(2):
+            sort_bytes(b)
+        for g in range(3):
+            sort_words(g, 0)
+            load_w(g, 1)
+        for g in range(3):
+            sort_words(g, 1)
+        sm_t = placed([P, 2, 4], F32, "sm_t", at_ws + 256)
+        nc.sync.dma_start(sm_t[:], sm.rearrange("(b p t) -> p b t", b=2, t=4))
+        wd = placed([P, 2 * 2 * N], U8, "wd", at_ws + 512)
         nc.sync.dma_start(wd[:].bitcast(I32).rearrange("p (a c) -> p a c", a=2), wd_words.bitcast(I32).rearrange("a p c -> p a c"))
-        wd_plane = lay.tile([P, 2 * N], U8, name="wd_plane", offset=at_wds, align_bytes=256)
-        nc.vector.memset(wd_plane[:].bitcast(I32), 0)
+        wd_plane = placed([P, 2 * N], U8, "wd_plane", at_ws - 256)
+        nc.gpsimd.memset(wd_plane[:].bitcast(I32), 0)
         for q in range(4):
             nc.sync.dma_start(
                 wd_plane[32 * q : 32 * q + 4, :].bitcast(I32).rearrange("p (a c) -> p a c", a=2),
                 wd_scales[:, 4 * q : 4 * q + 4, :].bitcast(I32).rearrange("a r c -> r a c"),
             )
 
-        def entries(half, g):
-            c0 = (J * g + HALF * half) // 16
-            return offsets[:, c0 : c0 + HALF // 16]
 
-        def gather_plane(dst, half, g):
-            nc.vector.tensor_copy(dst, tab_plane[:].indirect(entries(half, g)))
-
-        def gather_words(dst, half, g):
-            nc.vector.tensor_copy(dst, tab[:].bitcast(U32).indirect(entries(half, g)))
-
-        def sort_words(dst, src):
-            nc.vector.tensor_copy(
-                dst.rearrange("p (t c i) -> p c t i", t=4, i=4),
-                src.rearrange("p (c i t) -> p c t i", t=4, i=4),
-            )
-
-        def sort_bytes(dst, src):
-            nc.vector.tensor_copy(dst.rearrange("p (t m) -> p t m", t=4), src.rearrange("p (m t) -> p t m", t=4))
-
-        gs = {}
-        gw = {}
         for half, g in ((0, 0), (0, 1), (0, 2), (1, 0)):
-            t_ = keep.tile([P, HALF], U8, name="gs%d%d" % (half, g), align_bytes=256)
-            gs[half, g] = t_[:]
-            gather_plane(gs[half, g], half, g)
-        ws = [
-            keep.tile([P, 512], U8, name="ws0", align_bytes=256),
-            lay.tile([P, 512], U8, name="ws1", offset=at_w[2, 0] + 2048, align_bytes=256),
-        ]
-        w = {}
-        at_gw = (None, at_w[0, 0], at_w[1, 0] - 1024)
-        at_sorted = {(1, 0): at_w[0, 0] + 2048, (2, 0): at_w[1, 0] + 1024, (0, 1): at_w[2, 0], (1, 1): at_w[0, 1], (2, 1): at_w[1, 1]}
+            gather_plane(half, g)
+        for half in range(2):
+            for g in range(3):
+                gather_words(half, g)
+        for g in (1, 2):
+            gather_plane(1, g, at_w[g - 1])
 
-        def sort_w(g, b):
-            if (g, b) == (0, 0):
-                w[g, b] = wsx[:, 0:2048].bitcast(I32)
-            else:
-                t_ = lay.tile([P, 512], I32, name="w%d%d" % (g, b), offset=at_sorted[g, b], align_bytes=256)
-                w[g, b] = t_[:]
-            sort_words(w[g, b], w_raw[g, b][:, 0:512])
+        sm_of = [sm_t[:, b, :] for b in range(2)]
+        codes = [[tile([P, HALF], U32, "codes%d%d" % (half, b)) for b in range(2)] for half in range(2)]
+        planes = [[tile([P, HALF], U8, "plane%d%d" % (half, b)) for b in range(2)] for half in range(2)]
+        next_bank = [0]
 
-        for g in range(3):
-            if g == 0:
-                t_ = keep.tile([P, HALF], U32, name="gw00", align_bytes=256)
-            else:
-                t_ = lay.tile([P, HALF], U32, name="gw0%d" % g, offset=at_gw[g], align_bytes=256)
-            gw[0, g] = t_[:]
-            gather_words(gw[0, g], 0, g)
-            if g == 0:
-                sort_bytes(ws[0][:], wsx[:, 1536:2048])
-            sort_w(g, 0)
-        sort_bytes(ws[1][:], wsx[:, 2048:2560])
-        for g in range(3):
-            sort_w(g, 1)
-        gs_late = lay.tile([P, 2 * HALF], U8, name="gs_late", offset=at_w[2, 1], align_bytes=256)
-        gw_late = lay.tile([P, 3 * HALF], U32, name="gw_late", offset=at_w[2, 1] + 1024, align_bytes=256)
-        for g in range(3):
-            if g > 0:
-                gs[1, g] = gs_late[:, (g - 1) * HALF : g * HALF]
-                gather_plane(gs[1, g], 1, g)
-            gw[1, g] = gw_late[:, g * HALF : (g + 1) * HALF]
-            gather_words(gw[1, g], 1, g)
+        def bank(name, width=512):
+            t_ = psum.tile([P, width], F32, name=name, tag="bank%d" % (next_bank[0] % 8))
+            next_bank[0] = next_bank[0] + 1
+            return t_
 
-        banks = {}
-        acts = {}
-        codes = {}
-        planes = {}
-
-        def place(unit):
-            return unit // 8, (unit // 4) % 2, (unit // 2) % 2, unit % 2
-
-        bank_of = {2: 4, 3: 5, 6: 6, 7: 7}
-
-        def passes(unit, g):
-            half, jq, b, u = place(unit)
-            if g == 0:
-                banks[unit] = psum.tile([P, 2 * CHUNK], F32, name="a%d" % unit, tag="bank%d" % bank_of.get(unit, unit % 8))
-            cols = slice(jq * CHUNK, (jq + 1) * CHUNK)
-            for e in range(2):
-                r0 = 128 * (2 * u + e)
+        def first_layer(acc, half, b, j0, width, ts):
+            blocks = [(g, e) for g in range(3) for e in range(len(ts))]
+            for g, e in blocks:
+                r0 = 128 * ts[e]
                 nc.tensor.matmul_mx(
-                    out=banks[unit][:, e * CHUNK : (e + 1) * CHUNK],
+                    out=acc[:, e * width : (e + 1) * width],
                     lhsT=w[g, b][:, r0 : r0 + 128].bitcast(FP8X4),
                     lhsT_scale=ws[b][4 * (g + 1) : P, r0 : r0 + 128],
-                    rhs=gw[half, g][:, cols].bitcast(FP8X4),
-                    rhs_scale=gs[half, g][:, cols],
-                    start=(g == 0 and e == 0),
-                    stop=(g == 2 and e == 1),
+                    rhs=gw[half, g][:, j0 : j0 + width].bitcast(FP8X4),
+                    rhs_scale=gs[half, g][:, j0 : j0 + width],
+                    start=((g, e) == blocks[0]),
+                    stop=((g, e) == blocks[-1]),
                 )
 
-        def activate(unit):
-            pair = unit // 2
-            if unit % 2 == 0:
-                acts[pair] = keep.tile([P, 2, CHUNK, 2], F32, name="act%d" % pair, align_bytes=256)
-            nc.scalar.activation(acts[pair][:, unit % 2, :, :], banks[unit][:].rearrange("p (e j) -> p j e", e=2), GELU)
+        def quantise(hb, half, b, j0, width):
+            nc.vector.quantize_mx(
+                out=codes[half][b][:, j0 : j0 + width].bitcast(FP8X4), scales=planes[half][b][:, j0 : j0 + width], in_=hb[:]
+            )
 
-        hbs = {}
-
-        def smooth(pair, j0, j1):
-            if j0 == 0:
-                hbs[pair] = keep.tile([P, 4 * CHUNK], BF16, name="hb%d" % pair, align_bytes=256)
-            nc.vector.tensor_tensor(
-                hbs[pair][:, 4 * j0 : 4 * j1].rearrange("p (j u e) -> p j u e", u=2, e=2),
-                acts[pair][:, :, j0:j1, :].rearrange("p u j e -> p j u e"),
-                sm_t[:, pair % 2, :].rearrange("p (u e) -> p u e", u=2).unsqueeze(1).to_broadcast([P, j1 - j0, 2, 2]),
+        def wide_piece(half, b, j0, eng):
+            name = "%d%d%d" % (half, b, j0)
+            act = tile([P, 2, QUARTER, 2], F32, "act" + name)
+            for u in range(2):
+                acc = bank("a%s%d" % (name, u))
+                first_layer(acc, half, b, j0, QUARTER, (2 * u, 2 * u + 1))
+                nc.scalar.activation(act[:, u, :, :], acc[:].rearrange("p (e j) -> p j e", e=2), GELU)
+            hb = tile([P, 4 * QUARTER], BF16, "hb" + name)
+            eng.tensor_tensor(
+                hb[:].rearrange("p (j u e) -> p j u e", u=2, e=2),
+                act[:].rearrange("p u j e -> p j u e"),
+                sm_of[b].rearrange("p (u e) -> p u e", u=2).unsqueeze(1).to_broadcast([P, QUARTER, 2, 2]),
                 MULT,
             )
+            quantise(hb, half, b, j0, QUARTER)
 
-        narrow = {}
-
-        def narrow_passes(half, b, q, g, bank):
-            if g == 0:
-                narrow[half, q] = psum.tile([P, 4 * 128], F32, name="n%d%d" % (half, q), tag="bank%d" % bank)
-            cols = slice(q * 128, (q + 1) * 128)
-            for t in range(4):
-                nc.tensor.matmul_mx(
-                    out=narrow[half, q][:, t * 128 : (t + 1) * 128],
-                    lhsT=w[g, b][:, 128 * t : 128 * (t + 1)].bitcast(FP8X4),
-                    lhsT_scale=ws[b][4 * (g + 1) : P, 128 * t : 128 * (t + 1)],
-                    rhs=gw[half, g][:, cols].bitcast(FP8X4),
-                    rhs_scale=gs[half, g][:, cols],
-                    start=(g == 0 and t == 0),
-                    stop=(g == 2 and t == 3),
-                )
-
-        sm_wide = keep.tile([P, 128, 4], F32, name="sm_wide", align_bytes=256)
-        nc.scalar.copy(sm_wide[:], sm_t[:, 0, :].unsqueeze(1).to_broadcast([P, 128, 4]))
-
-        def narrow_activate(half, q):
-            act = keep.tile([P, 128, 4], F32, name="nact%d%d" % (half, q), align_bytes=256)
-            nc.scalar.activation(act[:], narrow[half, q][:].rearrange("p (t j) -> p j t", t=4), GELU)
-            return act
-
-        def narrow_finish(q):
-            pair = 2 * (q // 2)
-            act = narrow_activate(0, q)
-            if q % 2 == 0:
-                hbs[pair] = keep.tile([P, 4 * CHUNK], BF16, name="hb%d" % pair, align_bytes=256)
-            nc.gpsimd.tensor_tensor(
-                hbs[pair][:, 512 * (q % 2) : 512 * (q % 2 + 1)], act[:].rearrange("p j t -> p (j t)"), sm_wide[:].rearrange("p j t -> p (j t)"), MULT
-            )
-
-        def narrow_smooth(act, j0):
-            if j0 == 0:
-                hbs[7] = keep.tile([P, 4 * CHUNK], BF16, name="hb7", align_bytes=256)
+        def narrow_piece(half, b, j0):
+            name = "%d%d%d" % (half, b, j0)
+            act = tile([P, 128, 4], F32, "nact" + name)
+            acc = bank("n" + name)
+            first_layer(acc, half, b, j0, 128, (0, 1, 2, 3))
+            nc.scalar.activation(act[:], acc[:].rearrange("p (t j) -> p j t", t=4), GELU)
+            hb = tile([P, 512], BF16, "nhb" + name)
             nc.vector.tensor_tensor(
-                hbs[7][:, 4 * j0 : 4 * j0 + 512].rearrange("p (j t) -> p j t", t=4),
-                act[:],
-                sm_t[:, 1, :].unsqueeze(1).to_broadcast([P, 128, 4]),
-                MULT,
+                hb[:].rearrange("p (j t) -> p j t", t=4), act[:], sm_of[b].unsqueeze(1).to_broadcast([P, 128, 4]), MULT
+            )
+            quantise(hb, half, b, j0, 128)
+
+        def second_pass(y, half, b, nt, j0, width, start, stop):
+            nc.tensor.matmul_mx(
+                out=y,
+                lhsT=wd[:, 512 * b + 256 * nt : 512 * b + 256 * (nt + 1)].bitcast(FP4X4),
+                lhsT_scale=wd_plane[:, 256 * b + 128 * nt : 256 * b + 128 * (nt + 1)],
+                rhs=codes[half][b][:, j0 : j0 + width].bitcast(FP8X4),
+                rhs_scale=planes[half][b][:, j0 : j0 + width],
+                start=start,
+                stop=stop,
             )
 
-        def smooth_on_scalar(pair):
-            hp = keep.tile([P, 4, CHUNK], BF16, name="hp%d" % pair, align_bytes=256)
-            for t in range(4):
-                nc.scalar.activation(hp[:, t, :], acts[pair][:, t // 2, :, t % 2], COPY, scale=sm_t[:, pair % 2, t : t + 1])
-            hbs[pair] = keep.tile([P, 4 * CHUNK], BF16, name="hb%d" % pair, align_bytes=256)
-            nc.scalar.copy(
-                hbs[pair][:].rearrange("p (c i t) -> p c t i", i=4, t=4),
-                hp[:].rearrange("p t (c i) -> p c t i", i=4),
-            )
-
-        wide_codes = [keep.tile([P, HALF], U32, name="wcodes%d" % b, align_bytes=256) for b in range(2)]
-        wide_planes = [keep.tile([P, HALF], U8, name="wplane%d" % b, align_bytes=256) for b in range(2)]
-
-        def quantise(pair, j0, j1):
-            if pair < 4:
-                c0 = CHUNK * (pair // 2)
-                codes[pair] = wide_codes[pair % 2][:, c0 : c0 + CHUNK]
-                planes[pair] = wide_planes[pair % 2][:, c0 : c0 + CHUNK]
-            elif j0 == 0:
-                ct = keep.tile([P, CHUNK], U32, name="codes%d" % pair, align_bytes=256)
-                pt = keep.tile([P, CHUNK], U8, name="plane%d" % pair, align_bytes=256)
-                codes[pair] = ct[:]
-                planes[pair] = pt[:]
-            nc.vector.quantize_mx(out=codes[pair][:, j0:j1].bitcast(FP8X4), scales=planes[pair][:, j0:j1], in_=hbs[pair][:, 4 * j0 : 4 * j1])
+        def second_layer_wide(half, nt):
+            y = bank("yw%d%d" % (half, nt))
+            for b in range(2):
+                second_pass(y[:], half, b, nt, 0, HALF, b == 0, b == 1)
+            res = tile([P, HALF], F32, "resw%d%d" % (half, nt))
+            nc.scalar.copy(res[:], y[:])
+            nc.sync.dma_start(out[P * nt : P * (nt + 1), HALF * half : HALF * (half + 1)], res[:])
 
         out_v = out.rearrange("(nt p) j -> p nt j", p=P)
 
-        def second_layer(chunk, j0, j1, bank):
-            width = j1 - j0
-            y = psum.tile([P, 2 * width], F32, name="y%d_%d" % (chunk, j0), tag="bank%d" % bank)
-            blocks = [(b, nt, j) for b in range(2) for nt in range(2) for j in range(j0, j1, 128)]
+        def second_layer(half, j0, width):
+            y = bank("y%d%d" % (half, j0), 2 * width)
+            blocks = [(b, nt, j) for b in range(2) for nt in range(2) for j in range(0, width, 128)]
             for b, nt, j in blocks:
-                pair = 2 * chunk + b
-                nc.tensor.matmul_mx(
-                    out=y[:, nt * width + j - j0 : nt * width + j - j0 + 128],
-                    lhsT=wd[:, 512 * b + 256 * nt : 512 * b + 256 * (nt + 1)].bitcast(FP4X4),
-                    lhsT_scale=wd_plane[:, 256 * b + 128 * nt : 256 * b + 128 * (nt + 1)],
-                    rhs=codes[pair][:, j : j + 128].bitcast(FP8X4),
-                    rhs_scale=planes[pair][:, j : j + 128],
-                    start=((b, nt, j) == blocks[0]),
-                    stop=((b, nt, j) == blocks[-1]),
+                second_pass(
+                    y[:, nt * width + j : nt * width + j + 128], half, b, nt, j0 + j, 128, (b, nt, j) == blocks[0], (b, nt, j) == blocks[-1]
                 )
-            res = keep.tile([P, 2, width], F32, name="res%d_%d" % (chunk, j0), align_bytes=256)
+            res = tile([P, 2, width], F32, "res%d%d" % (half, j0))
             nc.scalar.copy(res[:], y[:].rearrange("p (nt j) -> p nt j", nt=2))
-            nc.sync.dma_start(out_v[:, :, chunk * CHUNK + j0 : chunk * CHUNK + j1], res[:])
+            nc.sync.dma_start(out_v[:, :, HALF * half + j0 : HALF * half + j0 + width], res[:])
 
-        def second_layer_wide(nt):
-            y = psum.tile([P, HALF], F32, name="yw%d" % nt, tag="bank%d" % nt)
-            for b in range(2):
-                nc.tensor.matmul_mx(
-                    out=y[:],
-                    lhsT=wd[:, 512 * b + 256 * nt : 512 * b + 256 * (nt + 1)].bitcast(FP4X4),
-                    lhsT_scale=wd_plane[:, 256 * b + 128 * nt : 256 * b + 128 * (nt + 1)],
-                    rhs=wide_codes[b][:].bitcast(FP8X4),
-                    rhs_scale=wide_planes[b][:],
-                    start=(b == 0),
-                    stop=(b == 1),
-                )
-            res = keep.tile([P, HALF], F32, name="resw%d" % nt, align_bytes=256)
-            nc.scalar.copy(res[:], y[:])
-            nc.sync.dma_start(out[P * nt : P * (nt + 1), 0:HALF], res[:])
-
-        for g in range(2):
-            for q in range(4):
-                narrow_passes(0, 0, q, g, q)
-        for q in range(4):
-            narrow_passes(0, 0, q, 2, q)
-            narrow_finish(q)
-        for unit in (2, 3, 6, 7):
-            for g in range(3):
-                passes(unit, g)
-            activate(unit)
-        quantise(0, 0, CHUNK)
-        quantise(2, 0, CHUNK)
-        smooth(1, 0, CHUNK)
-        smooth_on_scalar(3)
-        early = (8, 9, 10, 11)
-        for g in range(2):
-            for unit in early:
-                passes(unit, g)
-        for unit in range(8, 14):
-            for g in range(2 if unit in early else 0, 3):
-                passes(unit, g)
-            activate(unit)
-            if unit == 9:
-                quantise(3, 0, CHUNK)
-                quantise(1, 0, CHUNK)
-            if unit % 2 == 1:
-                smooth(unit // 2, 0, CHUNK)
-                if unit > 9:
-                    quantise(unit // 2 - 1, 0, CHUNK)
-        last = []
-        for q in (2, 3):
-            for g in range(3):
-                narrow_passes(1, 1, q, g, 4 + q)
-            last.append(narrow_activate(1, q))
-        second_layer_wide(0)
-        second_layer_wide(1)
-        narrow_smooth(last[0], 0)
-        quantise(6, 0, CHUNK)
-        second_layer(2, 0, CHUNK, 2)
-        narrow_smooth(last[1], 128)
-        quantise(7, 0, 128)
-        second_layer(3, 0, 128, 3)
-        quantise(7, 128, CHUNK)
-        second_layer(3, 128, CHUNK, 4)
+        pieces = [(0, b, j0) for b in range(2) for j0 in (0, QUARTER)] + [(1, 0, 0), (1, 1, 0), (1, 0, QUARTER)]
+        for i, (half, b, j0) in enumerate(pieces):
+            wide_piece(half, b, j0, nc.gpsimd if i < ON_GPSIMD else nc.vector)
+        narrow_piece(1, 1, 256)
+        narrow_piece(1, 1, 384)
+        second_layer_wide(0, 0)
+        second_layer_wide(0, 1)
+        second_layer(1, 0, QUARTER)
+        second_layer(1, 256, 128)
+        second_layer(1, 384, 128)

@@ -14,12 +14,13 @@ U8 = mybir.dt.uint8
 FP8X4 = mybir.dt.float8_e4m3fn_x4
 FP4X4 = mybir.dt.float4_e2m1fn_x4
 GELU = mybir.ActivationFunctionType.Gelu_apprx_tanh
+COPY = mybir.ActivationFunctionType.Copy
 MULT = mybir.AluOpType.mult
 
 P = 128
 HALF = 512
 QUARTER = 256
-ON_GPSIMD = 2
+SPLIT = 2048
 
 
 def tile_list_rvq_gelu_none_kernel(tc, tab_words, tab_scales, w0_words, w0_scales, w1_words, w1_scales,
@@ -39,25 +40,25 @@ def tile_list_rvq_gelu_none_kernel(tc, tab_words, tab_scales, w0_words, w0_scale
             return lay.tile(shape, dtype, name=name, offset=offset, align_bytes=256)
 
         at_tab = 0
-        at_w = [4 * T + 2048 * g for g in range(3)]
-        at_ws = at_w[2] + 2048 + 256
+        at_w = {(g, b): 4 * T + 2048 * (3 * b + g) for b in range(2) for g in range(3)}
+        at_ws = at_w[2, 1] + 3 * 2048
 
         offsets = keep.tile([P, 3 * J // 16], U16, name="offsets")
         nc.sync.dma_start(offsets[:], offs)
 
         tab_plane = tile([P, T], U8, "tab_plane")
         ws_raw = placed([P, R], U8, "ws_raw", at_ws)
-        zeros = placed([P, 9, 128], I32, "zeros", at_w[0] - 256)
-        nc.gpsimd.memset(ws_raw[0:96, :].bitcast(I32), 0)
-        nc.gpsimd.memset(tab_plane[:, 0 : T // 2].bitcast(I32), 0)
-        nc.vector.memset(tab_plane[:, T // 2 : T].bitcast(I32), 0)
-        nc.vector.memset(zeros[96:128, 0:9:8, :], 0)
-        nc.vector.tensor_copy(ws_raw[96:128, :].bitcast(I32).rearrange("p (a c) -> p a c", a=2), zeros[96:128, 0:9:8, :])
+        zeros = lay.tile([P, 4, 1024], I32, name="zeros", offset=at_w[0, 0] - 4096 + 128)
+        nc.gpsimd.memset(tab_plane[:, 0:SPLIT].bitcast(I32), 0)
+        nc.gpsimd.memset(ws_raw[0:64, :].bitcast(I32), 0)
+        nc.vector.memset(tab_plane[:, SPLIT:T].bitcast(I32), 0)
+        nc.vector.memset(zeros[64:128, :, 960:1024], 0)
+        nc.vector.tensor_copy(ws_raw[64:128, :].bitcast(I32).rearrange("p (a c) -> p a c", a=4), zeros[64:128, :, 960:1024])
 
         w_raw = {}
 
         def load_w(g, b):
-            w_raw[g, b] = placed([P, 512], I32, "w_raw%d%d" % (g, b), at_w[g])
+            w_raw[g, b] = placed([P, 512], I32, "w_raw%d%d" % (g, b), at_w[g, b])
             nc.sync.dma_start(w_raw[g, b][:], w_words[g][0].rearrange("p r i -> p (r i)")[:, 2048 * b : 2048 * (b + 1)].bitcast(I32))
 
         def load_w_scales(eng, q):
@@ -69,12 +70,13 @@ def tile_list_rvq_gelu_none_kernel(tc, tab_words, tab_scales, w0_words, w0_scale
             nc.sync.dma_start(tab_plane[32 * q : 32 * q + 4, :].bitcast(I32), tab_scales[0, 4 * q : 4 * q + 4, :].bitcast(I32))
         load_w_scales(nc.gpsimd, 0)
         load_w_scales(nc.gpsimd, 1)
-        load_w_scales(nc.sync, 2)
-        load_w_scales(nc.sync, 3)
         tab = placed([P, T], I32, "tab", at_tab)
         nc.sync.dma_start(tab[:], tab_words[0].rearrange("p t i -> p (t i)").bitcast(I32))
-        for g in range(3):
-            load_w(g, 0)
+        load_w(0, 0)
+        load_w_scales(nc.sync, 2)
+        load_w_scales(nc.sync, 3)
+        for g, b in ((1, 0), (2, 0), (0, 1), (1, 1), (2, 1)):
+            load_w(g, b)
 
         def entries(half, g):
             c0 = (J * g + HALF * half) // 16
@@ -88,37 +90,42 @@ def tile_list_rvq_gelu_none_kernel(tc, tab_words, tab_scales, w0_words, w0_scale
             gs[half, g] = tile([P, HALF], U8, name) if offset is None else placed([P, HALF], U8, name, offset)
             nc.vector.tensor_copy(gs[half, g][:], tab_plane[:].indirect(entries(half, g)))
 
-        def gather_words(half, g):
-            gw[half, g] = tile([P, HALF], U32, "gw%d%d" % (half, g))
+        def gather_words(half, g, offset=None):
+            name = "gw%d%d" % (half, g)
+            gw[half, g] = tile([P, HALF], U32, name) if offset is None else placed([P, HALF], U32, name, offset)
             nc.vector.tensor_copy(gw[half, g][:], tab[:].bitcast(U32).indirect(entries(half, g)))
 
-        ws = {}
         w = {}
-
-        def sort_bytes(b):
-            ws[b] = tile([P, 512], U8, "ws%d" % b)
-            nc.gpsimd.tensor_copy(
-                ws[b][:].rearrange("p (t m) -> p t m", t=4), ws_raw[:, 512 * b : 512 * (b + 1)].rearrange("p (m t) -> p t m", t=4)
-            )
 
         def sort_words(g, b):
             w[g, b] = tile([P, 512], I32, "w%d%d" % (g, b))
-            nc.gpsimd.tensor_copy(
-                w[g, b][:].rearrange("p (t m) -> p t m", t=4), w_raw[g, b][:].rearrange("p (m t) -> p t m", t=4)
+            nc.vector.tensor_copy(
+                w[g, b][:].rearrange("p (t c i) -> p c t i", t=4, i=4), w_raw[g, b][:].rearrange("p (c i t) -> p c t i", t=4, i=4)
             )
 
-        for b in range(2):
-            sort_bytes(b)
         for g in range(3):
-            sort_words(g, 0)
-            load_w(g, 1)
+            gather_plane(0, g)
+        gather_words(0, 0)
+        sort_words(0, 0)
+        ws = tile([P, R], U8, "ws")
+        nc.vector.tensor_copy(ws[:].rearrange("p (b t m) -> p b t m", b=2, t=4), ws_raw[:].rearrange("p (b m t) -> p b t m", b=2, t=4))
+        gather_words(0, 1, at_ws)
+        sort_words(1, 0)
+        gather_words(0, 2, at_w[1, 0])
+        sort_words(2, 0)
         for g in range(3):
             sort_words(g, 1)
-        sm_t = placed([P, 2, 4], F32, "sm_t", at_ws + 256)
+        gather_plane(1, 0, at_w[2, 0])
+        gather_words(1, 0, at_w[0, 1])
+        gather_plane(1, 1, at_w[1, 1])
+        gather_words(1, 1, at_w[2, 1] - 1024)
+        gather_plane(1, 2, at_w[2, 1] + 1024)
+        gather_words(1, 2, at_w[2, 1] + 1536)
+        sm_t = placed([P, 2, 4], F32, "sm_t", at_w[0, 0])
         nc.sync.dma_start(sm_t[:], sm.rearrange("(b p t) -> p b t", b=2, t=4))
-        wd = placed([P, 2 * 2 * N], U8, "wd", at_ws + 512)
+        wd = placed([P, 2 * 2 * N], U8, "wd", at_w[0, 0] + 256)
         nc.sync.dma_start(wd[:].bitcast(I32).rearrange("p (a c) -> p a c", a=2), wd_words.bitcast(I32).rearrange("a p c -> p a c"))
-        wd_plane = placed([P, 2 * N], U8, "wd_plane", at_ws - 256)
+        wd_plane = placed([P, 2 * N], U8, "wd_plane", at_w[0, 0] + 256 + 1024)
         nc.gpsimd.memset(wd_plane[:].bitcast(I32), 0)
         for q in range(4):
             nc.sync.dma_start(
@@ -126,14 +133,6 @@ def tile_list_rvq_gelu_none_kernel(tc, tab_words, tab_scales, w0_words, w0_scale
                 wd_scales[:, 4 * q : 4 * q + 4, :].bitcast(I32).rearrange("a r c -> r a c"),
             )
 
-
-        for half, g in ((0, 0), (0, 1), (0, 2), (1, 0)):
-            gather_plane(half, g)
-        for half in range(2):
-            for g in range(3):
-                gather_words(half, g)
-        for g in (1, 2):
-            gather_plane(1, g, at_w[g - 1])
 
         sm_of = [sm_t[:, b, :] for b in range(2)]
         codes = [[tile([P, HALF], U32, "codes%d%d" % (half, b)) for b in range(2)] for half in range(2)]
@@ -145,39 +144,54 @@ def tile_list_rvq_gelu_none_kernel(tc, tab_words, tab_scales, w0_words, w0_scale
             next_bank[0] = next_bank[0] + 1
             return t_
 
-        def first_layer(acc, half, b, j0, width, ts):
-            blocks = [(g, e) for g in range(3) for e in range(len(ts))]
-            for g, e in blocks:
-                r0 = 128 * ts[e]
-                nc.tensor.matmul_mx(
-                    out=acc[:, e * width : (e + 1) * width],
-                    lhsT=w[g, b][:, r0 : r0 + 128].bitcast(FP8X4),
-                    lhsT_scale=ws[b][4 * (g + 1) : P, r0 : r0 + 128],
-                    rhs=gw[half, g][:, j0 : j0 + width].bitcast(FP8X4),
-                    rhs_scale=gs[half, g][:, j0 : j0 + width],
-                    start=((g, e) == blocks[0]),
-                    stop=((g, e) == blocks[-1]),
-                )
+        def first_layer(acc, half, b, j0, width, ts, gs_now=(0, 1, 2)):
+            for g in gs_now:
+                for e in range(len(ts)):
+                    r0 = 128 * ts[e]
+                    nc.tensor.matmul_mx(
+                        out=acc[:, e * width : (e + 1) * width],
+                        lhsT=w[g, b][:, r0 : r0 + 128].bitcast(FP8X4),
+                        lhsT_scale=ws[4 * (g + 1) : P, 512 * b + r0 : 512 * b + r0 + 128],
+                        rhs=gw[half, g][:, j0 : j0 + width].bitcast(FP8X4),
+                        rhs_scale=gs[half, g][:, j0 : j0 + width],
+                        start=(g == 0 and e == 0),
+                        stop=(g == 2 and e == len(ts) - 1),
+                    )
 
         def quantise(hb, half, b, j0, width):
             nc.vector.quantize_mx(
                 out=codes[half][b][:, j0 : j0 + width].bitcast(FP8X4), scales=planes[half][b][:, j0 : j0 + width], in_=hb[:]
             )
 
+        accs = {}
+
+        def open_piece(half, b, j0, g):
+            for u in range(2):
+                if g == 0:
+                    accs[half, b, j0, u] = bank("a%d%d%d%d" % (half, b, j0, u))
+                first_layer(accs[half, b, j0, u], half, b, j0, QUARTER, (2 * u, 2 * u + 1), (g,))
+
         def wide_piece(half, b, j0, eng):
             name = "%d%d%d" % (half, b, j0)
             act = tile([P, 2, QUARTER, 2], F32, "act" + name)
             for u in range(2):
-                acc = bank("a%s%d" % (name, u))
-                first_layer(acc, half, b, j0, QUARTER, (2 * u, 2 * u + 1))
+                opened = (half, b, j0, u) in accs
+                acc = accs[half, b, j0, u] if opened else bank("a%s%d" % (name, u))
+                first_layer(acc, half, b, j0, QUARTER, (2 * u, 2 * u + 1), (2,) if opened else (0, 1, 2))
                 nc.scalar.activation(act[:, u, :, :], acc[:].rearrange("p (e j) -> p j e", e=2), GELU)
             hb = tile([P, 4 * QUARTER], BF16, "hb" + name)
-            eng.tensor_tensor(
-                hb[:].rearrange("p (j u e) -> p j u e", u=2, e=2),
-                act[:].rearrange("p u j e -> p j u e"),
-                sm_of[b].rearrange("p (u e) -> p u e", u=2).unsqueeze(1).to_broadcast([P, QUARTER, 2, 2]),
-                MULT,
-            )
+            if eng is nc.scalar:
+                hp = tile([P, 4, QUARTER], BF16, "hp" + name)
+                for t in range(4):
+                    nc.scalar.activation(hp[:, t, :], act[:, t // 2, :, t % 2], COPY, scale=sm_t[:, b, t : t + 1])
+                nc.scalar.copy(hb[:].rearrange("p (c i t) -> p c t i", i=4, t=4), hp[:].rearrange("p t (c i) -> p c t i", i=4))
+            else:
+                eng.tensor_tensor(
+                    hb[:].rearrange("p (j u e) -> p j u e", u=2, e=2),
+                    act[:].rearrange("p u j e -> p j u e"),
+                    sm_of[b].rearrange("p (u e) -> p u e", u=2).unsqueeze(1).to_broadcast([P, QUARTER, 2, 2]),
+                    MULT,
+                )
             quantise(hb, half, b, j0, QUARTER)
 
         def narrow_piece(half, b, j0):
@@ -224,9 +238,19 @@ def tile_list_rvq_gelu_none_kernel(tc, tab_words, tab_scales, w0_words, w0_scale
             nc.scalar.copy(res[:], y[:].rearrange("p (nt j) -> p nt j", nt=2))
             nc.sync.dma_start(out_v[:, :, HALF * half + j0 : HALF * half + j0 + width], res[:])
 
-        pieces = [(0, b, j0) for b in range(2) for j0 in (0, QUARTER)] + [(1, 0, 0), (1, 1, 0), (1, 0, QUARTER)]
-        for i, (half, b, j0) in enumerate(pieces):
-            wide_piece(half, b, j0, nc.gpsimd if i < ON_GPSIMD else nc.vector)
+        for g in range(2):
+            for j0 in (0, QUARTER):
+                open_piece(0, 0, j0, g)
+        wide_piece(0, 0, 0, nc.gpsimd)
+        wide_piece(0, 0, QUARTER, nc.gpsimd)
+        wide_piece(0, 1, 0, nc.vector)
+        wide_piece(0, 1, QUARTER, nc.scalar)
+        late = ((0, 0), (1, 0), (0, QUARTER))
+        for g in range(2):
+            for b, j0 in late:
+                open_piece(1, b, j0, g)
+        for b, j0 in late:
+            wide_piece(1, b, j0, nc.vector)
         narrow_piece(1, 1, 256)
         narrow_piece(1, 1, 384)
         second_layer_wide(0, 0)

@@ -42,6 +42,7 @@ def tile_list_rvq_gelu_none_kernel(tc, tab_words, tab_scales, w0_words, w0_scale
         at_tab = 0
         at_w = {(g, b): 4 * T + 2048 * (3 * b + g) for b in range(2) for g in range(3)}
         at_ws = at_w[2, 1] + 3 * 2048
+        at_acts = at_ws + 2048
 
         offsets = keep.tile([P, 3 * J // 16], U16, name="offsets")
         nc.sync.dma_start(offsets[:], offs)
@@ -58,25 +59,28 @@ def tile_list_rvq_gelu_none_kernel(tc, tab_words, tab_scales, w0_words, w0_scale
         w_raw = {}
 
         def load_w(g, b):
-            w_raw[g, b] = placed([P, 512], I32, "w_raw%d%d" % (g, b), at_w[g, b])
+            name = "w_raw%d%d" % (g, b)
+            w_raw[g, b] = tile([P, 512], I32, name) if (g, b) == (0, 0) else placed([P, 512], I32, name, at_w[g, b])
             nc.sync.dma_start(w_raw[g, b][:], w_words[g][0].rearrange("p r i -> p (r i)")[:, 2048 * b : 2048 * (b + 1)].bitcast(I32))
 
-        def load_w_scales(eng, q):
-            for g in range(3):
+        def load_w_scales(eng, rows):
+            for q, g in rows:
                 row = 32 * q + 4 * (g + 1)
                 eng.dma_start(ws_raw[row : row + 4, :].bitcast(I32), w_scales[g][0, 4 * q : 4 * q + 4, :].bitcast(I32))
 
-        for q in range(4):
-            nc.sync.dma_start(tab_plane[32 * q : 32 * q + 4, :].bitcast(I32), tab_scales[0, 4 * q : 4 * q + 4, :].bitcast(I32))
-        load_w_scales(nc.gpsimd, 0)
-        load_w_scales(nc.gpsimd, 1)
+        load_w(0, 0)
+        for r in range(4):
+            nc.sync.dma_start(tab_plane[r:P:32, :].bitcast(I32), tab_scales[0, r:16:4, :].bitcast(I32))
+        rows = [(q, g) for q in range(4) for g in range(3)]
+        load_w_scales(nc.gpsimd, rows[0:4])
+        load_w_scales(nc.sync, rows[4:5])
         tab = placed([P, T], I32, "tab", at_tab)
         nc.sync.dma_start(tab[:], tab_words[0].rearrange("p t i -> p (t i)").bitcast(I32))
-        load_w(0, 0)
-        load_w_scales(nc.sync, 2)
-        load_w_scales(nc.sync, 3)
+        load_w_scales(nc.sync, rows[5:12])
         for g, b in ((1, 0), (2, 0), (0, 1), (1, 1), (2, 1)):
             load_w(g, b)
+        sm_t = placed([P, 2, 4], F32, "sm_t", at_w[0, 0])
+        nc.sync.dma_start(sm_t[:], sm.rearrange("(b p t) -> p b t", b=2, t=4))
 
         def entries(half, g):
             c0 = (J * g + HALF * half) // 16
@@ -103,29 +107,26 @@ def tile_list_rvq_gelu_none_kernel(tc, tab_words, tab_scales, w0_words, w0_scale
                 w[g, b][:].rearrange("p (t c i) -> p c t i", t=4, i=4), w_raw[g, b][:].rearrange("p (c i t) -> p c t i", t=4, i=4)
             )
 
-        for g in range(3):
-            gather_plane(0, g)
-        gather_words(0, 0)
         sort_words(0, 0)
+        for half, g in ((0, 0), (0, 1), (0, 2), (1, 0)):
+            gather_plane(half, g)
+        gather_words(0, 0)
         ws = tile([P, R], U8, "ws")
         nc.vector.tensor_copy(ws[:].rearrange("p (b t m) -> p b t m", b=2, t=4), ws_raw[:].rearrange("p (b m t) -> p b t m", b=2, t=4))
         gather_words(0, 1, at_ws)
         sort_words(1, 0)
-        gather_words(0, 2, at_w[1, 0])
+        gather_words(0, 2, at_w[1, 0] - 1792)
         sort_words(2, 0)
         for g in range(3):
             sort_words(g, 1)
-        gather_plane(1, 0, at_w[2, 0])
         gather_words(1, 0, at_w[0, 1])
         gather_plane(1, 1, at_w[1, 1])
         gather_words(1, 1, at_w[2, 1] - 1024)
         gather_plane(1, 2, at_w[2, 1] + 1024)
         gather_words(1, 2, at_w[2, 1] + 1536)
-        sm_t = placed([P, 2, 4], F32, "sm_t", at_w[0, 0])
-        nc.sync.dma_start(sm_t[:], sm.rearrange("(b p t) -> p b t", b=2, t=4))
-        wd = placed([P, 2 * 2 * N], U8, "wd", at_w[0, 0] + 256)
+        wd = placed([P, 2 * 2 * N], U8, "wd", at_w[2, 0] + 256)
         nc.sync.dma_start(wd[:].bitcast(I32).rearrange("p (a c) -> p a c", a=2), wd_words.bitcast(I32).rearrange("a p c -> p a c"))
-        wd_plane = placed([P, 2 * N], U8, "wd_plane", at_w[0, 0] + 256 + 1024)
+        wd_plane = placed([P, 2 * N], U8, "wd_plane", at_w[2, 0] + 256 + 1024)
         nc.gpsimd.memset(wd_plane[:].bitcast(I32), 0)
         for q in range(4):
             nc.sync.dma_start(
@@ -171,28 +172,35 @@ def tile_list_rvq_gelu_none_kernel(tc, tab_words, tab_scales, w0_words, w0_scale
                     accs[half, b, j0, u] = bank("a%d%d%d%d" % (half, b, j0, u))
                 first_layer(accs[half, b, j0, u], half, b, j0, QUARTER, (2 * u, 2 * u + 1), (g,))
 
-        def wide_piece(half, b, j0, eng):
-            name = "%d%d%d" % (half, b, j0)
-            act = tile([P, 2, QUARTER, 2], F32, "act" + name)
+        def smooth(act, half, b, j0, lo, hi, on):
+            name = "%d%d%d" % (half, b, j0 + lo)
+            width = hi - lo
+            hb = tile([P, 4 * width], BF16, "hb" + name)
+            if on == "scalar":
+                hp = placed([P, 24, width], BF16, "hp" + name, at_acts)[:, 0:4, :]
+                for t in range(4):
+                    nc.scalar.activation(hp[:, t, :], act[:, t // 2, lo:hi, t % 2], COPY, scale=sm_t[:, b, t : t + 1])
+                nc.scalar.copy(hb[:].rearrange("p (c i t) -> p c t i", i=4, t=4), hp.rearrange("p t (c i) -> p c t i", i=4))
+            else:
+                eng = nc.gpsimd if on == "gpsimd" else nc.vector
+                eng.tensor_tensor(
+                    hb[:].rearrange("p (j u e) -> p j u e", u=2, e=2),
+                    act[:, :, lo:hi, :].rearrange("p u j e -> p j u e"),
+                    sm_of[b].rearrange("p (u e) -> p u e", u=2).unsqueeze(1).to_broadcast([P, width, 2, 2]),
+                    MULT,
+                )
+            quantise(hb, half, b, j0 + lo, width)
+
+        def wide_piece(half, b, j0, offset=None):
+            name = "act%d%d%d" % (half, b, j0)
+            shape = [P, 2, QUARTER, 2]
+            act = tile(shape, F32, name) if offset is None else placed(shape, F32, name, offset)
             for u in range(2):
                 opened = (half, b, j0, u) in accs
                 acc = accs[half, b, j0, u] if opened else bank("a%s%d" % (name, u))
                 first_layer(acc, half, b, j0, QUARTER, (2 * u, 2 * u + 1), (2,) if opened else (0, 1, 2))
                 nc.scalar.activation(act[:, u, :, :], acc[:].rearrange("p (e j) -> p j e", e=2), GELU)
-            hb = tile([P, 4 * QUARTER], BF16, "hb" + name)
-            if eng is nc.scalar:
-                hp = tile([P, 4, QUARTER], BF16, "hp" + name)
-                for t in range(4):
-                    nc.scalar.activation(hp[:, t, :], act[:, t // 2, :, t % 2], COPY, scale=sm_t[:, b, t : t + 1])
-                nc.scalar.copy(hb[:].rearrange("p (c i t) -> p c t i", i=4, t=4), hp[:].rearrange("p t (c i) -> p c t i", i=4))
-            else:
-                eng.tensor_tensor(
-                    hb[:].rearrange("p (j u e) -> p j u e", u=2, e=2),
-                    act[:].rearrange("p u j e -> p j u e"),
-                    sm_of[b].rearrange("p (u e) -> p u e", u=2).unsqueeze(1).to_broadcast([P, QUARTER, 2, 2]),
-                    MULT,
-                )
-            quantise(hb, half, b, j0, QUARTER)
+            return act
 
         def narrow_piece(half, b, j0):
             name = "%d%d%d" % (half, b, j0)
@@ -241,16 +249,18 @@ def tile_list_rvq_gelu_none_kernel(tc, tab_words, tab_scales, w0_words, w0_scale
         for g in range(2):
             for j0 in (0, QUARTER):
                 open_piece(0, 0, j0, g)
-        wide_piece(0, 0, 0, nc.gpsimd)
-        wide_piece(0, 0, QUARTER, nc.gpsimd)
-        wide_piece(0, 1, 0, nc.vector)
-        wide_piece(0, 1, QUARTER, nc.scalar)
+        for j0 in (0, QUARTER):
+            smooth(wide_piece(0, 0, j0), 0, 0, j0, 0, QUARTER, "gpsimd")
+        third = wide_piece(0, 1, 0)
+        smooth(third, 0, 1, 0, 0, 128, "gpsimd")
+        smooth(wide_piece(0, 1, QUARTER), 0, 1, QUARTER, 0, QUARTER, "scalar")
+        smooth(third, 0, 1, 0, 128, QUARTER, "vector")
         late = ((0, 0), (1, 0), (0, QUARTER))
         for g in range(2):
             for b, j0 in late:
                 open_piece(1, b, j0, g)
-        for b, j0 in late:
-            wide_piece(1, b, j0, nc.vector)
+        for i, (b, j0) in enumerate(late):
+            smooth(wide_piece(1, b, j0, at_acts + 4096 * i), 1, b, j0, 0, QUARTER, "vector")
         narrow_piece(1, 1, 256)
         narrow_piece(1, 1, 384)
         second_layer_wide(0, 0)

@@ -43,6 +43,7 @@ def tile_list_rvq_gelu_none_kernel(tc, tab_words, tab_scales, w0_words, w0_scale
         at_w = {(g, b): 4 * T + 2048 * (3 * b + g) for b in range(2) for g in range(3)}
         at_ws = at_w[2, 1] + 3 * 2048
         at_acts = at_ws + 2048
+        at_hb = at_acts + 3 * 4096 + 1024
 
         offsets = keep.tile([P, 3 * J // 16], U16, name="offsets")
         nc.sync.dma_start(offsets[:], offs)
@@ -161,7 +162,7 @@ def tile_list_rvq_gelu_none_kernel(tc, tab_words, tab_scales, w0_words, w0_scale
 
         def quantise(hb, half, b, j0, width):
             nc.vector.quantize_mx(
-                out=codes[half][b][:, j0 : j0 + width].bitcast(FP8X4), scales=planes[half][b][:, j0 : j0 + width], in_=hb[:]
+                out=codes[half][b][:, j0 : j0 + width].bitcast(FP8X4), scales=planes[half][b][:, j0 : j0 + width], in_=hb
             )
 
         accs = {}
@@ -172,24 +173,30 @@ def tile_list_rvq_gelu_none_kernel(tc, tab_words, tab_scales, w0_words, w0_scale
                     accs[half, b, j0, u] = bank("a%d%d%d%d" % (half, b, j0, u))
                 first_layer(accs[half, b, j0, u], half, b, j0, QUARTER, (2 * u, 2 * u + 1), (g,))
 
-        def smooth(act, half, b, j0, lo, hi, on):
+        def smooth(act, half, b, j0, lo, hi, on, into=None):
             name = "%d%d%d" % (half, b, j0 + lo)
             width = hi - lo
-            hb = tile([P, 4 * width], BF16, "hb" + name)
+            if into is not None:
+                hb = into[:, 4 * (j0 + lo) : 4 * (j0 + hi)]
+            elif half == 0 and on != "gpsimd":
+                hb = placed([P, 4 * width], BF16, "hb" + name, at_hb + 8 * (j0 + lo))[:]
+            else:
+                hb = tile([P, 4 * width], BF16, "hb" + name)[:]
             if on == "scalar":
-                hp = placed([P, 24, width], BF16, "hp" + name, at_acts)[:, 0:4, :]
+                hp = placed([P, 48, width], BF16, "hp" + name, at_acts)[:, 0:4, :] if j0 == QUARTER else tile([P, 4, width], BF16, "hp" + name)[:]
                 for t in range(4):
                     nc.scalar.activation(hp[:, t, :], act[:, t // 2, lo:hi, t % 2], COPY, scale=sm_t[:, b, t : t + 1])
-                nc.scalar.copy(hb[:].rearrange("p (c i t) -> p c t i", i=4, t=4), hp.rearrange("p t (c i) -> p c t i", i=4))
+                nc.scalar.copy(hb.rearrange("p (c i t) -> p c t i", i=4, t=4), hp.rearrange("p t (c i) -> p c t i", i=4))
             else:
                 eng = nc.gpsimd if on == "gpsimd" else nc.vector
                 eng.tensor_tensor(
-                    hb[:].rearrange("p (j u e) -> p j u e", u=2, e=2),
+                    hb.rearrange("p (j u e) -> p j u e", u=2, e=2),
                     act[:, :, lo:hi, :].rearrange("p u j e -> p j u e"),
                     sm_of[b].rearrange("p (u e) -> p u e", u=2).unsqueeze(1).to_broadcast([P, width, 2, 2]),
                     MULT,
                 )
-            quantise(hb, half, b, j0 + lo, width)
+            if into is None:
+                quantise(hb, half, b, j0 + lo, width)
 
         def wide_piece(half, b, j0, offset=None):
             name = "act%d%d%d" % (half, b, j0)
@@ -202,17 +209,21 @@ def tile_list_rvq_gelu_none_kernel(tc, tab_words, tab_scales, w0_words, w0_scale
                 nc.scalar.activation(act[:, u, :, :], acc[:].rearrange("p (e j) -> p j e", e=2), GELU)
             return act
 
-        def narrow_piece(half, b, j0):
+        def open_narrow(half, b, j0, g):
+            if g == 0:
+                accs[half, b, j0] = bank("n%d%d%d" % (half, b, j0))
+            first_layer(accs[half, b, j0], half, b, j0, 128, (0, 1, 2, 3), (g,))
+
+        def narrow_piece(half, b, j0, eng, into=None):
             name = "%d%d%d" % (half, b, j0)
             act = tile([P, 128, 4], F32, "nact" + name)
-            acc = bank("n" + name)
-            first_layer(acc, half, b, j0, 128, (0, 1, 2, 3))
-            nc.scalar.activation(act[:], acc[:].rearrange("p (t j) -> p j t", t=4), GELU)
-            hb = tile([P, 512], BF16, "nhb" + name)
-            nc.vector.tensor_tensor(
-                hb[:].rearrange("p (j t) -> p j t", t=4), act[:], sm_of[b].unsqueeze(1).to_broadcast([P, 128, 4]), MULT
-            )
-            quantise(hb, half, b, j0, 128)
+            for g in range(2 if (half, b, j0) in accs else 0, 3):
+                open_narrow(half, b, j0, g)
+            nc.scalar.activation(act[:], accs[half, b, j0][:].rearrange("p (t j) -> p j t", t=4), GELU)
+            hb = tile([P, 512], BF16, "nhb" + name)[:] if into is None else into[:, 4 * j0 : 4 * j0 + 512]
+            eng.tensor_tensor(hb.rearrange("p (j t) -> p j t", t=4), act[:], sm_of[b].unsqueeze(1).to_broadcast([P, 128, 4]), MULT)
+            if into is None:
+                quantise(hb, half, b, j0, 128)
 
         def second_pass(y, half, b, nt, j0, width, start, stop):
             nc.tensor.matmul_mx(
@@ -247,22 +258,33 @@ def tile_list_rvq_gelu_none_kernel(tc, tab_words, tab_scales, w0_words, w0_scale
             nc.sync.dma_start(out_v[:, :, HALF * half + j0 : HALF * half + j0 + width], res[:])
 
         for g in range(2):
-            for j0 in (0, QUARTER):
-                open_piece(0, 0, j0, g)
-        for j0 in (0, QUARTER):
-            smooth(wide_piece(0, 0, j0), 0, 0, j0, 0, QUARTER, "gpsimd")
+            for j0 in (0, 128):
+                open_narrow(0, 0, j0, g)
+            open_piece(0, 0, QUARTER, g)
+        whole = [tile([P, 4 * HALF], BF16, "whole0")]
+        for j0 in (0, 128):
+            narrow_piece(0, 0, j0, nc.gpsimd, whole[0])
+        smooth(wide_piece(0, 0, QUARTER), 0, 0, QUARTER, 0, QUARTER, "gpsimd", whole[0])
+        quantise(whole[0][:], 0, 0, 0, HALF)
         third = wide_piece(0, 1, 0)
         smooth(third, 0, 1, 0, 0, 128, "gpsimd")
-        smooth(wide_piece(0, 1, QUARTER), 0, 1, QUARTER, 0, QUARTER, "scalar")
-        smooth(third, 0, 1, 0, 128, QUARTER, "vector")
-        late = ((0, 0), (1, 0), (0, QUARTER))
+        middle = placed([P, 4 * HALF], BF16, "middle", at_hb - 1024)
+        smooth(third, 0, 1, 0, 128, QUARTER, "scalar", middle)
+        fourth = wide_piece(0, 1, QUARTER)
+        smooth(fourth, 0, 1, QUARTER, 0, 128, "scalar", middle)
+        quantise(middle[:, 512:1536], 0, 1, 128, QUARTER)
+        smooth(fourth, 0, 1, QUARTER, 128, QUARTER, "vector")
+        whole.append(placed([P, 4 * HALF], BF16, "whole1", at_hb))
+        late = ((0, 0), (0, QUARTER), (1, 0))
         for g in range(2):
-            for b, j0 in late:
+            for b, j0 in late[:2]:
                 open_piece(1, b, j0, g)
         for i, (b, j0) in enumerate(late):
-            smooth(wide_piece(1, b, j0, at_acts + 4096 * i), 1, b, j0, 0, QUARTER, "vector")
-        narrow_piece(1, 1, 256)
-        narrow_piece(1, 1, 384)
+            smooth(wide_piece(1, b, j0, at_acts + 4096 * i), 1, b, j0, 0, QUARTER, "vector", whole[1] if b == 0 else None)
+            if i == 1:
+                quantise(whole[1][:], 1, 0, 0, HALF)
+        narrow_piece(1, 1, 256, nc.vector)
+        narrow_piece(1, 1, 384, nc.vector)
         second_layer_wide(0, 0)
         second_layer_wide(0, 1)
         second_layer(1, 0, QUARTER)

@@ -112,9 +112,14 @@ def tile_list_rvq_gelu_none_kernel(tc, tab_words, tab_scales, w0_words, w0_scale
         for half, g in ((0, 0), (0, 1), (0, 2), (1, 0)):
             gather_plane(half, g)
         gather_words(0, 0)
-        ws = tile([P, R], U8, "ws")
-        nc.vector.tensor_copy(ws[:].rearrange("p (b t m) -> p b t m", b=2, t=4), ws_raw[:].rearrange("p (b m t) -> p b t m", b=2, t=4))
-        gather_words(0, 1, at_ws)
+        ws = [tile([P, HALF], U8, "ws0"), tile([P, HALF], U8, "ws1")]
+
+        def sort_scales(eng, b):
+            eng.tensor_copy(ws[b][:].rearrange("p (t m) -> p t m", t=4), ws_raw[:, HALF * b : HALF * (b + 1)].rearrange("p (m t) -> p t m", t=4))
+
+        sort_scales(nc.gpsimd, 0)
+        sort_scales(nc.gpsimd, 1)
+        gather_words(0, 1)
         sort_words(1, 0)
         gather_words(0, 2, at_w[1, 0] - 1792)
         sort_words(2, 0)
@@ -153,7 +158,7 @@ def tile_list_rvq_gelu_none_kernel(tc, tab_words, tab_scales, w0_words, w0_scale
                     nc.tensor.matmul_mx(
                         out=acc[:, e * width : (e + 1) * width],
                         lhsT=w[g, b][:, r0 : r0 + 128].bitcast(FP8X4),
-                        lhsT_scale=ws[4 * (g + 1) : P, 512 * b + r0 : 512 * b + r0 + 128],
+                        lhsT_scale=ws[b][4 * (g + 1) : P, r0 : r0 + 128],
                         rhs=gw[half, g][:, j0 : j0 + width].bitcast(FP8X4),
                         rhs_scale=gs[half, g][:, j0 : j0 + width],
                         start=(g == 0 and e == 0),
@@ -257,6 +262,12 @@ def tile_list_rvq_gelu_none_kernel(tc, tab_words, tab_scales, w0_words, w0_scale
             nc.scalar.copy(res[:], y[:].rearrange("p (nt j) -> p nt j", nt=2))
             nc.sync.dma_start(out_v[:, :, HALF * half + j0 : HALF * half + j0 + width], res[:])
 
+        warm = psum.tile([P, 512], F32, name="warm", tag="bank7")
+        for i in range(4):
+            nc.tensor.matmul_mx(
+                out=warm[:], lhsT=w[0, 0][:, 0:128].bitcast(FP8X4), lhsT_scale=gs[0, 2][:, 0:128],
+                rhs=w[0, 0][:].bitcast(FP8X4), rhs_scale=gs[0, 2][:], start=True, stop=True,
+            )
         for g in range(2):
             for j0 in (0, 128):
                 open_narrow(0, 0, j0, g)

@@ -51,11 +51,13 @@ def tile_list_rvq_gelu_none_kernel(tc, tab_words, tab_scales, w0_words, w0_scale
         tab_plane = tile([P, T], U8, "tab_plane")
         ws_raw = placed([P, R], U8, "ws_raw", at_ws)
         zeros = lay.tile([P, 4, 1024], I32, name="zeros", offset=at_w[0, 0] - 4096 + 128)
+        nc.gpsimd.memset(zeros[:, 0, 0:32], 0)
         nc.gpsimd.memset(tab_plane[:, 0:SPLIT].bitcast(I32), 0)
         nc.gpsimd.memset(ws_raw[0:64, :].bitcast(I32), 0)
         nc.vector.memset(tab_plane[:, SPLIT:T].bitcast(I32), 0)
-        nc.vector.memset(zeros[64:128, :, 960:1024], 0)
-        nc.vector.tensor_copy(ws_raw[64:128, :].bitcast(I32).rearrange("p (a c) -> p a c", a=4), zeros[64:128, :, 960:1024])
+        nc.vector.tensor_copy(
+            ws_raw[64:128, :].bitcast(I32).rearrange("p (a c) -> p a c", c=32), zeros[64:128, 0:1, 0:32].to_broadcast([64, R // 128, 32])
+        )
 
         w_raw = {}
 
@@ -75,10 +77,11 @@ def tile_list_rvq_gelu_none_kernel(tc, tab_words, tab_scales, w0_words, w0_scale
         rows = [(q, g) for q in range(4) for g in range(3)]
         load_w_scales(nc.gpsimd, rows[0:4])
         load_w_scales(nc.sync, rows[4:5])
+        load_w(1, 0)
         tab = placed([P, T], I32, "tab", at_tab)
         nc.sync.dma_start(tab[:], tab_words[0].rearrange("p t i -> p (t i)").bitcast(I32))
         load_w_scales(nc.sync, rows[5:12])
-        for g, b in ((1, 0), (2, 0), (0, 1), (1, 1), (2, 1)):
+        for g, b in ((2, 0), (0, 1), (1, 1), (2, 1)):
             load_w(g, b)
         sm_t = placed([P, 2, 4], F32, "sm_t", at_w[0, 0])
         nc.sync.dma_start(sm_t[:], sm.rearrange("(b p t) -> p b t", b=2, t=4))
@@ -102,9 +105,9 @@ def tile_list_rvq_gelu_none_kernel(tc, tab_words, tab_scales, w0_words, w0_scale
 
         w = {}
 
-        def sort_words(g, b):
+        def sort_words(g, b, eng=nc.vector):
             w[g, b] = tile([P, 512], I32, "w%d%d" % (g, b))
-            nc.vector.tensor_copy(
+            eng.tensor_copy(
                 w[g, b][:].rearrange("p (t c i) -> p c t i", t=4, i=4), w_raw[g, b][:].rearrange("p (c i t) -> p c t i", t=4, i=4)
             )
 
@@ -117,12 +120,12 @@ def tile_list_rvq_gelu_none_kernel(tc, tab_words, tab_scales, w0_words, w0_scale
         def sort_scales(eng, b):
             eng.tensor_copy(ws[b][:].rearrange("p (t m) -> p t m", t=4), ws_raw[:, HALF * b : HALF * (b + 1)].rearrange("p (m t) -> p t m", t=4))
 
+        sort_words(1, 0, nc.gpsimd)
         sort_scales(nc.gpsimd, 0)
         sort_scales(nc.gpsimd, 1)
         gather_words(0, 1)
-        sort_words(1, 0)
-        gather_words(0, 2, at_w[1, 0] - 1792)
-        sort_words(2, 0)
+        gather_words(0, 2)
+        sort_words(2, 0, nc.gpsimd)
         for g in range(3):
             sort_words(g, 1)
         gather_words(1, 0, at_w[0, 1])
@@ -171,9 +174,11 @@ def tile_list_rvq_gelu_none_kernel(tc, tab_words, tab_scales, w0_words, w0_scale
             )
 
         accs = {}
+        done = {}
 
-        def open_piece(half, b, j0, g):
-            for u in range(2):
+        def open_piece(half, b, j0, g, us=(0, 1)):
+            for u in us:
+                done[half, b, j0, u] = g + 1
                 if g == 0:
                     accs[half, b, j0, u] = bank("a%d%d%d%d" % (half, b, j0, u))
                 first_layer(accs[half, b, j0, u], half, b, j0, QUARTER, (2 * u, 2 * u + 1), (g,))
@@ -210,7 +215,7 @@ def tile_list_rvq_gelu_none_kernel(tc, tab_words, tab_scales, w0_words, w0_scale
             for u in range(2):
                 opened = (half, b, j0, u) in accs
                 acc = accs[half, b, j0, u] if opened else bank("a%s%d" % (name, u))
-                first_layer(acc, half, b, j0, QUARTER, (2 * u, 2 * u + 1), (2,) if opened else (0, 1, 2))
+                first_layer(acc, half, b, j0, QUARTER, (2 * u, 2 * u + 1), range(done.get((half, b, j0, u), 0), 3))
                 nc.scalar.activation(act[:, u, :, :], acc[:].rearrange("p (e j) -> p j e", e=2), GELU)
             return act
 
@@ -263,15 +268,15 @@ def tile_list_rvq_gelu_none_kernel(tc, tab_words, tab_scales, w0_words, w0_scale
             nc.sync.dma_start(out_v[:, :, HALF * half + j0 : HALF * half + j0 + width], res[:])
 
         warm = psum.tile([P, 512], F32, name="warm", tag="bank7")
-        for i in range(4):
+        for plane in [gs[0, 1]] * 3 + [gs[1, 0]] * 2:
             nc.tensor.matmul_mx(
-                out=warm[:], lhsT=w[0, 0][:, 0:128].bitcast(FP8X4), lhsT_scale=gs[0, 2][:, 0:128],
-                rhs=w[0, 0][:].bitcast(FP8X4), rhs_scale=gs[0, 2][:], start=True, stop=True,
+                out=warm[:], lhsT=w[0, 0][:, 0:128].bitcast(FP8X4), lhsT_scale=plane[:, 0:128],
+                rhs=w[0, 0][:].bitcast(FP8X4), rhs_scale=plane[:], start=True, stop=True,
             )
         for g in range(2):
             for j0 in (0, 128):
                 open_narrow(0, 0, j0, g)
-            open_piece(0, 0, QUARTER, g)
+            open_piece(0, 0, QUARTER, g, (0, 1) if g == 0 else (0,))
         whole = [tile([P, 4 * HALF], BF16, "whole0")]
         for j0 in (0, 128):
             narrow_piece(0, 0, j0, nc.gpsimd, whole[0])

@@ -267,12 +267,6 @@ def tile_list_rvq_gelu_none_kernel(tc, tab_words, tab_scales, w0_words, w0_scale
             nc.scalar.copy(res[:], y[:].rearrange("p (nt j) -> p nt j", nt=2))
             nc.sync.dma_start(out_v[:, :, HALF * half + j0 : HALF * half + j0 + width], res[:])
 
-        warm = psum.tile([P, 512], F32, name="warm", tag="bank7")
-        for plane in [gs[0, 1]] * 3 + [gs[1, 0]] * 2:
-            nc.tensor.matmul_mx(
-                out=warm[:], lhsT=w[0, 0][:, 0:128].bitcast(FP8X4), lhsT_scale=plane[:, 0:128],
-                rhs=w[0, 0][:].bitcast(FP8X4), rhs_scale=plane[:], start=True, stop=True,
-            )
         for g in range(2):
             for j0 in (0, 128):
                 open_narrow(0, 0, j0, g)

@@ -20,7 +20,7 @@ MULT = mybir.AluOpType.mult
 P = 128
 HALF = 512
 QUARTER = 256
-SPLIT = 2048
+EIGHTH = 128
 
 
 def tile_list_rvq_gelu_none_kernel(tc, tab_words, tab_scales, w0_words, w0_scales, w1_words, w1_scales,
@@ -33,62 +33,59 @@ def tile_list_rvq_gelu_none_kernel(tc, tab_words, tab_scales, w0_words, w0_scale
         lay = ctx.enter_context(tc.tile_pool(name="lay", bufs=1))
         psum = ctx.enter_context(tc.psum_pool(name="psum", bufs=1))
 
-        def tile(shape, dtype, name, tag=None):
-            return keep.tile(shape, dtype, name=name, tag=tag or name, align_bytes=256)
+        def tile(shape, dtype, name):
+            return keep.tile(shape, dtype, name=name, align_bytes=256)
 
         def placed(shape, dtype, name, offset):
             return lay.tile(shape, dtype, name=name, offset=offset, align_bytes=256)
 
         at_tab = 0
-        at_w = {(g, b): 4 * T + 2048 * (3 * b + g) for b in range(2) for g in range(3)}
-        at_ws = at_w[2, 1] + 3 * 2048
-        at_acts = at_ws + 2048
-        at_hb = at_acts + 3 * 4096 + 1024
+        base0 = 4 * T
+        base1 = base0 + 4608 + 2048
+        at_w = {(2, 0): base0, (0, 0): base0 + 2048, (0, 1): base0 + 2304 + 256, (1, 1): base1, (1, 0): base1 + 1792, (2, 1): base1 + 2048}
+        at_sm = base0 + 2048 + 256
+        at_ws = base1 + 4096 + 2048
+        at_sorted = {(0, 1): at_ws - 1792, (1, 1): at_ws + 768, (2, 1): base1 - 1792}
 
         offsets = keep.tile([P, 3 * J // 16], U16, name="offsets")
         nc.sync.dma_start(offsets[:], offs)
 
         tab_plane = tile([P, T], U8, "tab_plane")
         ws_raw = placed([P, R], U8, "ws_raw", at_ws)
-        zeros = lay.tile([P, 4, 1024], I32, name="zeros", offset=at_w[0, 0] - 4096 + 128)
-        nc.gpsimd.memset(zeros[:, 0, 0:32], 0)
-        nc.gpsimd.memset(tab_plane[:, 0:SPLIT].bitcast(I32), 0)
+        zeros = lay.tile([P, 32], I32, name="zeros", offset=base0 - 64)
+        nc.gpsimd.memset(zeros[64:P, :], 0)
         nc.gpsimd.memset(ws_raw[0:64, :].bitcast(I32), 0)
-        nc.vector.memset(tab_plane[:, SPLIT:T].bitcast(I32), 0)
+        nc.vector.memset(tab_plane[:].bitcast(I32), 0)
         nc.vector.tensor_copy(
-            ws_raw[64:128, :].bitcast(I32).rearrange("p (a c) -> p a c", c=32), zeros[64:128, 0:1, 0:32].to_broadcast([64, R // 128, 32])
+            ws_raw[64:P, :].bitcast(I32).rearrange("p (a c) -> p a c", c=32), zeros[64:P, :].unsqueeze(1).to_broadcast([64, R // 128, 32])
         )
 
         w_raw = {}
 
         def load_w(g, b):
-            name = "w_raw%d%d" % (g, b)
-            w_raw[g, b] = tile([P, 512], I32, name) if (g, b) == (0, 0) else placed([P, 512], I32, name, at_w[g, b])
+            w_raw[g, b] = placed([P, 512], I32, "w_raw%d%d" % (g, b), at_w[g, b])
             nc.sync.dma_start(w_raw[g, b][:], w_words[g][0].rearrange("p r i -> p (r i)")[:, 2048 * b : 2048 * (b + 1)].bitcast(I32))
 
         def load_w_scales(eng, rows):
-            for q, g in rows:
+            for g, q in rows:
                 row = 32 * q + 4 * (g + 1)
                 eng.dma_start(ws_raw[row : row + 4, :].bitcast(I32), w_scales[g][0, 4 * q : 4 * q + 4, :].bitcast(I32))
 
         load_w(0, 0)
+        load_w(1, 0)
         for r in range(4):
             nc.sync.dma_start(tab_plane[r:P:32, :].bitcast(I32), tab_scales[0, r:16:4, :].bitcast(I32))
-        rows = [(q, g) for q in range(4) for g in range(3)]
-        load_w_scales(nc.gpsimd, rows[0:4])
-        load_w_scales(nc.sync, rows[4:5])
-        load_w(1, 0)
+        rows = [(g, q) for q in range(4) for g in range(3)]
+        load_w_scales(nc.gpsimd, rows[0:6])
         tab = placed([P, T], I32, "tab", at_tab)
         nc.sync.dma_start(tab[:], tab_words[0].rearrange("p t i -> p (t i)").bitcast(I32))
-        load_w_scales(nc.sync, rows[5:12])
-        for g, b in ((2, 0), (0, 1), (1, 1), (2, 1)):
-            load_w(g, b)
-        sm_t = placed([P, 2, 4], F32, "sm_t", at_w[0, 0])
+        load_w_scales(nc.sync, rows[6:12])
+        load_w(2, 0)
+        load_w(0, 1)
+        sm_t = placed([P, 2, 4], F32, "sm_t", at_sm)
         nc.sync.dma_start(sm_t[:], sm.rearrange("(b p t) -> p b t", b=2, t=4))
-
-        def entries(half, g):
-            c0 = (J * g + HALF * half) // 16
-            return offsets[:, c0 : c0 + HALF // 16]
+        load_w(1, 1)
+        load_w(2, 1)
 
         gs = {}
         gw = {}
@@ -96,46 +93,60 @@ def tile_list_rvq_gelu_none_kernel(tc, tab_words, tab_scales, w0_words, w0_scale
         def gather_plane(half, g, offset=None):
             name = "gs%d%d" % (half, g)
             gs[half, g] = tile([P, HALF], U8, name) if offset is None else placed([P, HALF], U8, name, offset)
-            nc.vector.tensor_copy(gs[half, g][:], tab_plane[:].indirect(entries(half, g)))
+            c0 = (J * g + HALF * half) // 16
+            nc.vector.tensor_copy(gs[half, g][:], tab_plane[:].indirect(offsets[:, c0 : c0 + HALF // 16]))
 
-        def gather_words(half, g, offset=None):
-            name = "gw%d%d" % (half, g)
-            gw[half, g] = tile([P, HALF], U32, name) if offset is None else placed([P, HALF], U32, name, offset)
-            nc.vector.tensor_copy(gw[half, g][:], tab[:].bitcast(U32).indirect(entries(half, g)))
+        def gather_words(q, g, offset=None):
+            name = "gw%d%d" % (q, g)
+            if offset is None:
+                gw[q, g] = keep.tile([P, QUARTER], U32, name=name, tag="gw%d%d" % (q % 3, g), align_bytes=256)
+            else:
+                gw[q, g] = placed([P, QUARTER], U32, name, offset)
+            c0 = (J * g + QUARTER * q) // 16
+            nc.vector.tensor_copy(gw[q, g][:], tab[:].bitcast(U32).indirect(offsets[:, c0 : c0 + QUARTER // 16]))
 
         w = {}
 
-        def sort_words(g, b, eng=nc.vector):
-            w[g, b] = tile([P, 512], I32, "w%d%d" % (g, b))
-            eng.tensor_copy(
-                w[g, b][:].rearrange("p (t c i) -> p c t i", t=4, i=4), w_raw[g, b][:].rearrange("p (c i t) -> p c t i", t=4, i=4)
-            )
+        def sort_words(g, b, on):
+            name = "w%d%d" % (g, b)
+            w[g, b] = placed([P, 512], U32, name, at_sorted[g, b]) if (g, b) in at_sorted else tile([P, 512], U32, name)
+            dst = w[g, b][:].rearrange("p (t c i) -> p c t i", t=4, i=4)
+            src = w_raw[g, b][:].bitcast(U32).rearrange("p (c i t) -> p c t i", t=4, i=4)
+            if on == "scalar":
+                nc.scalar.copy(dst, src)
+            else:
+                nc.gpsimd.tensor_copy(dst, src)
 
-        sort_words(0, 0)
-        for half, g in ((0, 0), (0, 1), (0, 2), (1, 0)):
-            gather_plane(half, g)
-        gather_words(0, 0)
-        ws = [tile([P, HALF], U8, "ws0"), tile([P, HALF], U8, "ws1")]
+        ws = {}
 
-        def sort_scales(eng, b):
-            eng.tensor_copy(ws[b][:].rearrange("p (t m) -> p t m", t=4), ws_raw[:, HALF * b : HALF * (b + 1)].rearrange("p (m t) -> p t m", t=4))
+        def sort_scales(b, pieces):
+            ws[b] = tile([P, HALF], U8, "ws%d" % b)
+            n = 4 // pieces
+            for i in range(pieces):
+                nc.gpsimd.tensor_copy(
+                    ws[b][:].rearrange("p (t m) -> p t m", t=4)[:, n * i : n * (i + 1), :],
+                    ws_raw[:, HALF * b : HALF * (b + 1)].rearrange("p (m t) -> p t m", t=4)[:, n * i : n * (i + 1), :],
+                )
 
-        sort_words(1, 0, nc.gpsimd)
-        sort_scales(nc.gpsimd, 0)
-        sort_scales(nc.gpsimd, 1)
-        gather_words(0, 1)
-        gather_words(0, 2)
-        sort_words(2, 0, nc.gpsimd)
         for g in range(3):
-            sort_words(g, 1)
-        gather_words(1, 0, at_w[0, 1])
-        gather_plane(1, 1, at_w[1, 1])
-        gather_words(1, 1, at_w[2, 1] - 1024)
-        gather_plane(1, 2, at_w[2, 1] + 1024)
-        gather_words(1, 2, at_w[2, 1] + 1536)
-        wd = placed([P, 2 * 2 * N], U8, "wd", at_w[2, 0] + 256)
+            gather_plane(0, g)
+        for q in range(2):
+            for g in range(3):
+                gather_words(q, g)
+        for g, b in ((0, 0), (1, 0), (2, 0)):
+            sort_words(g, b, "scalar")
+        sort_scales(0, 2)
+        sort_scales(1, 1)
+        sort_words(0, 1, "gpsimd")
+        sort_words(1, 1, "gpsimd")
+        sort_words(2, 1, "scalar")
+        for g in range(3):
+            gather_plane(1, g, at_w[g, 1] + 256)
+            gather_words(2, g, at_w[g, 1] + 768)
+
+        wd = placed([P, 2 * 2 * N], U8, "wd", at_w[2, 0])
         nc.sync.dma_start(wd[:].bitcast(I32).rearrange("p (a c) -> p a c", a=2), wd_words.bitcast(I32).rearrange("a p c -> p a c"))
-        wd_plane = placed([P, 2 * N], U8, "wd_plane", at_w[2, 0] + 256 + 1024)
+        wd_plane = placed([P, 2 * N], U8, "wd_plane", at_ws + 256)
         nc.gpsimd.memset(wd_plane[:].bitcast(I32), 0)
         for q in range(4):
             nc.sync.dma_start(
@@ -143,8 +154,6 @@ def tile_list_rvq_gelu_none_kernel(tc, tab_words, tab_scales, w0_words, w0_scale
                 wd_scales[:, 4 * q : 4 * q + 4, :].bitcast(I32).rearrange("a r c -> r a c"),
             )
 
-
-        sm_of = [sm_t[:, b, :] for b in range(2)]
         codes = [[tile([P, HALF], U32, "codes%d%d" % (half, b)) for b in range(2)] for half in range(2)]
         planes = [[tile([P, HALF], U8, "plane%d%d" % (half, b)) for b in range(2)] for half in range(2)]
         next_bank = [0]
@@ -154,86 +163,60 @@ def tile_list_rvq_gelu_none_kernel(tc, tab_words, tab_scales, w0_words, w0_scale
             next_bank[0] = next_bank[0] + 1
             return t_
 
-        def first_layer(acc, half, b, j0, width, ts, gs_now=(0, 1, 2)):
-            for g in gs_now:
-                for e in range(len(ts)):
-                    r0 = 128 * ts[e]
+        def first_layer(accs, q, b, j0, width):
+            per_bank = 4 // len(accs)
+            s0 = QUARTER * (q % 2) + j0
+            for g in range(3):
+                for t in range(4):
+                    e = t % per_bank
                     nc.tensor.matmul_mx(
-                        out=acc[:, e * width : (e + 1) * width],
-                        lhsT=w[g, b][:, r0 : r0 + 128].bitcast(FP8X4),
-                        lhsT_scale=ws[b][4 * (g + 1) : P, r0 : r0 + 128],
-                        rhs=gw[half, g][:, j0 : j0 + width].bitcast(FP8X4),
-                        rhs_scale=gs[half, g][:, j0 : j0 + width],
+                        out=accs[t // per_bank][:, e * width : (e + 1) * width],
+                        lhsT=w[g, b][:, 128 * t : 128 * (t + 1)].bitcast(FP8X4),
+                        lhsT_scale=ws[b][4 * (g + 1) : P, 128 * t : 128 * (t + 1)],
+                        rhs=gw[q, g][:, j0 : j0 + width].bitcast(FP8X4),
+                        rhs_scale=gs[q // 2, g][:, s0 : s0 + width],
                         start=(g == 0 and e == 0),
-                        stop=(g == 2 and e == len(ts) - 1),
+                        stop=(g == 2 and e == per_bank - 1),
                     )
+
+        def wide_unit(q, b):
+            act = tile([P, 2, QUARTER, 2], F32, "act%d%d" % (q, b))
+            accs = [bank("a%d%d%d" % (q, b, u)) for u in range(2)]
+            first_layer(accs, q, b, 0, QUARTER)
+            for u in range(2):
+                nc.scalar.activation(act[:, u, :, :], accs[u][:].rearrange("p (e j) -> p j e", e=2), GELU)
+            return act
+
+        def narrow_unit(q, b, j0):
+            act = tile([P, EIGHTH, 4], F32, "nact%d%d%d" % (q, b, j0))
+            acc = bank("n%d%d%d" % (q, b, j0))
+            first_layer([acc], q, b, j0, EIGHTH)
+            nc.scalar.activation(act[:], acc[:].rearrange("p (t j) -> p j t", t=4), GELU)
+            return act
+
+        def smooth(eng, act, b, lo, hi, hb):
+            eng.tensor_tensor(
+                hb.rearrange("p (j u e) -> p j u e", u=2, e=2),
+                act[:, :, lo:hi, :].rearrange("p u j e -> p j u e"),
+                sm_t[:, b, :].rearrange("p (u e) -> p u e", u=2).unsqueeze(1).to_broadcast([P, hi - lo, 2, 2]),
+                MULT,
+            )
+
+        def smooth_narrow(eng, act, b, hb):
+            eng.tensor_tensor(hb.rearrange("p (j t) -> p j t", t=4), act[:], sm_t[:, b, :].unsqueeze(1).to_broadcast([P, EIGHTH, 4]), MULT)
+
+        def smooth_scalar(act, b, lo, hi, hb, name):
+            hp = tile([P, 4, hi - lo], BF16, name)
+            for t in range(4):
+                nc.scalar.activation(hp[:, t, :], act[:, t // 2, lo:hi, t % 2], COPY, scale=sm_t[:, b, t : t + 1])
+            nc.scalar.copy(hb.rearrange("p (c i t) -> p c t i", i=4, t=4), hp[:].rearrange("p t (c i) -> p c t i", i=4))
 
         def quantise(hb, half, b, j0, width):
             nc.vector.quantize_mx(
                 out=codes[half][b][:, j0 : j0 + width].bitcast(FP8X4), scales=planes[half][b][:, j0 : j0 + width], in_=hb
             )
 
-        accs = {}
-        done = {}
-
-        def open_piece(half, b, j0, g, us=(0, 1)):
-            for u in us:
-                done[half, b, j0, u] = g + 1
-                if g == 0:
-                    accs[half, b, j0, u] = bank("a%d%d%d%d" % (half, b, j0, u))
-                first_layer(accs[half, b, j0, u], half, b, j0, QUARTER, (2 * u, 2 * u + 1), (g,))
-
-        def smooth(act, half, b, j0, lo, hi, on, into=None):
-            name = "%d%d%d" % (half, b, j0 + lo)
-            width = hi - lo
-            if into is not None:
-                hb = into[:, 4 * (j0 + lo) : 4 * (j0 + hi)]
-            elif half == 0 and on != "gpsimd":
-                hb = placed([P, 4 * width], BF16, "hb" + name, at_hb + 8 * (j0 + lo))[:]
-            else:
-                hb = tile([P, 4 * width], BF16, "hb" + name)[:]
-            if on == "scalar":
-                hp = placed([P, 48, width], BF16, "hp" + name, at_acts)[:, 0:4, :] if j0 == QUARTER else tile([P, 4, width], BF16, "hp" + name)[:]
-                for t in range(4):
-                    nc.scalar.activation(hp[:, t, :], act[:, t // 2, lo:hi, t % 2], COPY, scale=sm_t[:, b, t : t + 1])
-                nc.scalar.copy(hb.rearrange("p (c i t) -> p c t i", i=4, t=4), hp.rearrange("p t (c i) -> p c t i", i=4))
-            else:
-                eng = nc.gpsimd if on == "gpsimd" else nc.vector
-                eng.tensor_tensor(
-                    hb.rearrange("p (j u e) -> p j u e", u=2, e=2),
-                    act[:, :, lo:hi, :].rearrange("p u j e -> p j u e"),
-                    sm_of[b].rearrange("p (u e) -> p u e", u=2).unsqueeze(1).to_broadcast([P, width, 2, 2]),
-                    MULT,
-                )
-            if into is None:
-                quantise(hb, half, b, j0 + lo, width)
-
-        def wide_piece(half, b, j0, offset=None):
-            name = "act%d%d%d" % (half, b, j0)
-            shape = [P, 2, QUARTER, 2]
-            act = tile(shape, F32, name) if offset is None else placed(shape, F32, name, offset)
-            for u in range(2):
-                opened = (half, b, j0, u) in accs
-                acc = accs[half, b, j0, u] if opened else bank("a%s%d" % (name, u))
-                first_layer(acc, half, b, j0, QUARTER, (2 * u, 2 * u + 1), range(done.get((half, b, j0, u), 0), 3))
-                nc.scalar.activation(act[:, u, :, :], acc[:].rearrange("p (e j) -> p j e", e=2), GELU)
-            return act
-
-        def open_narrow(half, b, j0, g):
-            if g == 0:
-                accs[half, b, j0] = bank("n%d%d%d" % (half, b, j0))
-            first_layer(accs[half, b, j0], half, b, j0, 128, (0, 1, 2, 3), (g,))
-
-        def narrow_piece(half, b, j0, eng, into=None):
-            name = "%d%d%d" % (half, b, j0)
-            act = tile([P, 128, 4], F32, "nact" + name)
-            for g in range(2 if (half, b, j0) in accs else 0, 3):
-                open_narrow(half, b, j0, g)
-            nc.scalar.activation(act[:], accs[half, b, j0][:].rearrange("p (t j) -> p j t", t=4), GELU)
-            hb = tile([P, 512], BF16, "nhb" + name)[:] if into is None else into[:, 4 * j0 : 4 * j0 + 512]
-            eng.tensor_tensor(hb.rearrange("p (j t) -> p j t", t=4), act[:], sm_of[b].unsqueeze(1).to_broadcast([P, 128, 4]), MULT)
-            if into is None:
-                quantise(hb, half, b, j0, 128)
+        out_v = out.rearrange("(nt p) j -> p nt j", p=P)
 
         def second_pass(y, half, b, nt, j0, width, start, stop):
             nc.tensor.matmul_mx(
@@ -246,57 +229,60 @@ def tile_list_rvq_gelu_none_kernel(tc, tab_words, tab_scales, w0_words, w0_scale
                 stop=stop,
             )
 
-        def second_layer_wide(half, nt):
-            y = bank("yw%d%d" % (half, nt))
-            for b in range(2):
-                second_pass(y[:], half, b, nt, 0, HALF, b == 0, b == 1)
-            res = tile([P, HALF], F32, "resw%d%d" % (half, nt))
-            nc.scalar.copy(res[:], y[:])
-            nc.sync.dma_start(out[P * nt : P * (nt + 1), HALF * half : HALF * (half + 1)], res[:])
-
-        out_v = out.rearrange("(nt p) j -> p nt j", p=P)
-
         def second_layer(half, j0, width):
             y = bank("y%d%d" % (half, j0), 2 * width)
-            blocks = [(b, nt, j) for b in range(2) for nt in range(2) for j in range(0, width, 128)]
-            for b, nt, j in blocks:
-                second_pass(
-                    y[:, nt * width + j : nt * width + j + 128], half, b, nt, j0 + j, 128, (b, nt, j) == blocks[0], (b, nt, j) == blocks[-1]
-                )
+            for b in range(2):
+                for nt in range(2):
+                    second_pass(y[:, nt * width : (nt + 1) * width], half, b, nt, j0, width, b == 0 and nt == 0, b == 1 and nt == 1)
+            store(y, half, j0, width)
+
+        def store(y, half, j0, width):
             res = tile([P, 2, width], F32, "res%d%d" % (half, j0))
             nc.scalar.copy(res[:], y[:].rearrange("p (nt j) -> p nt j", nt=2))
             nc.sync.dma_start(out_v[:, :, HALF * half + j0 : HALF * half + j0 + width], res[:])
 
-        for g in range(2):
-            for j0 in (0, 128):
-                open_narrow(0, 0, j0, g)
-            open_piece(0, 0, QUARTER, g, (0, 1) if g == 0 else (0,))
-        whole = [tile([P, 4 * HALF], BF16, "whole0")]
-        for j0 in (0, 128):
-            narrow_piece(0, 0, j0, nc.gpsimd, whole[0])
-        smooth(wide_piece(0, 0, QUARTER), 0, 0, QUARTER, 0, QUARTER, "gpsimd", whole[0])
-        quantise(whole[0][:], 0, 0, 0, HALF)
-        third = wide_piece(0, 1, 0)
-        smooth(third, 0, 1, 0, 0, 128, "gpsimd")
-        middle = placed([P, 4 * HALF], BF16, "middle", at_hb - 1024)
-        smooth(third, 0, 1, 0, 128, QUARTER, "scalar", middle)
-        fourth = wide_piece(0, 1, QUARTER)
-        smooth(fourth, 0, 1, QUARTER, 0, 128, "scalar", middle)
-        quantise(middle[:, 512:1536], 0, 1, 128, QUARTER)
-        smooth(fourth, 0, 1, QUARTER, 128, QUARTER, "vector")
-        whole.append(placed([P, 4 * HALF], BF16, "whole1", at_hb))
-        late = ((0, 0), (0, QUARTER), (1, 0))
-        for g in range(2):
-            for b, j0 in late[:2]:
-                open_piece(1, b, j0, g)
-        for i, (b, j0) in enumerate(late):
-            smooth(wide_piece(1, b, j0, at_acts + 4096 * i), 1, b, j0, 0, QUARTER, "vector", whole[1] if b == 0 else None)
-            if i == 1:
-                quantise(whole[1][:], 1, 0, 0, HALF)
-        narrow_piece(1, 1, 256, nc.vector)
-        narrow_piece(1, 1, 384, nc.vector)
-        second_layer_wide(0, 0)
-        second_layer_wide(0, 1)
-        second_layer(1, 0, QUARTER)
-        second_layer(1, 256, 128)
-        second_layer(1, 384, 128)
+        hb0 = tile([P, 4 * HALF], BF16, "hb0")
+        for j0 in (0, EIGHTH):
+            smooth_narrow(nc.gpsimd, narrow_unit(0, 0, j0), 0, hb0[:, 4 * j0 : 4 * (j0 + EIGHTH)])
+        act = wide_unit(1, 0)
+        for lo in (0, EIGHTH):
+            j0 = QUARTER + lo
+            smooth(nc.gpsimd, act, 0, lo, lo + EIGHTH, hb0[:, 4 * j0 : 4 * (j0 + EIGHTH)])
+        hb_first = tile([P, 4 * EIGHTH], BF16, "hb_first")
+        hb_second = tile([P, 4 * EIGHTH], BF16, "hb_second")
+        act = wide_unit(0, 1)
+        smooth(nc.gpsimd, act, 1, 0, EIGHTH, hb_first[:])
+        smooth_scalar(act, 1, EIGHTH, QUARTER, hb_second[:], "hp0")
+        for g in range(3):
+            gather_words(3, g)
+
+        def late_unit(q, b):
+            hb = tile([P, 4 * QUARTER], BF16, "hb%d%d" % (q, b))
+            smooth(nc.vector, wide_unit(q, b), b, 0, QUARTER, hb[:])
+            return hb
+
+        hb = late_unit(1, 1)
+        quantise(hb0[:], 0, 0, 0, HALF)
+        quantise(hb_first[:], 0, 1, 0, EIGHTH)
+        quantise(hb_second[:], 0, 1, EIGHTH, EIGHTH)
+        quantise(hb[:], 0, 1, QUARTER, QUARTER)
+        for q, b in ((2, 0), (2, 1), (3, 0)):
+            quantise(late_unit(q, b)[:], 1, b, QUARTER * (q - 2), QUARTER)
+        narrow = []
+        for j0 in (0, EIGHTH):
+            act = narrow_unit(3, 1, j0)
+            hb = tile([P, 4 * EIGHTH], BF16, "nhb%d" % j0)
+            smooth_narrow(nc.vector, act, 1, hb[:])
+            narrow.append(hb)
+        for half, j0 in ((0, 0), (0, QUARTER), (1, 0)):
+            second_layer(half, j0, QUARTER)
+        ys = [bank("ylast%d" % i, QUARTER) for i in range(2)]
+        for b in range(2):
+            for i in range(2):
+                j0 = QUARTER + EIGHTH * i
+                if b == 1:
+                    quantise(narrow[i][:], 1, 1, j0, EIGHTH)
+                for nt in range(2):
+                    second_pass(ys[i][:, nt * EIGHTH : (nt + 1) * EIGHTH], 1, b, nt, j0, EIGHTH, b == 0 and nt == 0, b == 1 and nt == 1)
+                if b == 1:
+                    store(ys[i], 1, j0, EIGHTH)

@@ -21,6 +21,9 @@ P = 128
 HALF = 512
 QUARTER = 256
 EIGHTH = 128
+WARM_PASSES = 5
+TAB_EARLY = 512
+TAB_PIECES = ((TAB_EARLY, 1792), (1792, 2560), (2560, T))
 
 
 def tile_list_rvq_gelu_none_kernel(tc, tab_words, tab_scales, w0_words, w0_scales, w1_words, w1_scales,
@@ -41,77 +44,85 @@ def tile_list_rvq_gelu_none_kernel(tc, tab_words, tab_scales, w0_words, w0_scale
 
         at_tab = 0
         base0 = 4 * T
-        base1 = base0 + 4608 + 2048
-        at_w = {(2, 0): base0, (0, 0): base0 + 2048, (0, 1): base0 + 2304 + 256, (1, 1): base1, (1, 0): base1 + 1792, (2, 1): base1 + 2048}
-        at_sm = base0 + 2048 + 256
-        at_ws = base1 + 4096 + 2048
-        at_sorted = {(0, 1): at_ws - 1792, (1, 1): at_ws + 768, (2, 1): base1 - 1792}
+        at_w = {(0, 1): base0 + 4096, (1, 0): base0 + 6144, (1, 1): base0 + 8192, (2, 1): base0 + 10240, (0, 0): base0 + 12032, (2, 0): base0 + 13824}
+        at_sm = base0 + 12288
+        at_ws = base0 + 20480
+        at_act = at_ws + 1024
 
         offsets = keep.tile([P, 3 * J // 16], U16, name="offsets")
         nc.sync.dma_start(offsets[:], offs)
 
         tab_plane = tile([P, T], U8, "tab_plane")
         ws_raw = placed([P, R], U8, "ws_raw", at_ws)
-        zeros = lay.tile([P, 32], I32, name="zeros", offset=base0 - 64)
-        nc.gpsimd.memset(zeros[64:P, :], 0)
-        nc.gpsimd.memset(ws_raw[0:64, :].bitcast(I32), 0)
+        tab = placed([P, T], I32, "tab", at_tab)
+        zeros = tab[:].rearrange("p (a c) -> p a c", c=1024)[:, 0:4, 960:1024]
+        nc.gpsimd.memset(ws_raw[0:32, :].bitcast(I32), 0)
         nc.vector.memset(tab_plane[:].bitcast(I32), 0)
-        nc.vector.tensor_copy(
-            ws_raw[64:P, :].bitcast(I32).rearrange("p (a c) -> p a c", c=32), zeros[64:P, :].unsqueeze(1).to_broadcast([64, R // 128, 32])
-        )
+        nc.gpsimd.memset(zeros[32:64], 0)
+        nc.vector.memset(zeros[64:P], 0)
+        for lo, hi in ((32, 64), (64, P)):
+            nc.vector.tensor_copy(ws_raw[lo:hi, :].bitcast(I32).rearrange("p (a c) -> p a c", c=64), zeros[lo:hi])
+
+        warm = tile([P, 2], F32, "warm")
+        nc.vector.memset(warm[:, 0:1], 0.0)
+        nc.scalar.activation(warm[:, 1:2], warm[:, 0:1], GELU)
 
         w_raw = {}
+        for name, halves in (("w_first", ((0, 0),)), ("w_low", ((0, 1), (1, 0), (1, 1), (2, 1))), ("w_high", ((2, 0),))):
+            raw = placed([P, 512 * len(halves)], I32, name, at_w[halves[0]])
+            for i, key in enumerate(halves):
+                w_raw[key] = raw[:, 512 * i : 512 * (i + 1)]
 
         def load_w(g, b):
-            w_raw[g, b] = placed([P, 512], I32, "w_raw%d%d" % (g, b), at_w[g, b])
-            nc.sync.dma_start(w_raw[g, b][:], w_words[g][0].rearrange("p r i -> p (r i)")[:, 2048 * b : 2048 * (b + 1)].bitcast(I32))
+            nc.sync.dma_start(w_raw[g, b], w_words[g][0].rearrange("p r i -> p (r i)")[:, 2048 * b : 2048 * (b + 1)].bitcast(I32))
 
         def load_w_scales(eng, rows):
             for g, q in rows:
                 row = 32 * q + 4 * (g + 1)
                 eng.dma_start(ws_raw[row : row + 4, :].bitcast(I32), w_scales[g][0, 4 * q : 4 * q + 4, :].bitcast(I32))
 
+        rows = [(g, q) for q in range(4) for g in range(3)]
         load_w(0, 0)
-        load_w(1, 0)
+        words = tab_words[0].rearrange("p t i -> p (t i)").bitcast(I32)
+        nc.sync.dma_start(tab[:, 0:TAB_EARLY], words[:, 0:TAB_EARLY])
         for r in range(4):
             nc.sync.dma_start(tab_plane[r:P:32, :].bitcast(I32), tab_scales[0, r:16:4, :].bitcast(I32))
-        rows = [(g, q) for q in range(4) for g in range(3)]
-        load_w_scales(nc.gpsimd, rows[0:6])
-        tab = placed([P, T], I32, "tab", at_tab)
-        nc.sync.dma_start(tab[:], tab_words[0].rearrange("p t i -> p (t i)").bitcast(I32))
-        load_w_scales(nc.sync, rows[6:12])
-        load_w(2, 0)
-        load_w(0, 1)
+        load_w_scales(nc.gpsimd, rows[0:4])
+        for (lo, hi), behind in zip(TAB_PIECES, (rows[4:5], rows[5:9], rows[9:12])):
+            nc.sync.dma_start(tab[:, lo:hi], words[:, lo:hi])
+            load_w_scales(nc.sync, behind)
+        for g, b in ((1, 0), (2, 0), (0, 1), (1, 1), (2, 1)):
+            load_w(g, b)
         sm_t = placed([P, 2, 4], F32, "sm_t", at_sm)
         nc.sync.dma_start(sm_t[:], sm.rearrange("(b p t) -> p b t", b=2, t=4))
-        load_w(1, 1)
-        load_w(2, 1)
 
         gs = {}
         gw = {}
 
-        def gather_plane(half, g, offset=None):
-            name = "gs%d%d" % (half, g)
-            gs[half, g] = tile([P, HALF], U8, name) if offset is None else placed([P, HALF], U8, name, offset)
-            c0 = (J * g + HALF * half) // 16
-            nc.vector.tensor_copy(gs[half, g][:], tab_plane[:].indirect(offsets[:, c0 : c0 + HALF // 16]))
+        late_planes = placed([P, 3 * HALF], U8, "late_planes", at_w[2, 0] + 256)
+        late_words = placed([P, 4 * QUARTER], U32, "late_words", at_w[2, 0] + 1792)
 
-        def gather_words(q, g, offset=None):
-            name = "gw%d%d" % (q, g)
-            if offset is None:
-                gw[q, g] = keep.tile([P, QUARTER], U32, name=name, tag="gw%d%d" % (q % 3, g), align_bytes=256)
+        def gather_plane(half, g):
+            gs[half, g] = late_planes[:, HALF * g : HALF * (g + 1)] if half else tile([P, HALF], U8, "gs%d" % g)[:]
+            c0 = (J * g + HALF * half) // 16
+            nc.vector.tensor_copy(gs[half, g], tab_plane[:].indirect(offsets[:, c0 : c0 + HALF // 16]))
+
+        late = ((1, 1), (2, 0), (2, 1), (2, 2))
+
+        def gather_words(q, g):
+            if (q, g) in late:
+                gw[q, g] = late_words[:, QUARTER * late.index((q, g)) : QUARTER * (late.index((q, g)) + 1)]
             else:
-                gw[q, g] = placed([P, QUARTER], U32, name, offset)
+                gw[q, g] = keep.tile([P, QUARTER], U32, name="gw%d%d" % (q, g), tag="gw%d%d" % (q % 3, g), align_bytes=256)[:]
             c0 = (J * g + QUARTER * q) // 16
-            nc.vector.tensor_copy(gw[q, g][:], tab[:].bitcast(U32).indirect(offsets[:, c0 : c0 + QUARTER // 16]))
+            nc.vector.tensor_copy(gw[q, g], tab[:].bitcast(U32).indirect(offsets[:, c0 : c0 + QUARTER // 16]))
 
         w = {}
 
         def sort_words(g, b, on):
-            name = "w%d%d" % (g, b)
-            w[g, b] = placed([P, 512], U32, name, at_sorted[g, b]) if (g, b) in at_sorted else tile([P, 512], U32, name)
+            w[g, b] = tile([P, 512], U32, "w%d%d" % (g, b))
             dst = w[g, b][:].rearrange("p (t c i) -> p c t i", t=4, i=4)
-            src = w_raw[g, b][:].bitcast(U32).rearrange("p (c i t) -> p c t i", t=4, i=4)
+            src = w_raw[g, b].bitcast(U32).rearrange("p (c i t) -> p c t i", t=4, i=4)
             if on == "scalar":
                 nc.scalar.copy(dst, src)
             else:
@@ -120,39 +131,30 @@ def tile_list_rvq_gelu_none_kernel(tc, tab_words, tab_scales, w0_words, w0_scale
         ws = {}
 
         def sort_scales(b, pieces):
-            ws[b] = tile([P, HALF], U8, "ws%d" % b)
             n = 4 // pieces
             for i in range(pieces):
+                part = tile([P, 128 * n], U8, "ws%d%d" % (b, i))
                 nc.gpsimd.tensor_copy(
-                    ws[b][:].rearrange("p (t m) -> p t m", t=4)[:, n * i : n * (i + 1), :],
+                    part[:].rearrange("p (t m) -> p t m", t=n),
                     ws_raw[:, HALF * b : HALF * (b + 1)].rearrange("p (m t) -> p t m", t=4)[:, n * i : n * (i + 1), :],
                 )
+                for e in range(n):
+                    ws[b, n * i + e] = part[:, 128 * e : 128 * (e + 1)]
 
         for g in range(3):
             gather_plane(0, g)
-        for q in range(2):
-            for g in range(3):
-                gather_words(q, g)
+        for q, g in ((0, 0), (1, 0), (0, 1), (0, 2)):
+            gather_words(q, g)
+        gather_words(1, 1)
+        gather_words(1, 2)
         for g, b in ((0, 0), (1, 0), (2, 0)):
             sort_words(g, b, "scalar")
         sort_scales(0, 2)
         sort_scales(1, 1)
         sort_words(0, 1, "gpsimd")
-        sort_words(1, 1, "gpsimd")
-        sort_words(2, 1, "scalar")
         for g in range(3):
-            gather_plane(1, g, at_w[g, 1] + 256)
-            gather_words(2, g, at_w[g, 1] + 768)
-
-        wd = placed([P, 2 * 2 * N], U8, "wd", at_w[2, 0])
-        nc.sync.dma_start(wd[:].bitcast(I32).rearrange("p (a c) -> p a c", a=2), wd_words.bitcast(I32).rearrange("a p c -> p a c"))
-        wd_plane = placed([P, 2 * N], U8, "wd_plane", at_ws + 256)
-        nc.gpsimd.memset(wd_plane[:].bitcast(I32), 0)
-        for q in range(4):
-            nc.sync.dma_start(
-                wd_plane[32 * q : 32 * q + 4, :].bitcast(I32).rearrange("p (a c) -> p a c", a=2),
-                wd_scales[:, 4 * q : 4 * q + 4, :].bitcast(I32).rearrange("a r c -> r a c"),
-            )
+            gather_plane(1, g)
+            gather_words(2, g)
 
         codes = [[tile([P, HALF], U32, "codes%d%d" % (half, b)) for b in range(2)] for half in range(2)]
         planes = [[tile([P, HALF], U8, "plane%d%d" % (half, b)) for b in range(2)] for half in range(2)]
@@ -163,34 +165,35 @@ def tile_list_rvq_gelu_none_kernel(tc, tab_words, tab_scales, w0_words, w0_scale
             next_bank[0] = next_bank[0] + 1
             return t_
 
-        def first_layer(accs, q, b, j0, width):
+        def first_layer(accs, q, b, j0, width, order):
             per_bank = 4 // len(accs)
             s0 = QUARTER * (q % 2) + j0
-            for g in range(3):
+            for g in order:
                 for t in range(4):
                     e = t % per_bank
                     nc.tensor.matmul_mx(
                         out=accs[t // per_bank][:, e * width : (e + 1) * width],
                         lhsT=w[g, b][:, 128 * t : 128 * (t + 1)].bitcast(FP8X4),
-                        lhsT_scale=ws[b][4 * (g + 1) : P, 128 * t : 128 * (t + 1)],
+                        lhsT_scale=ws[b, t][4 * (g + 1) : P, :],
                         rhs=gw[q, g][:, j0 : j0 + width].bitcast(FP8X4),
                         rhs_scale=gs[q // 2, g][:, s0 : s0 + width],
                         start=(g == 0 and e == 0),
                         stop=(g == 2 and e == per_bank - 1),
                     )
 
-        def wide_unit(q, b):
-            act = tile([P, 2, QUARTER, 2], F32, "act%d%d" % (q, b))
-            accs = [bank("a%d%d%d" % (q, b, u)) for u in range(2)]
-            first_layer(accs, q, b, 0, QUARTER)
+        def wide_unit(q, b, opened=None):
+            shape, name = [P, 2, QUARTER, 2], "act%d%d" % (q, b)
+            act = placed(shape, F32, name, at_act) if (q, b) == (0, 1) else tile(shape, F32, name)
+            accs = opened or [bank("a%d%d%d" % (q, b, u)) for u in range(2)]
+            first_layer(accs, q, b, 0, QUARTER, (1, 2) if opened else (0, 1, 2))
             for u in range(2):
                 nc.scalar.activation(act[:, u, :, :], accs[u][:].rearrange("p (e j) -> p j e", e=2), GELU)
             return act
 
-        def narrow_unit(q, b, j0):
+        def narrow_unit(q, b, j0, opened=None):
             act = tile([P, EIGHTH, 4], F32, "nact%d%d%d" % (q, b, j0))
-            acc = bank("n%d%d%d" % (q, b, j0))
-            first_layer([acc], q, b, j0, EIGHTH)
+            acc = opened or bank("n%d%d%d" % (q, b, j0))
+            first_layer([acc], q, b, j0, EIGHTH, (2,) if opened else (0, 1, 2))
             nc.scalar.activation(act[:], acc[:].rearrange("p (t j) -> p j t", t=4), GELU)
             return act
 
@@ -241,18 +244,45 @@ def tile_list_rvq_gelu_none_kernel(tc, tab_words, tab_scales, w0_words, w0_scale
             nc.scalar.copy(res[:], y[:].rearrange("p (nt j) -> p nt j", nt=2))
             nc.sync.dma_start(out_v[:, :, HALF * half + j0 : HALF * half + j0 + width], res[:])
 
+        idle = bank("idle")
+        for i in range(WARM_PASSES):
+            nc.tensor.matmul_mx(
+                out=idle[:], lhsT=w[0, 0][:, 0:128].bitcast(FP8X4), lhsT_scale=gs[0, 0][:, 0:128],
+                rhs=w[0, 0][:].bitcast(FP8X4), rhs_scale=gs[0, 0], start=True, stop=True,
+            )
+        next_bank[0] = 0
         hb0 = tile([P, 4 * HALF], BF16, "hb0")
-        for j0 in (0, EIGHTH):
-            smooth_narrow(nc.gpsimd, narrow_unit(0, 0, j0), 0, hb0[:, 4 * j0 : 4 * (j0 + EIGHTH)])
-        act = wide_unit(1, 0)
+        first = {j0: bank("first%d" % j0) for j0 in (0, EIGHTH)}
+        second = [bank("second%d" % u) for u in range(2)]
+        for j0 in first:
+            first_layer([first[j0]], 0, 0, j0, EIGHTH, (0,))
+        first_layer(second, 1, 0, 0, QUARTER, (0,))
+        for j0 in first:
+            first_layer([first[j0]], 0, 0, j0, EIGHTH, (1,))
+        for j0 in first:
+            smooth_narrow(nc.gpsimd, narrow_unit(0, 0, j0, first[j0]), 0, hb0[:, 4 * j0 : 4 * (j0 + EIGHTH)])
+        for g in (1, 2):
+            sort_words(g, 1, "scalar")
+        act = wide_unit(1, 0, second)
         for lo in (0, EIGHTH):
             j0 = QUARTER + lo
             smooth(nc.gpsimd, act, 0, lo, lo + EIGHTH, hb0[:, 4 * j0 : 4 * (j0 + EIGHTH)])
         hb_first = tile([P, 4 * EIGHTH], BF16, "hb_first")
-        hb_second = tile([P, 4 * EIGHTH], BF16, "hb_second")
+        hb_middle = tile([P, 4 * QUARTER], BF16, "hb_middle")
+        hb_last = tile([P, 4 * EIGHTH], BF16, "hb_last")
         act = wide_unit(0, 1)
         smooth(nc.gpsimd, act, 1, 0, EIGHTH, hb_first[:])
-        smooth_scalar(act, 1, EIGHTH, QUARTER, hb_second[:], "hp0")
+        smooth_scalar(act, 1, EIGHTH, QUARTER, hb_middle[:, 0:512], "hp0")
+        wd = placed([P, 2 * 2 * N], U8, "wd", at_w[0, 1] + 256)
+        nc.sync.dma_start(wd[:].bitcast(I32).rearrange("p (a c) -> p a c", a=2), wd_words.bitcast(I32).rearrange("a p c -> p a c"))
+        wd_plane = placed([P, 2 * N], U8, "wd_plane", at_act)
+        nc.gpsimd.memset(wd_plane[:].bitcast(I32), 0)
+        for q in range(4):
+            nc.sync.dma_start(
+                wd_plane[32 * q : 32 * q + 4, :].bitcast(I32).rearrange("p (a c) -> p a c", a=2),
+                wd_scales[:, 4 * q : 4 * q + 4, :].bitcast(I32).rearrange("a r c -> r a c"),
+            )
+
         for g in range(3):
             gather_words(3, g)
 
@@ -261,11 +291,13 @@ def tile_list_rvq_gelu_none_kernel(tc, tab_words, tab_scales, w0_words, w0_scale
             smooth(nc.vector, wide_unit(q, b), b, 0, QUARTER, hb[:])
             return hb
 
-        hb = late_unit(1, 1)
+        act = wide_unit(1, 1)
+        smooth_scalar(act, 1, 0, EIGHTH, hb_middle[:, 512:1024], "hp1")
         quantise(hb0[:], 0, 0, 0, HALF)
+        smooth(nc.vector, act, 1, EIGHTH, QUARTER, hb_last[:])
         quantise(hb_first[:], 0, 1, 0, EIGHTH)
-        quantise(hb_second[:], 0, 1, EIGHTH, EIGHTH)
-        quantise(hb[:], 0, 1, QUARTER, QUARTER)
+        quantise(hb_middle[:], 0, 1, EIGHTH, QUARTER)
+        quantise(hb_last[:], 0, 1, 3 * EIGHTH, EIGHTH)
         for q, b in ((2, 0), (2, 1), (3, 0)):
             quantise(late_unit(q, b)[:], 1, b, QUARTER * (q - 2), QUARTER)
         narrow = []

@@ -91,7 +91,7 @@ def tile_list_rvq_gelu_none_kernel(tc, tab_words, tab_scales, w0_words, w0_scale
         for (lo, hi), behind in zip(TAB_PIECES, (rows[4:5], rows[5:9], rows[9:12])):
             nc.sync.dma_start(tab[:, lo:hi], words[:, lo:hi])
             load_w_scales(nc.sync, behind)
-        for g, b in ((1, 0), (2, 0), (0, 1), (1, 1), (2, 1)):
+        for g, b in ((1, 0), (2, 0), (2, 1), (0, 1), (1, 1)):
             load_w(g, b)
         sm_t = placed([P, 2, 4], F32, "sm_t", at_sm)
         nc.sync.dma_start(sm_t[:], sm.rearrange("(b p t) -> p b t", b=2, t=4))
@@ -147,7 +147,7 @@ def tile_list_rvq_gelu_none_kernel(tc, tab_words, tab_scales, w0_words, w0_scale
             gather_words(q, g)
         gather_words(1, 1)
         gather_words(1, 2)
-        for g, b in ((0, 0), (1, 0), (2, 0)):
+        for g, b in ((0, 0), (1, 0), (2, 0), (2, 1)):
             sort_words(g, b, "scalar")
         sort_scales(0, 2)
         sort_scales(1, 1)
@@ -239,9 +239,12 @@ def tile_list_rvq_gelu_none_kernel(tc, tab_words, tab_scales, w0_words, w0_scale
                     second_pass(y[:, nt * width : (nt + 1) * width], half, b, nt, j0, width, b == 0 and nt == 0, b == 1 and nt == 1)
             store(y, half, j0, width)
 
-        def store(y, half, j0, width):
+        def store(y, half, j0, width, on="scalar"):
             res = tile([P, 2, width], F32, "res%d%d" % (half, j0))
-            nc.scalar.copy(res[:], y[:].rearrange("p (nt j) -> p nt j", nt=2))
+            if on == "scalar":
+                nc.scalar.copy(res[:], y[:].rearrange("p (nt j) -> p nt j", nt=2))
+            else:
+                nc.vector.tensor_copy(res[:], y[:].rearrange("p (nt j) -> p nt j", nt=2))
             nc.sync.dma_start(out_v[:, :, HALF * half + j0 : HALF * half + j0 + width], res[:])
 
         idle = bank("idle")
@@ -261,8 +264,7 @@ def tile_list_rvq_gelu_none_kernel(tc, tab_words, tab_scales, w0_words, w0_scale
             first_layer([first[j0]], 0, 0, j0, EIGHTH, (1,))
         for j0 in first:
             smooth_narrow(nc.gpsimd, narrow_unit(0, 0, j0, first[j0]), 0, hb0[:, 4 * j0 : 4 * (j0 + EIGHTH)])
-        for g in (1, 2):
-            sort_words(g, 1, "scalar")
+        sort_words(1, 1, "scalar")
         act = wide_unit(1, 0, second)
         for lo in (0, EIGHTH):
             j0 = QUARTER + lo
@@ -298,8 +300,14 @@ def tile_list_rvq_gelu_none_kernel(tc, tab_words, tab_scales, w0_words, w0_scale
         quantise(hb_first[:], 0, 1, 0, EIGHTH)
         quantise(hb_middle[:], 0, 1, EIGHTH, QUARTER)
         quantise(hb_last[:], 0, 1, 3 * EIGHTH, EIGHTH)
-        for q, b in ((2, 0), (2, 1), (3, 0)):
-            quantise(late_unit(q, b)[:], 1, b, QUARTER * (q - 2), QUARTER)
+        for b in range(2):
+            quantise(late_unit(2, b)[:], 1, b, 0, QUARTER)
+        act = wide_unit(3, 0)
+        halves = [tile([P, 4 * EIGHTH], BF16, "hb30%d" % i) for i in range(2)]
+        smooth_scalar(act, 0, 0, EIGHTH, halves[0][:], "hp2")
+        smooth(nc.vector, act, 0, EIGHTH, QUARTER, halves[1][:])
+        for i in (1, 0):
+            quantise(halves[i][:], 1, 0, QUARTER + EIGHTH * i, EIGHTH)
         narrow = []
         for j0 in (0, EIGHTH):
             act = narrow_unit(3, 1, j0)
@@ -317,4 +325,4 @@ def tile_list_rvq_gelu_none_kernel(tc, tab_words, tab_scales, w0_words, w0_scale
                 for nt in range(2):
                     second_pass(ys[i][:, nt * EIGHTH : (nt + 1) * EIGHTH], 1, b, nt, j0, EIGHTH, b == 0 and nt == 0, b == 1 and nt == 1)
                 if b == 1:
-                    store(ys[i], 1, j0, EIGHTH)
+                    store(ys[i], 1, j0, EIGHTH, ("vector", "scalar")[i])

@@ -46,7 +46,7 @@ def tile_list_rvq_gelu_none_kernel(tc, tab_words, tab_scales, w0_words, w0_scale
         base0 = 4 * T
         at_w = {(0, 1): base0 + 4096, (1, 0): base0 + 6144, (1, 1): base0 + 8192, (2, 1): base0 + 10240, (0, 0): base0 + 12032, (2, 0): base0 + 13824}
         at_sm = base0 + 12288
-        at_ws = base0 + 20480
+        at_ws = base0 + 21504
         at_act = at_ws + 1024
 
         offsets = keep.tile([P, 3 * J // 16], U16, name="offsets")
@@ -55,16 +55,14 @@ def tile_list_rvq_gelu_none_kernel(tc, tab_words, tab_scales, w0_words, w0_scale
         tab_plane = tile([P, T], U8, "tab_plane")
         ws_raw = placed([P, R], U8, "ws_raw", at_ws)
         tab = placed([P, T], I32, "tab", at_tab)
-        zeros = tab[:].rearrange("p (a c) -> p a c", c=1024)[:, 0:4, 960:1024]
-        nc.gpsimd.memset(ws_raw[0:32, :].bitcast(I32), 0)
+        zeros = tab[:].rearrange("p (a c) -> p a c", c=1024)[:, :, 1016:1024]
+        nc.gpsimd.memset(zeros, 0)
         nc.vector.memset(tab_plane[:].bitcast(I32), 0)
-        nc.gpsimd.memset(zeros[32:64], 0)
-        nc.vector.memset(zeros[64:P], 0)
-        for lo, hi in ((32, 64), (64, P)):
-            nc.vector.tensor_copy(ws_raw[lo:hi, :].bitcast(I32).rearrange("p (a c) -> p a c", c=64), zeros[lo:hi])
-
+        nc.vector.tensor_copy(
+            ws_raw[:].bitcast(I32).rearrange("p (a r c) -> p a r c", a=4, c=8), zeros.unsqueeze(2).to_broadcast([P, 4, 8, 8])
+        )
         warm = tile([P, 2], F32, "warm")
-        nc.vector.memset(warm[:, 0:1], 0.0)
+        nc.gpsimd.memset(warm[:, 0:1], 0.0)
         nc.scalar.activation(warm[:, 1:2], warm[:, 0:1], GELU)
 
         w_raw = {}
@@ -87,8 +85,8 @@ def tile_list_rvq_gelu_none_kernel(tc, tab_words, tab_scales, w0_words, w0_scale
         nc.sync.dma_start(tab[:, 0:TAB_EARLY], words[:, 0:TAB_EARLY])
         for r in range(4):
             nc.sync.dma_start(tab_plane[r:P:32, :].bitcast(I32), tab_scales[0, r:16:4, :].bitcast(I32))
-        load_w_scales(nc.gpsimd, rows[0:4])
-        for (lo, hi), behind in zip(TAB_PIECES, (rows[4:5], rows[5:9], rows[9:12])):
+        load_w_scales(nc.gpsimd, rows[0:3])
+        for (lo, hi), behind in zip(TAB_PIECES, (rows[3:4], rows[4:8], rows[8:12])):
             nc.sync.dma_start(tab[:, lo:hi], words[:, lo:hi])
             load_w_scales(nc.sync, behind)
         for g, b in ((1, 0), (2, 0), (2, 1), (0, 1), (1, 1)):
@@ -100,14 +98,14 @@ def tile_list_rvq_gelu_none_kernel(tc, tab_words, tab_scales, w0_words, w0_scale
         gw = {}
 
         late_planes = placed([P, 3 * HALF], U8, "late_planes", at_w[2, 0] + 256)
-        late_words = placed([P, 4 * QUARTER], U32, "late_words", at_w[2, 0] + 1792)
+        late_words = placed([P, 5 * QUARTER], U32, "late_words", at_w[2, 0] + 1792)
 
         def gather_plane(half, g):
             gs[half, g] = late_planes[:, HALF * g : HALF * (g + 1)] if half else tile([P, HALF], U8, "gs%d" % g)[:]
             c0 = (J * g + HALF * half) // 16
             nc.vector.tensor_copy(gs[half, g], tab_plane[:].indirect(offsets[:, c0 : c0 + HALF // 16]))
 
-        late = ((1, 1), (2, 0), (2, 1), (2, 2))
+        late = ((1, 0), (1, 1), (2, 0), (2, 1), (2, 2))
 
         def gather_words(q, g):
             if (q, g) in late:
@@ -143,10 +141,9 @@ def tile_list_rvq_gelu_none_kernel(tc, tab_words, tab_scales, w0_words, w0_scale
 
         for g in range(3):
             gather_plane(0, g)
-        for q, g in ((0, 0), (1, 0), (0, 1), (0, 2)):
-            gather_words(q, g)
-        gather_words(1, 1)
-        gather_words(1, 2)
+        for q in range(2):
+            for g in range(3):
+                gather_words(q, g)
         for g, b in ((0, 0), (1, 0), (2, 0), (2, 1)):
             sort_words(g, b, "scalar")
         sort_scales(0, 2)
@@ -181,11 +178,11 @@ def tile_list_rvq_gelu_none_kernel(tc, tab_words, tab_scales, w0_words, w0_scale
                         stop=(g == 2 and e == per_bank - 1),
                     )
 
-        def wide_unit(q, b, opened=None):
+        def wide_unit(q, b):
             shape, name = [P, 2, QUARTER, 2], "act%d%d" % (q, b)
             act = placed(shape, F32, name, at_act) if (q, b) == (0, 1) else tile(shape, F32, name)
-            accs = opened or [bank("a%d%d%d" % (q, b, u)) for u in range(2)]
-            first_layer(accs, q, b, 0, QUARTER, (1, 2) if opened else (0, 1, 2))
+            accs = [bank("a%d%d%d" % (q, b, u)) for u in range(2)]
+            first_layer(accs, q, b, 0, QUARTER, (0, 1, 2))
             for u in range(2):
                 nc.scalar.activation(act[:, u, :, :], accs[u][:].rearrange("p (e j) -> p j e", e=2), GELU)
             return act
@@ -256,16 +253,13 @@ def tile_list_rvq_gelu_none_kernel(tc, tab_words, tab_scales, w0_words, w0_scale
         next_bank[0] = 0
         hb0 = tile([P, 4 * HALF], BF16, "hb0")
         first = {j0: bank("first%d" % j0) for j0 in (0, EIGHTH)}
-        second = [bank("second%d" % u) for u in range(2)]
-        for j0 in first:
-            first_layer([first[j0]], 0, 0, j0, EIGHTH, (0,))
-        first_layer(second, 1, 0, 0, QUARTER, (0,))
-        for j0 in first:
-            first_layer([first[j0]], 0, 0, j0, EIGHTH, (1,))
+        for g in range(2):
+            for j0 in first:
+                first_layer([first[j0]], 0, 0, j0, EIGHTH, (g,))
         for j0 in first:
             smooth_narrow(nc.gpsimd, narrow_unit(0, 0, j0, first[j0]), 0, hb0[:, 4 * j0 : 4 * (j0 + EIGHTH)])
         sort_words(1, 1, "scalar")
-        act = wide_unit(1, 0, second)
+        act = wide_unit(1, 0)
         for lo in (0, EIGHTH):
             j0 = QUARTER + lo
             smooth(nc.gpsimd, act, 0, lo, lo + EIGHTH, hb0[:, 4 * j0 : 4 * (j0 + EIGHTH)])

@@ -149,6 +149,7 @@ def tile_list_rvq_gelu_none_kernel(tc, tab_words, tab_scales, w0_words, w0_scale
         sort_scales(0, 2)
         sort_scales(1, 1)
         sort_words(0, 1, "gpsimd")
+        sort_words(1, 1, "gpsimd")
         for g in range(3):
             gather_plane(1, g)
             gather_words(2, g)
@@ -258,7 +259,6 @@ def tile_list_rvq_gelu_none_kernel(tc, tab_words, tab_scales, w0_words, w0_scale
                 first_layer([first[j0]], 0, 0, j0, EIGHTH, (g,))
         for j0 in first:
             smooth_narrow(nc.gpsimd, narrow_unit(0, 0, j0, first[j0]), 0, hb0[:, 4 * j0 : 4 * (j0 + EIGHTH)])
-        sort_words(1, 1, "scalar")
         act = wide_unit(1, 0)
         for lo in (0, EIGHTH):
             j0 = QUARTER + lo
@@ -271,7 +271,7 @@ def tile_list_rvq_gelu_none_kernel(tc, tab_words, tab_scales, w0_words, w0_scale
         smooth_scalar(act, 1, EIGHTH, QUARTER, hb_middle[:, 0:512], "hp0")
         wd = placed([P, 2 * 2 * N], U8, "wd", at_w[0, 1] + 256)
         nc.sync.dma_start(wd[:].bitcast(I32).rearrange("p (a c) -> p a c", a=2), wd_words.bitcast(I32).rearrange("a p c -> p a c"))
-        wd_plane = placed([P, 2 * N], U8, "wd_plane", at_act)
+        wd_plane = placed([P, 2 * N], U8, "wd_plane", at_ws)
         nc.gpsimd.memset(wd_plane[:].bitcast(I32), 0)
         for q in range(4):
             nc.sync.dma_start(

@@ -98,14 +98,14 @@ def tile_list_rvq_gelu_none_kernel(tc, tab_words, tab_scales, w0_words, w0_scale
         gw = {}
 
         late_planes = placed([P, 3 * HALF], U8, "late_planes", at_w[2, 0] + 256)
-        late_words = placed([P, 5 * QUARTER], U32, "late_words", at_w[2, 0] + 1792)
+        late_words = placed([P, 3 * QUARTER], U32, "late_words", at_w[2, 0] + 1792)
 
         def gather_plane(half, g):
             gs[half, g] = late_planes[:, HALF * g : HALF * (g + 1)] if half else tile([P, HALF], U8, "gs%d" % g)[:]
             c0 = (J * g + HALF * half) // 16
             nc.vector.tensor_copy(gs[half, g], tab_plane[:].indirect(offsets[:, c0 : c0 + HALF // 16]))
 
-        late = ((1, 0), (1, 1), (2, 0), (2, 1), (2, 2))
+        late = ((2, 0), (2, 1), (2, 2))
 
         def gather_words(q, g):
             if (q, g) in late:
@@ -141,9 +141,8 @@ def tile_list_rvq_gelu_none_kernel(tc, tab_words, tab_scales, w0_words, w0_scale
 
         for g in range(3):
             gather_plane(0, g)
-        for q in range(2):
-            for g in range(3):
-                gather_words(q, g)
+        for q, g in ((0, 0), (0, 1), (0, 2), (1, 2), (1, 1), (1, 0)):
+            gather_words(q, g)
         for g, b in ((0, 0), (1, 0), (2, 0), (2, 1)):
             sort_words(g, b, "scalar")
         sort_scales(0, 2)
@@ -163,7 +162,7 @@ def tile_list_rvq_gelu_none_kernel(tc, tab_words, tab_scales, w0_words, w0_scale
             next_bank[0] = next_bank[0] + 1
             return t_
 
-        def first_layer(accs, q, b, j0, width, order):
+        def first_layer(accs, q, b, j0, width, order, whole=(0, 1, 2)):
             per_bank = 4 // len(accs)
             s0 = QUARTER * (q % 2) + j0
             for g in order:
@@ -175,15 +174,15 @@ def tile_list_rvq_gelu_none_kernel(tc, tab_words, tab_scales, w0_words, w0_scale
                         lhsT_scale=ws[b, t][4 * (g + 1) : P, :],
                         rhs=gw[q, g][:, j0 : j0 + width].bitcast(FP8X4),
                         rhs_scale=gs[q // 2, g][:, s0 : s0 + width],
-                        start=(g == 0 and e == 0),
-                        stop=(g == 2 and e == per_bank - 1),
+                        start=(g == whole[0] and e == 0),
+                        stop=(g == whole[2] and e == per_bank - 1),
                     )
 
-        def wide_unit(q, b):
+        def wide_unit(q, b, order=(0, 1, 2)):
             shape, name = [P, 2, QUARTER, 2], "act%d%d" % (q, b)
             act = placed(shape, F32, name, at_act) if (q, b) == (0, 1) else tile(shape, F32, name)
             accs = [bank("a%d%d%d" % (q, b, u)) for u in range(2)]
-            first_layer(accs, q, b, 0, QUARTER, (0, 1, 2))
+            first_layer(accs, q, b, 0, QUARTER, order, order)
             for u in range(2):
                 nc.scalar.activation(act[:, u, :, :], accs[u][:].rearrange("p (e j) -> p j e", e=2), GELU)
             return act
@@ -259,7 +258,7 @@ def tile_list_rvq_gelu_none_kernel(tc, tab_words, tab_scales, w0_words, w0_scale
                 first_layer([first[j0]], 0, 0, j0, EIGHTH, (g,))
         for j0 in first:
             smooth_narrow(nc.gpsimd, narrow_unit(0, 0, j0, first[j0]), 0, hb0[:, 4 * j0 : 4 * (j0 + EIGHTH)])
-        act = wide_unit(1, 0)
+        act = wide_unit(1, 0, (2, 1, 0))
         for lo in (0, EIGHTH):
             j0 = QUARTER + lo
             smooth(nc.gpsimd, act, 0, lo, lo + EIGHTH, hb0[:, 4 * j0 : 4 * (j0 + EIGHTH)])

@@ -22,6 +22,7 @@ HALF = 512
 QUARTER = 256
 EIGHTH = 128
 WARM_PASSES = 5
+POOL_PLACES = 192
 TAB_EARLY = 512
 TAB_PIECES = ((TAB_EARLY, 1792), (1792, 2560), (2560, T))
 
@@ -48,6 +49,7 @@ def tile_list_rvq_gelu_none_kernel(tc, tab_words, tab_scales, w0_words, w0_scale
         at_sm = base0 + 12288
         at_ws = base0 + 21504
         at_act = at_ws + 1024
+        at_hb = at_act + 4096
 
         offsets = keep.tile([P, 3 * J // 16], U16, name="offsets")
         nc.sync.dma_start(offsets[:], offs)
@@ -153,14 +155,13 @@ def tile_list_rvq_gelu_none_kernel(tc, tab_words, tab_scales, w0_words, w0_scale
             gather_plane(1, g)
             gather_words(2, g)
 
-        codes = [[tile([P, HALF], U32, "codes%d%d" % (half, b)) for b in range(2)] for half in range(2)]
-        planes = [[tile([P, HALF], U8, "plane%d%d" % (half, b)) for b in range(2)] for half in range(2)]
         next_bank = [0]
 
-        def bank(name, width=512):
-            t_ = psum.tile([P, width], F32, name=name, tag="bank%d" % (next_bank[0] % 8))
-            next_bank[0] = next_bank[0] + 1
-            return t_
+        def bank(name, width=512, at=None):
+            if at is None:
+                at = next_bank[0] % 8
+                next_bank[0] = next_bank[0] + 1
+            return psum.tile([P, width], F32, name=name, tag="bank%d" % at)
 
         def first_layer(accs, q, b, j0, width, order, whole=(0, 1, 2)):
             per_bank = 4 // len(accs)
@@ -185,64 +186,61 @@ def tile_list_rvq_gelu_none_kernel(tc, tab_words, tab_scales, w0_words, w0_scale
             first_layer(accs, q, b, 0, QUARTER, order, order)
             for u in range(2):
                 nc.scalar.activation(act[:, u, :, :], accs[u][:].rearrange("p (e j) -> p j e", e=2), GELU)
-            return act
+            return act[:].rearrange("p u j e -> p j u e")
 
-        def narrow_unit(q, b, j0, opened=None):
-            act = tile([P, EIGHTH, 4], F32, "nact%d%d%d" % (q, b, j0))
-            acc = opened or bank("n%d%d%d" % (q, b, j0))
-            first_layer([acc], q, b, j0, EIGHTH, (2,) if opened else (0, 1, 2))
-            nc.scalar.activation(act[:], acc[:].rearrange("p (t j) -> p j t", t=4), GELU)
-            return act
+        def narrow_gelu(act, acc):
+            nc.scalar.activation(act, acc[:].rearrange("p (t j) -> p j t", t=4), GELU)
+
+        def pairs(act):
+            return act.rearrange("p j (u e) -> p j u e", u=2)
 
         def smooth(eng, act, b, lo, hi, hb):
             eng.tensor_tensor(
                 hb.rearrange("p (j u e) -> p j u e", u=2, e=2),
-                act[:, :, lo:hi, :].rearrange("p u j e -> p j u e"),
+                act[:, lo:hi, :, :],
                 sm_t[:, b, :].rearrange("p (u e) -> p u e", u=2).unsqueeze(1).to_broadcast([P, hi - lo, 2, 2]),
                 MULT,
             )
 
         def smooth_narrow(eng, act, b, hb):
-            eng.tensor_tensor(hb.rearrange("p (j t) -> p j t", t=4), act[:], sm_t[:, b, :].unsqueeze(1).to_broadcast([P, EIGHTH, 4]), MULT)
+            places = act.shape[1]
+            eng.tensor_tensor(hb.rearrange("p (j t) -> p j t", t=4), act, sm_t[:, b, :].unsqueeze(1).to_broadcast([P, places, 4]), MULT)
 
         def smooth_scalar(act, b, lo, hi, hb, name):
             hp = tile([P, 4, hi - lo], BF16, name)
             for t in range(4):
-                nc.scalar.activation(hp[:, t, :], act[:, t // 2, lo:hi, t % 2], COPY, scale=sm_t[:, b, t : t + 1])
+                nc.scalar.activation(hp[:, t, :], act[:, lo:hi, t // 2, t % 2], COPY, scale=sm_t[:, b, t : t + 1])
             nc.scalar.copy(hb.rearrange("p (c i t) -> p c t i", i=4, t=4), hp[:].rearrange("p t (c i) -> p c t i", i=4))
 
-        def quantise(hb, half, b, j0, width):
-            nc.vector.quantize_mx(
-                out=codes[half][b][:, j0 : j0 + width].bitcast(FP8X4), scales=planes[half][b][:, j0 : j0 + width], in_=hb
-            )
+        codes = {key: tile([P, HALF], U32, "codes%s" % key) for key in ("00", "01")}
+        planes = {key: tile([P, HALF], U8, "plane%s" % key) for key in ("00", "01")}
+        codes["1"] = tile([P, 2 * HALF], U32, "codes1")
+        planes["1"] = tile([P, 2 * HALF], U8, "plane1")
 
-        out_v = out.rearrange("(nt p) j -> p nt j", p=P)
+        def quantise(hb, key, c0):
+            width = hb.shape[1] // 4
+            nc.vector.quantize_mx(out=codes[key][:, c0 : c0 + width].bitcast(FP8X4), scales=planes[key][:, c0 : c0 + width], in_=hb)
 
-        def second_pass(y, half, b, nt, j0, width, start, stop):
+        def second_pass(y, key, c0, width, b, nt, start, stop):
             nc.tensor.matmul_mx(
                 out=y,
                 lhsT=wd[:, 512 * b + 256 * nt : 512 * b + 256 * (nt + 1)].bitcast(FP4X4),
                 lhsT_scale=wd_plane[:, 256 * b + 128 * nt : 256 * b + 128 * (nt + 1)],
-                rhs=codes[half][b][:, j0 : j0 + width].bitcast(FP8X4),
-                rhs_scale=planes[half][b][:, j0 : j0 + width],
+                rhs=codes[key][:, c0 : c0 + width].bitcast(FP8X4),
+                rhs_scale=planes[key][:, c0 : c0 + width],
                 start=start,
                 stop=stop,
             )
 
-        def second_layer(half, j0, width):
-            y = bank("y%d%d" % (half, j0), 2 * width)
-            for b in range(2):
-                for nt in range(2):
-                    second_pass(y[:, nt * width : (nt + 1) * width], half, b, nt, j0, width, b == 0 and nt == 0, b == 1 and nt == 1)
-            store(y, half, j0, width)
+        out_v = out.rearrange("(nt p) j -> p nt j", p=P)
 
-        def store(y, half, j0, width, on="scalar"):
-            res = tile([P, 2, width], F32, "res%d%d" % (half, j0))
+        def store(y, j0, width, on):
+            res = tile([P, 2, width], F32, "res%d" % j0)
             if on == "scalar":
                 nc.scalar.copy(res[:], y[:].rearrange("p (nt j) -> p nt j", nt=2))
             else:
                 nc.vector.tensor_copy(res[:], y[:].rearrange("p (nt j) -> p nt j", nt=2))
-            nc.sync.dma_start(out_v[:, :, HALF * half + j0 : HALF * half + j0 + width], res[:])
+            nc.sync.dma_start(out_v[:, :, j0 : j0 + width], res[:])
 
         idle = bank("idle")
         for i in range(WARM_PASSES):
@@ -251,23 +249,30 @@ def tile_list_rvq_gelu_none_kernel(tc, tab_words, tab_scales, w0_words, w0_scale
                 rhs=w[0, 0][:].bitcast(FP8X4), rhs_scale=gs[0, 0], start=True, stop=True,
             )
         next_bank[0] = 0
-        hb0 = tile([P, 4 * HALF], BF16, "hb0")
+
+        rest = QUARTER - POOL_PLACES
+        hb_pool = [placed([P, 2 * 4 * POOL_PLACES], BF16, "hb_pool%d" % b, at_hb + 4096 * b) for b in range(2)]
+        hb_act = [tile([P, 2 * 4 * rest], BF16, "hb_act%d" % b) for b in range(2)]
+
+        def share(act, q, b, narrow=None):
+            dst = hb_pool[b][:, 4 * POOL_PLACES * q : 4 * POOL_PLACES * (q + 1)]
+            if narrow is None:
+                smooth(nc.gpsimd, act, b, 0, POOL_PLACES, dst)
+            else:
+                smooth_narrow(nc.gpsimd, narrow[:, 0:POOL_PLACES, :], b, dst)
+            smooth_scalar(act, b, POOL_PLACES, QUARTER, hb_act[b][:, 4 * rest * q : 4 * rest * (q + 1)], "hp%d%d" % (q, b))
+
         first = {j0: bank("first%d" % j0) for j0 in (0, EIGHTH)}
+        act00 = tile([P, QUARTER, 4], F32, "act00")
         for g in range(2):
             for j0 in first:
                 first_layer([first[j0]], 0, 0, j0, EIGHTH, (g,))
         for j0 in first:
-            smooth_narrow(nc.gpsimd, narrow_unit(0, 0, j0, first[j0]), 0, hb0[:, 4 * j0 : 4 * (j0 + EIGHTH)])
-        act = wide_unit(1, 0, (2, 1, 0))
-        for lo in (0, EIGHTH):
-            j0 = QUARTER + lo
-            smooth(nc.gpsimd, act, 0, lo, lo + EIGHTH, hb0[:, 4 * j0 : 4 * (j0 + EIGHTH)])
-        hb_first = tile([P, 4 * EIGHTH], BF16, "hb_first")
-        hb_middle = tile([P, 4 * QUARTER], BF16, "hb_middle")
-        hb_last = tile([P, 4 * EIGHTH], BF16, "hb_last")
-        act = wide_unit(0, 1)
-        smooth(nc.gpsimd, act, 1, 0, EIGHTH, hb_first[:])
-        smooth_scalar(act, 1, EIGHTH, QUARTER, hb_middle[:, 0:512], "hp0")
+            first_layer([first[j0]], 0, 0, j0, EIGHTH, (2,))
+            narrow_gelu(act00[:, j0 : j0 + EIGHTH, :], first[j0])
+        share(pairs(act00[:]), 0, 0, act00)
+        share(wide_unit(1, 0, (2, 1, 0)), 1, 0)
+        share(wide_unit(0, 1), 0, 1)
         wd = placed([P, 2 * 2 * N], U8, "wd", at_w[0, 1] + 256)
         nc.sync.dma_start(wd[:].bitcast(I32).rearrange("p (a c) -> p a c", a=2), wd_words.bitcast(I32).rearrange("a p c -> p a c"))
         wd_plane = placed([P, 2 * N], U8, "wd_plane", at_ws)
@@ -277,45 +282,53 @@ def tile_list_rvq_gelu_none_kernel(tc, tab_words, tab_scales, w0_words, w0_scale
                 wd_plane[32 * q : 32 * q + 4, :].bitcast(I32).rearrange("p (a c) -> p a c", a=2),
                 wd_scales[:, 4 * q : 4 * q + 4, :].bitcast(I32).rearrange("a r c -> r a c"),
             )
-
         for g in range(3):
             gather_words(3, g)
-
-        def late_unit(q, b):
-            hb = tile([P, 4 * QUARTER], BF16, "hb%d%d" % (q, b))
-            smooth(nc.vector, wide_unit(q, b), b, 0, QUARTER, hb[:])
-            return hb
-
-        act = wide_unit(1, 1)
-        smooth_scalar(act, 1, 0, EIGHTH, hb_middle[:, 512:1024], "hp1")
-        quantise(hb0[:], 0, 0, 0, HALF)
-        smooth(nc.vector, act, 1, EIGHTH, QUARTER, hb_last[:])
-        quantise(hb_first[:], 0, 1, 0, EIGHTH)
-        quantise(hb_middle[:], 0, 1, EIGHTH, QUARTER)
-        quantise(hb_last[:], 0, 1, 3 * EIGHTH, EIGHTH)
+        share(wide_unit(1, 1), 1, 1)
         for b in range(2):
-            quantise(late_unit(2, b)[:], 1, b, 0, QUARTER)
-        act = wide_unit(3, 0)
-        halves = [tile([P, 4 * EIGHTH], BF16, "hb30%d" % i) for i in range(2)]
-        smooth_scalar(act, 0, 0, EIGHTH, halves[0][:], "hp2")
-        smooth(nc.vector, act, 0, EIGHTH, QUARTER, halves[1][:])
-        for i in (1, 0):
-            quantise(halves[i][:], 1, 0, QUARTER + EIGHTH * i, EIGHTH)
+            quantise(hb_pool[b][:], "0%d" % b, 0)
+            quantise(hb_act[b][:], "0%d" % b, 2 * POOL_PLACES)
+
+        acts = [wide_unit(q, b) for q, b in ((2, 0), (2, 1), (3, 0))]
+        for first_piece in (0, 3):
+            pair = placed([P, 8 * EIGHTH], BF16, "pair%d" % first_piece, at_hb + 4096)
+            single = placed([P, 4 * EIGHTH], BF16, "single%d" % first_piece, at_hb + 4096 + 2048)
+            for i, hb in enumerate((pair[:, 0:512], pair[:, 512:1024], single[:])):
+                unit, part = divmod(first_piece + i, 2)
+                smooth(nc.vector, acts[unit], unit % 2, EIGHTH * part, EIGHTH * (part + 1), hb)
+            quantise(pair[:], "1", EIGHTH * first_piece)
+            quantise(single[:], "1", EIGHTH * (first_piece + 2))
+
+        for nt in range(2):
+            y = bank("y0%d" % nt)
+            for b in range(2):
+                second_pass(y[:], "0%d" % b, 0, HALF, b, nt, b == 0, b == 1)
+            res = tile([P, 2, QUARTER], F32, "res0%d" % nt)
+            nc.scalar.copy(res[:, :, 0:POOL_PLACES], y[:, 0 : 2 * POOL_PLACES].rearrange("p (q j) -> p q j", q=2))
+            nc.scalar.copy(res[:, :, POOL_PLACES:QUARTER], y[:, 2 * POOL_PLACES : HALF].rearrange("p (q j) -> p q j", q=2))
+            nc.sync.dma_start(out_v[:, nt, 0:HALF], res[:].rearrange("p q j -> p (q j)"))
         narrow = []
         for j0 in (0, EIGHTH):
-            act = narrow_unit(3, 1, j0)
-            hb = tile([P, 4 * EIGHTH], BF16, "nhb%d" % j0)
-            smooth_narrow(nc.vector, act, 1, hb[:])
+            acc = bank("n%d" % j0, at=6 if j0 else 0)
+            first_layer([acc], 3, 1, j0, EIGHTH, (0, 1, 2))
+            act = tile([P, EIGHTH, 4], F32, "nact%d" % j0)
+            narrow_gelu(act[:], acc)
+            hb = placed([P, 4 * EIGHTH], BF16, "nhb%d" % j0, at_hb + 4096 + 8 * j0)
+            smooth_narrow(nc.vector, act[:], 1, hb[:])
             narrow.append(hb)
-        for half, j0 in ((0, 0), (0, QUARTER), (1, 0)):
-            second_layer(half, j0, QUARTER)
-        ys = [bank("ylast%d" % i, QUARTER) for i in range(2)]
+
+        y = bank("y2", at=1)
+        for b in range(2):
+            for nt in range(2):
+                second_pass(y[:, nt * QUARTER : (nt + 1) * QUARTER], "1", QUARTER * b, QUARTER, b, nt, b == 0 and nt == 0, b == 1 and nt == 1)
+        store(y, HALF, QUARTER, "scalar")
+        ys = [bank("ylast%d" % i, QUARTER, at=2 + i) for i in range(2)]
         for b in range(2):
             for i in range(2):
-                j0 = QUARTER + EIGHTH * i
+                c0 = HALF + QUARTER * b + EIGHTH * i
                 if b == 1:
-                    quantise(narrow[i][:], 1, 1, j0, EIGHTH)
+                    quantise(narrow[i][:], "1", c0)
                 for nt in range(2):
-                    second_pass(ys[i][:, nt * EIGHTH : (nt + 1) * EIGHTH], 1, b, nt, j0, EIGHTH, b == 0 and nt == 0, b == 1 and nt == 1)
+                    second_pass(ys[i][:, nt * EIGHTH : (nt + 1) * EIGHTH], "1", c0, EIGHTH, b, nt, b == 0 and nt == 0, b == 1 and nt == 1)
                 if b == 1:
-                    store(ys[i], 1, j0, EIGHTH, ("vector", "scalar")[i])
+                    store(ys[i], 3 * QUARTER + EIGHTH * i, EIGHTH, ("scalar", "vector")[i])

@@ -1,6 +1,7 @@
 from contextlib import ExitStack
 
 import concourse.mybir as mybir
+from concourse.masks import make_identity
 
 K, R, N, T, J = 512, 1024, 256, 4096, 1024
 FLOPS = 2 * 3 * K * R * J + 2 * R * N * J
@@ -22,9 +23,8 @@ HALF = 512
 QUARTER = 256
 EIGHTH = 128
 WARM_PASSES = 5
-POOL_PLACES = 192
 TAB_EARLY = 512
-TAB_PIECES = ((TAB_EARLY, 1792), (1792, 2560), (2560, T))
+TAB_PIECES = ((TAB_EARLY, 2304), (2304, T))
 
 
 def tile_list_rvq_gelu_none_kernel(tc, tab_words, tab_scales, w0_words, w0_scales, w1_words, w1_scales,
@@ -50,6 +50,7 @@ def tile_list_rvq_gelu_none_kernel(tc, tab_words, tab_scales, w0_words, w0_scale
         at_ws = base0 + 21504
         at_act = at_ws + 1024
         at_hb = at_act + 4096
+        at_last = at_hb + 8192
 
         offsets = keep.tile([P, 3 * J // 16], U16, name="offsets")
         nc.sync.dma_start(offsets[:], offs)
@@ -60,6 +61,11 @@ def tile_list_rvq_gelu_none_kernel(tc, tab_words, tab_scales, w0_words, w0_scale
         zeros = tab[:].rearrange("p (a c) -> p a c", c=1024)[:, :, 1016:1024]
         nc.gpsimd.memset(zeros, 0)
         nc.vector.memset(tab_plane[:].bitcast(I32), 0)
+        ident = tile([P, P], F32, "ident")
+        nc.vector.memset(ident[:], 0.0)
+        make_identity(nc, ident[:], nomemset=True)
+        sm_rows = tile([P, HALF], F32, "sm_rows")
+        nc.vector.memset(sm_rows[:], 0.0)
         nc.vector.tensor_copy(
             ws_raw[:].bitcast(I32).rearrange("p (a r c) -> p a r c", a=4, c=8), zeros.unsqueeze(2).to_broadcast([P, 4, 8, 8])
         )
@@ -87,14 +93,18 @@ def tile_list_rvq_gelu_none_kernel(tc, tab_words, tab_scales, w0_words, w0_scale
         nc.sync.dma_start(tab[:, 0:TAB_EARLY], words[:, 0:TAB_EARLY])
         for r in range(4):
             nc.sync.dma_start(tab_plane[r:P:32, :].bitcast(I32), tab_scales[0, r:16:4, :].bitcast(I32))
+        nc.sync.dma_start(sm_rows[0:2, :], sm.rearrange("(b m) -> b m", b=2))
         load_w_scales(nc.gpsimd, rows[0:3])
-        for (lo, hi), behind in zip(TAB_PIECES, (rows[3:4], rows[4:8], rows[8:12])):
+        load_w_scales(nc.sync, rows[3:4])
+        for (lo, hi), behind in zip(TAB_PIECES, (rows[4:9], rows[9:12])):
             nc.sync.dma_start(tab[:, lo:hi], words[:, lo:hi])
             load_w_scales(nc.sync, behind)
-        for g, b in ((1, 0), (2, 0), (2, 1), (0, 1), (1, 1)):
-            load_w(g, b)
+        load_w(1, 0)
+        load_w(2, 0)
         sm_t = placed([P, 2, 4], F32, "sm_t", at_sm)
         nc.sync.dma_start(sm_t[:], sm.rearrange("(b p t) -> p b t", b=2, t=4))
+        for g in range(3):
+            load_w(g, 1)
 
         gs = {}
         gw = {}
@@ -145,8 +155,8 @@ def tile_list_rvq_gelu_none_kernel(tc, tab_words, tab_scales, w0_words, w0_scale
             gather_plane(0, g)
         for q, g in ((0, 0), (0, 1), (0, 2), (1, 2), (1, 1), (1, 0)):
             gather_words(q, g)
-        for g, b in ((0, 0), (1, 0), (2, 0), (2, 1)):
-            sort_words(g, b, "scalar")
+        for g in range(3):
+            sort_words(g, 0, "scalar")
         sort_scales(0, 2)
         sort_scales(1, 1)
         sort_words(0, 1, "gpsimd")
@@ -159,7 +169,7 @@ def tile_list_rvq_gelu_none_kernel(tc, tab_words, tab_scales, w0_words, w0_scale
 
         def bank(name, width=512, at=None):
             if at is None:
-                at = next_bank[0] % 8
+                at = next_bank[0] % 7
                 next_bank[0] = next_bank[0] + 1
             return psum.tile([P, width], F32, name=name, tag="bank%d" % at)
 
@@ -179,13 +189,15 @@ def tile_list_rvq_gelu_none_kernel(tc, tab_words, tab_scales, w0_words, w0_scale
                         stop=(g == whole[2] and e == per_bank - 1),
                     )
 
-        def wide_unit(q, b, order=(0, 1, 2)):
+        def wide_unit(q, b, order=(0, 1, 2), cuts=1):
             shape, name = [P, 2, QUARTER, 2], "act%d%d" % (q, b)
             act = placed(shape, F32, name, at_act) if (q, b) == (0, 1) else tile(shape, F32, name)
             accs = [bank("a%d%d%d" % (q, b, u)) for u in range(2)]
             first_layer(accs, q, b, 0, QUARTER, order, order)
-            for u in range(2):
-                nc.scalar.activation(act[:, u, :, :], accs[u][:].rearrange("p (e j) -> p j e", e=2), GELU)
+            step = QUARTER // cuts
+            for lo in range(0, QUARTER, step):
+                for u in range(2):
+                    nc.scalar.activation(act[:, u, lo : lo + step, :], accs[u][:].rearrange("p (e j) -> p j e", e=2)[:, lo : lo + step, :], GELU)
             return act[:].rearrange("p u j e -> p j u e")
 
         def narrow_gelu(act, acc):
@@ -194,17 +206,23 @@ def tile_list_rvq_gelu_none_kernel(tc, tab_words, tab_scales, w0_words, w0_scale
         def pairs(act):
             return act.rearrange("p j (u e) -> p j u e", u=2)
 
-        def smooth(eng, act, b, lo, hi, hb):
-            eng.tensor_tensor(
+        sm_bank = bank("sm_bank", at=7)
+        for t in range(4):
+            nc.tensor.transpose(sm_bank[:, P * t : P * (t + 1)], sm_rows[:, t:HALF:4], ident[:])
+        factors = {"gpsimd": sm_t[:], "vector": sm_bank[:].rearrange("p (t c) -> p c t", t=4)}
+        engines = {"gpsimd": nc.gpsimd, "vector": nc.vector}
+
+        def smooth(on, act, b, lo, hi, hb):
+            engines[on].tensor_tensor(
                 hb.rearrange("p (j u e) -> p j u e", u=2, e=2),
                 act[:, lo:hi, :, :],
-                sm_t[:, b, :].rearrange("p (u e) -> p u e", u=2).unsqueeze(1).to_broadcast([P, hi - lo, 2, 2]),
+                factors[on][:, b, :].rearrange("p (u e) -> p u e", u=2).unsqueeze(1).to_broadcast([P, hi - lo, 2, 2]),
                 MULT,
             )
 
-        def smooth_narrow(eng, act, b, hb):
+        def smooth_narrow(on, act, b, hb):
             places = act.shape[1]
-            eng.tensor_tensor(hb.rearrange("p (j t) -> p j t", t=4), act, sm_t[:, b, :].unsqueeze(1).to_broadcast([P, places, 4]), MULT)
+            engines[on].tensor_tensor(hb.rearrange("p (j t) -> p j t", t=4), act, factors[on][:, b, :].unsqueeze(1).to_broadcast([P, places, 4]), MULT)
 
         def smooth_scalar(act, b, lo, hi, hb, name):
             hp = tile([P, 4, hi - lo], BF16, name)
@@ -213,9 +231,11 @@ def tile_list_rvq_gelu_none_kernel(tc, tab_words, tab_scales, w0_words, w0_scale
             nc.scalar.copy(hb.rearrange("p (c i t) -> p c t i", i=4, t=4), hp[:].rearrange("p t (c i) -> p c t i", i=4))
 
         codes = {key: tile([P, HALF], U32, "codes%s" % key) for key in ("00", "01")}
-        planes = {key: tile([P, HALF], U8, "plane%s" % key) for key in ("00", "01")}
-        codes["1"] = tile([P, 2 * HALF], U32, "codes1")
-        planes["1"] = tile([P, 2 * HALF], U8, "plane1")
+        planes = {"0%d" % b: placed([P, HALF], U8, "plane0%d" % b, at_act + HALF * b) for b in range(2)}
+        codes["2"] = tile([P, HALF], U32, "codes2")
+        codes["3"] = placed([P, HALF], U32, "codes3", at_last)
+        for key in ("2", "3"):
+            planes[key] = tile([P, HALF], U8, "plane%s" % key)
 
         def quantise(hb, key, c0):
             width = hb.shape[1] // 4
@@ -250,29 +270,27 @@ def tile_list_rvq_gelu_none_kernel(tc, tab_words, tab_scales, w0_words, w0_scale
             )
         next_bank[0] = 0
 
-        rest = QUARTER - POOL_PLACES
-        hb_pool = [placed([P, 2 * 4 * POOL_PLACES], BF16, "hb_pool%d" % b, at_hb + 4096 * b) for b in range(2)]
-        hb_act = [tile([P, 2 * 4 * rest], BF16, "hb_act%d" % b) for b in range(2)]
+        hb_first = [placed([P, 4 * HALF], BF16, "hb_first%d" % b, at_hb + 4096 * b) for b in range(2)]
 
-        def share(act, q, b, narrow=None):
-            dst = hb_pool[b][:, 4 * POOL_PLACES * q : 4 * POOL_PLACES * (q + 1)]
-            if narrow is None:
-                smooth(nc.gpsimd, act, b, 0, POOL_PLACES, dst)
-            else:
-                smooth_narrow(nc.gpsimd, narrow[:, 0:POOL_PLACES, :], b, dst)
-            smooth_scalar(act, b, POOL_PLACES, QUARTER, hb_act[b][:, 4 * rest * q : 4 * rest * (q + 1)], "hp%d%d" % (q, b))
+        def part(hb, i, count=1):
+            return hb[:, 4 * EIGHTH * i : 4 * EIGHTH * (i + count)]
 
         first = {j0: bank("first%d" % j0) for j0 in (0, EIGHTH)}
-        act00 = tile([P, QUARTER, 4], F32, "act00")
         for g in range(2):
             for j0 in first:
                 first_layer([first[j0]], 0, 0, j0, EIGHTH, (g,))
         for j0 in first:
             first_layer([first[j0]], 0, 0, j0, EIGHTH, (2,))
-            narrow_gelu(act00[:, j0 : j0 + EIGHTH, :], first[j0])
-        share(pairs(act00[:]), 0, 0, act00)
-        share(wide_unit(1, 0, (2, 1, 0)), 1, 0)
-        share(wide_unit(0, 1), 0, 1)
+            act = tile([P, EIGHTH, 4], F32, "first_act%d" % j0)
+            narrow_gelu(act[:], first[j0])
+            smooth_narrow("gpsimd", act[:], 0, part(hb_first[0], j0 // EIGHTH))
+        sort_words(2, 1, "scalar")
+        act = wide_unit(1, 0, (2, 1, 0))
+        smooth("gpsimd", act, 0, 0, EIGHTH, part(hb_first[0], 2))
+        smooth_scalar(act, 0, EIGHTH, QUARTER, part(hb_first[0], 3), "hp10")
+        act = wide_unit(0, 1, cuts=2)
+        for lo in (0, EIGHTH):
+            smooth("gpsimd", act, 1, lo, lo + EIGHTH, part(hb_first[1], lo // EIGHTH))
         wd = placed([P, 2 * 2 * N], U8, "wd", at_w[0, 1] + 256)
         nc.sync.dma_start(wd[:].bitcast(I32).rearrange("p (a c) -> p a c", a=2), wd_words.bitcast(I32).rearrange("a p c -> p a c"))
         wd_plane = placed([P, 2 * N], U8, "wd_plane", at_ws)
@@ -284,51 +302,50 @@ def tile_list_rvq_gelu_none_kernel(tc, tab_words, tab_scales, w0_words, w0_scale
             )
         for g in range(3):
             gather_words(3, g)
-        share(wide_unit(1, 1), 1, 1)
+        act11 = wide_unit(1, 1)
+        smooth_scalar(act11, 1, 0, EIGHTH, part(hb_first[1], 2), "hp11")
+        smooth("vector", act11, 1, EIGHTH, QUARTER, part(hb_first[1], 3))
         for b in range(2):
-            quantise(hb_pool[b][:], "0%d" % b, 0)
-            quantise(hb_act[b][:], "0%d" % b, 2 * POOL_PLACES)
+            quantise(hb_first[b][:], "0%d" % b, 0)
 
         acts = [wide_unit(q, b) for q, b in ((2, 0), (2, 1), (3, 0))]
-        for first_piece in (0, 3):
-            pair = placed([P, 8 * EIGHTH], BF16, "pair%d" % first_piece, at_hb + 4096)
-            single = placed([P, 4 * EIGHTH], BF16, "single%d" % first_piece, at_hb + 4096 + 2048)
-            for i, hb in enumerate((pair[:, 0:512], pair[:, 512:1024], single[:])):
-                unit, part = divmod(first_piece + i, 2)
-                smooth(nc.vector, acts[unit], unit % 2, EIGHTH * part, EIGHTH * (part + 1), hb)
-            quantise(pair[:], "1", EIGHTH * first_piece)
-            quantise(single[:], "1", EIGHTH * (first_piece + 2))
-
-        for nt in range(2):
-            y = bank("y0%d" % nt)
-            for b in range(2):
-                second_pass(y[:], "0%d" % b, 0, HALF, b, nt, b == 0, b == 1)
-            res = tile([P, 2, QUARTER], F32, "res0%d" % nt)
-            nc.scalar.copy(res[:, :, 0:POOL_PLACES], y[:, 0 : 2 * POOL_PLACES].rearrange("p (q j) -> p q j", q=2))
-            nc.scalar.copy(res[:, :, POOL_PLACES:QUARTER], y[:, 2 * POOL_PLACES : HALF].rearrange("p (q j) -> p q j", q=2))
-            nc.sync.dma_start(out_v[:, nt, 0:HALF], res[:].rearrange("p q j -> p (q j)"))
-        narrow = []
         for j0 in (0, EIGHTH):
-            acc = bank("n%d" % j0, at=6 if j0 else 0)
+            acc = bank("n%d" % j0)
             first_layer([acc], 3, 1, j0, EIGHTH, (0, 1, 2))
-            act = tile([P, EIGHTH, 4], F32, "nact%d" % j0)
+            act = placed([P, EIGHTH, 4], F32, "nact%d" % j0, at_last) if j0 else tile([P, EIGHTH, 4], F32, "nact0")
             narrow_gelu(act[:], acc)
-            hb = placed([P, 4 * EIGHTH], BF16, "nhb%d" % j0, at_hb + 4096 + 8 * j0)
-            smooth_narrow(nc.vector, act[:], 1, hb[:])
-            narrow.append(hb)
+            acts.append(act[:])
+        ab = placed([P, 8 * EIGHTH], BF16, "ab", at_hb + 4096)
+        cd = placed([P, 8 * EIGHTH], BF16, "cd", at_hb)
+        smooth("gpsimd", acts[0], 0, 0, EIGHTH, part(ab, 0))
+        smooth("vector", acts[1], 1, 0, QUARTER, cd[:])
+        smooth("vector", acts[0], 0, EIGHTH, QUARTER, part(ab, 1))
+        quantise(cd[:], "2", QUARTER)
+        quantise(ab[:], "2", 0)
+        ef = placed([P, 8 * EIGHTH], BF16, "ef", at_hb + 4096)
+        gh = placed([P, 8 * EIGHTH], BF16, "gh", at_hb)
+        smooth("gpsimd", acts[2], 0, 0, EIGHTH, part(ef, 0))
+        smooth_narrow("vector", acts[3], 1, part(gh, 0))
+        smooth("vector", acts[2], 0, EIGHTH, QUARTER, part(ef, 1))
+        smooth_narrow("vector", acts[4], 1, part(gh, 1))
+        quantise(ef[:], "3", 0)
+        quantise(gh[:], "3", QUARTER)
 
-        y = bank("y2", at=1)
+        for q in range(3):
+            y = bank("y%d" % q, at=q)
+            for b in range(2):
+                key, c0 = ("0%d" % b, QUARTER * q) if q < 2 else ("2", QUARTER * b)
+                for nt in range(2):
+                    second_pass(y[:, nt * QUARTER : (nt + 1) * QUARTER], key, c0, QUARTER, b, nt, b == 0 and nt == 0, b == 1 and nt == 1)
+            store(y, QUARTER * q, QUARTER, "scalar")
+        ys = [bank("ylast%d" % nt, QUARTER, at=3 + nt) for nt in range(2)]
         for b in range(2):
             for nt in range(2):
-                second_pass(y[:, nt * QUARTER : (nt + 1) * QUARTER], "1", QUARTER * b, QUARTER, b, nt, b == 0 and nt == 0, b == 1 and nt == 1)
-        store(y, HALF, QUARTER, "scalar")
-        ys = [bank("ylast%d" % i, QUARTER, at=2 + i) for i in range(2)]
-        for b in range(2):
-            for i in range(2):
-                c0 = HALF + QUARTER * b + EIGHTH * i
-                if b == 1:
-                    quantise(narrow[i][:], "1", c0)
-                for nt in range(2):
-                    second_pass(ys[i][:, nt * EIGHTH : (nt + 1) * EIGHTH], "1", c0, EIGHTH, b, nt, b == 0 and nt == 0, b == 1 and nt == 1)
-                if b == 1:
-                    store(ys[i], 3 * QUARTER + EIGHTH * i, EIGHTH, ("scalar", "vector")[i])
+                second_pass(ys[nt][:], "3", QUARTER * b, QUARTER, b, nt, b == 0, b == 1)
+        for nt in range(2):
+            res = tile([P, QUARTER], F32, "res_last%d" % nt)
+            if nt == 0:
+                nc.scalar.copy(res[:], ys[nt][:])
+            else:
+                nc.vector.tensor_copy(res[:], ys[nt][:])
+            nc.sync.dma_start(out_v[:, nt, 3 * QUARTER : J], res[:])

@@ -1,7 +1,6 @@
 from contextlib import ExitStack
 
 import concourse.mybir as mybir
-from concourse.masks import make_identity
 
 K, R, N, T, J = 512, 1024, 256, 4096, 1024
 FLOPS = 2 * 3 * K * R * J + 2 * R * N * J
@@ -59,13 +58,14 @@ def tile_list_rvq_gelu_none_kernel(tc, tab_words, tab_scales, w0_words, w0_scale
         ws_raw = placed([P, R], U8, "ws_raw", at_ws)
         tab = placed([P, T], I32, "tab", at_tab)
         zeros = tab[:].rearrange("p (a c) -> p a c", c=1024)[:, :, 1016:1024]
+        sm_rows = tile([P, HALF], F32, "sm_rows")
+        nc.gpsimd.memset(sm_rows[:], 0.0)
         nc.gpsimd.memset(zeros, 0)
         nc.vector.memset(tab_plane[:].bitcast(I32), 0)
         ident = tile([P, P], F32, "ident")
         nc.vector.memset(ident[:], 0.0)
-        make_identity(nc, ident[:], nomemset=True)
-        sm_rows = tile([P, HALF], F32, "sm_rows")
-        nc.vector.memset(sm_rows[:], 0.0)
+        for b in range(2):
+            nc.vector.memset(ident[32 * b : 32 * b + 1, b : b + 1], 1.0)
         nc.vector.tensor_copy(
             ws_raw[:].bitcast(I32).rearrange("p (a r c) -> p a r c", a=4, c=8), zeros.unsqueeze(2).to_broadcast([P, 4, 8, 8])
         )
@@ -91,9 +91,9 @@ def tile_list_rvq_gelu_none_kernel(tc, tab_words, tab_scales, w0_words, w0_scale
         load_w(0, 0)
         words = tab_words[0].rearrange("p t i -> p (t i)").bitcast(I32)
         nc.sync.dma_start(tab[:, 0:TAB_EARLY], words[:, 0:TAB_EARLY])
+        nc.sync.dma_start(sm_rows[0:64:32, :], sm.rearrange("(b m) -> b m", b=2))
         for r in range(4):
             nc.sync.dma_start(tab_plane[r:P:32, :].bitcast(I32), tab_scales[0, r:16:4, :].bitcast(I32))
-        nc.sync.dma_start(sm_rows[0:2, :], sm.rearrange("(b m) -> b m", b=2))
         load_w_scales(nc.gpsimd, rows[0:3])
         load_w_scales(nc.sync, rows[3:4])
         for (lo, hi), behind in zip(TAB_PIECES, (rows[4:9], rows[9:12])):
@@ -312,27 +312,26 @@ def tile_list_rvq_gelu_none_kernel(tc, tab_words, tab_scales, w0_words, w0_scale
         for j0 in (0, EIGHTH):
             acc = bank("n%d" % j0)
             first_layer([acc], 3, 1, j0, EIGHTH, (0, 1, 2))
-            act = placed([P, EIGHTH, 4], F32, "nact%d" % j0, at_last) if j0 else tile([P, EIGHTH, 4], F32, "nact0")
+            act = tile([P, EIGHTH, 4], F32, "nact%d" % j0) if j0 else placed([P, EIGHTH, 4], F32, "nact0", at_last)
             narrow_gelu(act[:], acc)
             acts.append(act[:])
-        ab = placed([P, 8 * EIGHTH], BF16, "ab", at_hb + 4096)
-        cd = placed([P, 8 * EIGHTH], BF16, "cd", at_hb)
-        smooth("gpsimd", acts[0], 0, 0, EIGHTH, part(ab, 0))
-        smooth("vector", acts[1], 1, 0, QUARTER, cd[:])
-        smooth("vector", acts[0], 0, EIGHTH, QUARTER, part(ab, 1))
-        quantise(cd[:], "2", QUARTER)
+        ab = placed([P, 8 * EIGHTH], BF16, "ab", at_hb)
+        cd = placed([P, 8 * EIGHTH], BF16, "cd", at_hb + 4096)
+        smooth("vector", acts[0], 0, 0, QUARTER, ab[:])
+        smooth("gpsimd", acts[1], 1, 0, EIGHTH, part(cd, 0))
+        smooth("vector", acts[1], 1, EIGHTH, QUARTER, part(cd, 1))
         quantise(ab[:], "2", 0)
-        ef = placed([P, 8 * EIGHTH], BF16, "ef", at_hb + 4096)
-        gh = placed([P, 8 * EIGHTH], BF16, "gh", at_hb)
-        smooth("gpsimd", acts[2], 0, 0, EIGHTH, part(ef, 0))
-        smooth_narrow("vector", acts[3], 1, part(gh, 0))
-        smooth("vector", acts[2], 0, EIGHTH, QUARTER, part(ef, 1))
+        quantise(cd[:], "2", QUARTER)
+        ef = placed([P, 8 * EIGHTH], BF16, "ef", at_hb)
+        gh = placed([P, 8 * EIGHTH], BF16, "gh", at_hb + 4096)
+        smooth("vector", acts[2], 0, 0, QUARTER, ef[:])
+        smooth_narrow("gpsimd", acts[3], 1, part(gh, 0))
         smooth_narrow("vector", acts[4], 1, part(gh, 1))
         quantise(ef[:], "3", 0)
         quantise(gh[:], "3", QUARTER)
 
         for q in range(3):
-            y = bank("y%d" % q, at=q)
+            y = bank("y%d" % q, at=(2, 0, 1)[q])
             for b in range(2):
                 key, c0 = ("0%d" % b, QUARTER * q) if q < 2 else ("2", QUARTER * b)
                 for nt in range(2):

@@ -22,7 +22,7 @@ HALF = 512
 QUARTER = 256
 EIGHTH = 128
 WARM_PASSES = 5
-TAB_EARLY = 512
+TAB_EARLY = 256
 TAB_PIECES = ((TAB_EARLY, 2304), (2304, T))
 
 
@@ -58,20 +58,23 @@ def tile_list_rvq_gelu_none_kernel(tc, tab_words, tab_scales, w0_words, w0_scale
         ws_raw = placed([P, R], U8, "ws_raw", at_ws)
         tab = placed([P, T], I32, "tab", at_tab)
         zeros = tab[:].rearrange("p (a c) -> p a c", c=1024)[:, :, 1016:1024]
-        sm_rows = tile([P, HALF], F32, "sm_rows")
-        nc.gpsimd.memset(sm_rows[:], 0.0)
+        nc.gpsimd.memset(tab_plane[:, 0 : T // 2].bitcast(I32), 0)
         nc.gpsimd.memset(zeros, 0)
-        nc.vector.memset(tab_plane[:].bitcast(I32), 0)
+        nc.vector.memset(tab_plane[:, T // 2 : T].bitcast(I32), 0)
         ident = tile([P, P], F32, "ident")
         nc.vector.memset(ident[:], 0.0)
         for b in range(2):
-            nc.vector.memset(ident[32 * b : 32 * b + 1, b : b + 1], 1.0)
+            nc.vector.memset(ident[0 : 31 + b, b : b + 1], 1.0)
+            nc.vector.memset(ident[0 : 30 + b, b : b + 1], 0.0)
         nc.vector.tensor_copy(
             ws_raw[:].bitcast(I32).rearrange("p (a r c) -> p a r c", a=4, c=8), zeros.unsqueeze(2).to_broadcast([P, 4, 8, 8])
         )
         warm = tile([P, 2], F32, "warm")
         nc.gpsimd.memset(warm[:, 0:1], 0.0)
         nc.scalar.activation(warm[:, 1:2], warm[:, 0:1], GELU)
+        sm_rows = tile([P, HALF], F32, "sm_rows")
+        for lo, hi in ((0, 30), (32, 64), (64, P)):
+            nc.scalar.activation(sm_rows[lo:hi, :], warm[lo:hi, 0:1].to_broadcast([hi - lo, HALF]), COPY)
 
         w_raw = {}
         for name, halves in (("w_first", ((0, 0),)), ("w_low", ((0, 1), (1, 0), (1, 1), (2, 1))), ("w_high", ((2, 0),))):
@@ -91,7 +94,7 @@ def tile_list_rvq_gelu_none_kernel(tc, tab_words, tab_scales, w0_words, w0_scale
         load_w(0, 0)
         words = tab_words[0].rearrange("p t i -> p (t i)").bitcast(I32)
         nc.sync.dma_start(tab[:, 0:TAB_EARLY], words[:, 0:TAB_EARLY])
-        nc.sync.dma_start(sm_rows[0:64:32, :], sm.rearrange("(b m) -> b m", b=2))
+        nc.sync.dma_start(sm_rows[30:32, :], sm.rearrange("(b m) -> b m", b=2))
         for r in range(4):
             nc.sync.dma_start(tab_plane[r:P:32, :].bitcast(I32), tab_scales[0, r:16:4, :].bitcast(I32))
         load_w_scales(nc.gpsimd, rows[0:3])

@@ -21,7 +21,7 @@ P = 128
 HALF = 512
 QUARTER = 256
 EIGHTH = 128
-WARM_PASSES = 5
+WARM_PASSES = (0, 0, 1, 1, 2)
 TAB_EARLY = 256
 TAB_PIECES = ((TAB_EARLY, 2304), (2304, T))
 
@@ -47,7 +47,7 @@ def tile_list_rvq_gelu_none_kernel(tc, tab_words, tab_scales, w0_words, w0_scale
         at_w = {(0, 1): base0 + 4096, (1, 0): base0 + 6144, (1, 1): base0 + 8192, (2, 1): base0 + 10240, (0, 0): base0 + 12032, (2, 0): base0 + 13824}
         at_sm = base0 + 12288
         at_ws = base0 + 21504
-        at_act = at_ws + 1024
+        at_act = at_ws + 2048
         at_hb = at_act + 4096
         at_last = at_hb + 8192
 
@@ -55,7 +55,8 @@ def tile_list_rvq_gelu_none_kernel(tc, tab_words, tab_scales, w0_words, w0_scale
         nc.sync.dma_start(offsets[:], offs)
 
         tab_plane = tile([P, T], U8, "tab_plane")
-        ws_raw = placed([P, R], U8, "ws_raw", at_ws)
+        ws_both = placed([P, 2 * R], U8, "ws_both", at_ws)
+        ws_raw = [ws_both[:, 0:R], ws_both[:, R : 2 * R]]
         tab = placed([P, T], I32, "tab", at_tab)
         zeros = tab[:].rearrange("p (a c) -> p a c", c=1024)[:, :, 1016:1024]
         nc.gpsimd.memset(tab_plane[:, 0 : T // 2].bitcast(I32), 0)
@@ -66,9 +67,7 @@ def tile_list_rvq_gelu_none_kernel(tc, tab_words, tab_scales, w0_words, w0_scale
         for b in range(2):
             nc.vector.memset(ident[0 : 31 + b, b : b + 1], 1.0)
             nc.vector.memset(ident[0 : 30 + b, b : b + 1], 0.0)
-        nc.vector.tensor_copy(
-            ws_raw[:].bitcast(I32).rearrange("p (a r c) -> p a r c", a=4, c=8), zeros.unsqueeze(2).to_broadcast([P, 4, 8, 8])
-        )
+        nc.vector.tensor_copy(ws_both[:].bitcast(I32).rearrange("p (a r c) -> p a r c", a=4, c=8), zeros.unsqueeze(2).to_broadcast([P, 4, 16, 8]))
         warm = tile([P, 2], F32, "warm")
         nc.gpsimd.memset(warm[:, 0:1], 0.0)
         nc.scalar.activation(warm[:, 1:2], warm[:, 0:1], GELU)
@@ -88,18 +87,18 @@ def tile_list_rvq_gelu_none_kernel(tc, tab_words, tab_scales, w0_words, w0_scale
         def load_w_scales(eng, rows):
             for g, q in rows:
                 row = 32 * q + 4 * (g + 1)
-                eng.dma_start(ws_raw[row : row + 4, :].bitcast(I32), w_scales[g][0, 4 * q : 4 * q + 4, :].bitcast(I32))
+                eng.dma_start(ws_raw[g // 2][row : row + 4, :].bitcast(I32), w_scales[g][0, 4 * q : 4 * q + 4, :].bitcast(I32))
 
-        rows = [(g, q) for q in range(4) for g in range(3)]
+        rows = [(g, q) for q in range(4) for g in range(2)] + [(2, q) for q in range(4)]
         load_w(0, 0)
         words = tab_words[0].rearrange("p t i -> p (t i)").bitcast(I32)
         nc.sync.dma_start(tab[:, 0:TAB_EARLY], words[:, 0:TAB_EARLY])
         nc.sync.dma_start(sm_rows[30:32, :], sm.rearrange("(b m) -> b m", b=2))
         for r in range(4):
             nc.sync.dma_start(tab_plane[r:P:32, :].bitcast(I32), tab_scales[0, r:16:4, :].bitcast(I32))
-        load_w_scales(nc.gpsimd, rows[0:3])
-        load_w_scales(nc.sync, rows[3:4])
-        for (lo, hi), behind in zip(TAB_PIECES, (rows[4:9], rows[9:12])):
+        load_w_scales(nc.gpsimd, rows[0:1] + rows[8:10])
+        load_w_scales(nc.sync, rows[1:2])
+        for (lo, hi), behind in zip(TAB_PIECES, (rows[2:8], rows[10:12])):
             nc.sync.dma_start(tab[:, lo:hi], words[:, lo:hi])
             load_w_scales(nc.sync, behind)
         load_w(1, 0)
@@ -143,16 +142,9 @@ def tile_list_rvq_gelu_none_kernel(tc, tab_words, tab_scales, w0_words, w0_scale
 
         ws = {}
 
-        def sort_scales(b, pieces):
-            n = 4 // pieces
-            for i in range(pieces):
-                part = tile([P, 128 * n], U8, "ws%d%d" % (b, i))
-                nc.gpsimd.tensor_copy(
-                    part[:].rearrange("p (t m) -> p t m", t=n),
-                    ws_raw[:, HALF * b : HALF * (b + 1)].rearrange("p (m t) -> p t m", t=4)[:, n * i : n * (i + 1), :],
-                )
-                for e in range(n):
-                    ws[b, n * i + e] = part[:, 128 * e : 128 * (e + 1)]
+        def sort_scales(i, b):
+            ws[i, b] = tile([P, HALF], U8, "ws%d%d" % (i, b))
+            nc.gpsimd.tensor_copy(ws[i, b][:].rearrange("p (t m) -> p t m", t=4), ws_raw[i][:, HALF * b : HALF * (b + 1)].rearrange("p (m t) -> p t m", t=4))
 
         for g in range(3):
             gather_plane(0, g)
@@ -160,8 +152,9 @@ def tile_list_rvq_gelu_none_kernel(tc, tab_words, tab_scales, w0_words, w0_scale
             gather_words(q, g)
         for g in range(3):
             sort_words(g, 0, "scalar")
-        sort_scales(0, 2)
-        sort_scales(1, 1)
+        for i in range(2):
+            for b in range(2):
+                sort_scales(i, b)
         sort_words(0, 1, "gpsimd")
         sort_words(1, 1, "gpsimd")
         for g in range(3):
@@ -172,7 +165,7 @@ def tile_list_rvq_gelu_none_kernel(tc, tab_words, tab_scales, w0_words, w0_scale
 
         def bank(name, width=512, at=None):
             if at is None:
-                at = next_bank[0] % 7
+                at = next_bank[0] % 6
                 next_bank[0] = next_bank[0] + 1
             return psum.tile([P, width], F32, name=name, tag="bank%d" % at)
 
@@ -185,7 +178,7 @@ def tile_list_rvq_gelu_none_kernel(tc, tab_words, tab_scales, w0_words, w0_scale
                     nc.tensor.matmul_mx(
                         out=accs[t // per_bank][:, e * width : (e + 1) * width],
                         lhsT=w[g, b][:, 128 * t : 128 * (t + 1)].bitcast(FP8X4),
-                        lhsT_scale=ws[b, t][4 * (g + 1) : P, :],
+                        lhsT_scale=ws[g // 2, b][4 * (g + 1) : P, 128 * t : 128 * (t + 1)],
                         rhs=gw[q, g][:, j0 : j0 + width].bitcast(FP8X4),
                         rhs_scale=gs[q // 2, g][:, s0 : s0 + width],
                         start=(g == whole[0] and e == 0),
@@ -266,10 +259,10 @@ def tile_list_rvq_gelu_none_kernel(tc, tab_words, tab_scales, w0_words, w0_scale
             nc.sync.dma_start(out_v[:, :, j0 : j0 + width], res[:])
 
         idle = bank("idle")
-        for i in range(WARM_PASSES):
+        for g in WARM_PASSES:
             nc.tensor.matmul_mx(
-                out=idle[:], lhsT=w[0, 0][:, 0:128].bitcast(FP8X4), lhsT_scale=gs[0, 0][:, 0:128],
-                rhs=w[0, 0][:].bitcast(FP8X4), rhs_scale=gs[0, 0], start=True, stop=True,
+                out=idle[:], lhsT=w[0, 0][:, 0:128].bitcast(FP8X4), lhsT_scale=gs[0, g][:, 0:128],
+                rhs=w[0, 0][:].bitcast(FP8X4), rhs_scale=gs[0, g], start=True, stop=True,
             )
         next_bank[0] = 0
 
@@ -334,13 +327,13 @@ def tile_list_rvq_gelu_none_kernel(tc, tab_words, tab_scales, w0_words, w0_scale
         quantise(gh[:], "3", QUARTER)
 
         for q in range(3):
-            y = bank("y%d" % q, at=(2, 0, 1)[q])
+            y = bank("y%d" % q, at=(6, 4, 5)[q])
             for b in range(2):
                 key, c0 = ("0%d" % b, QUARTER * q) if q < 2 else ("2", QUARTER * b)
                 for nt in range(2):
                     second_pass(y[:, nt * QUARTER : (nt + 1) * QUARTER], key, c0, QUARTER, b, nt, b == 0 and nt == 0, b == 1 and nt == 1)
             store(y, QUARTER * q, QUARTER, "scalar")
-        ys = [bank("ylast%d" % nt, QUARTER, at=3 + nt) for nt in range(2)]
+        ys = [bank("ylast%d" % nt, QUARTER, at=nt) for nt in range(2)]
         for b in range(2):
             for nt in range(2):
                 second_pass(ys[nt][:], "3", QUARTER * b, QUARTER, b, nt, b == 0, b == 1)

from contextlib import ExitStack

import concourse.mybir as mybir

K, R, N, T, J = 512, 1024, 256, 4096, 1024
FLOPS = 2 * 3 * K * R * J + 2 * R * N * J

F32 = mybir.dt.float32
BF16 = mybir.dt.bfloat16
I32 = mybir.dt.int32
U32 = mybir.dt.uint32
U16 = mybir.dt.uint16
U8 = mybir.dt.uint8
FP8X4 = mybir.dt.float8_e4m3fn_x4
FP4X4 = mybir.dt.float4_e2m1fn_x4
GELU = mybir.ActivationFunctionType.Gelu_apprx_tanh
COPY = mybir.ActivationFunctionType.Copy
MULT = mybir.AluOpType.mult

P = 128
HALF = 512
QUARTER = 256
EIGHTH = 128
WARM_PASSES = (0, 0, 1, 1, 2)
TAB_EARLY = 256
TAB_PIECES = ((TAB_EARLY, 2304), (2304, T))


def tile_list_rvq_gelu_none_kernel(tc, tab_words, tab_scales, w0_words, w0_scales, w1_words, w1_scales,
        w2_words, w2_scales, sm, wd_words, wd_scales, offs, out):
    nc = tc.nc
    w_words = (w0_words, w1_words, w2_words)
    w_scales = (w0_scales, w1_scales, w2_scales)
    with ExitStack() as ctx:
        keep = ctx.enter_context(tc.tile_pool(name="keep", bufs=1))
        lay = ctx.enter_context(tc.tile_pool(name="lay", bufs=1))
        psum = ctx.enter_context(tc.psum_pool(name="psum", bufs=1))

        def tile(shape, dtype, name):
            return keep.tile(shape, dtype, name=name, align_bytes=256)

        def placed(shape, dtype, name, offset):
            return lay.tile(shape, dtype, name=name, offset=offset, align_bytes=256)

        at_tab = 0
        base0 = 4 * T
        at_w = {(0, 1): base0 + 4096, (1, 0): base0 + 6144, (1, 1): base0 + 8192, (2, 1): base0 + 10240, (0, 0): base0 + 12032, (2, 0): base0 + 13824}
        at_sm = base0 + 12288
        at_ws = base0 + 21504
        at_act = at_ws + 2048
        at_hb = at_act + 4096
        at_last = at_hb + 8192

        offsets = keep.tile([P, 3 * J // 16], U16, name="offsets")
        nc.sync.dma_start(offsets[:], offs)

        tab_plane = tile([P, T], U8, "tab_plane")
        ws_both = placed([P, 2 * R], U8, "ws_both", at_ws)
        ws_raw = [ws_both[:, 0:R], ws_both[:, R : 2 * R]]
        tab = placed([P, T], I32, "tab", at_tab)
        zeros = tab[:].rearrange("p (a c) -> p a c", c=1024)[:, :, 1016:1024]
        nc.gpsimd.memset(tab_plane[:, 0 : T // 2].bitcast(I32), 0)
        nc.gpsimd.memset(zeros, 0)
        nc.vector.memset(tab_plane[:, T // 2 : T].bitcast(I32), 0)
        ident = tile([P, P], F32, "ident")
        nc.vector.memset(ident[:], 0.0)
        for b in range(2):
            nc.vector.memset(ident[0 : 31 + b, b : b + 1], 1.0)
            nc.vector.memset(ident[0 : 30 + b, b : b + 1], 0.0)
        nc.vector.tensor_copy(ws_both[:].bitcast(I32).rearrange("p (a r c) -> p a r c", a=4, c=8), zeros.unsqueeze(2).to_broadcast([P, 4, 16, 8]))
        warm = tile([P, 2], F32, "warm")
        nc.gpsimd.memset(warm[:, 0:1], 0.0)
        nc.scalar.activation(warm[:, 1:2], warm[:, 0:1], GELU)
        sm_rows = tile([P, HALF], F32, "sm_rows")
        for lo, hi in ((0, 30), (32, 64), (64, P)):
            nc.scalar.activation(sm_rows[lo:hi, :], warm[lo:hi, 0:1].to_broadcast([hi - lo, HALF]), COPY)

        w_raw = {}
        for name, halves in (("w_first", ((0, 0),)), ("w_low", ((0, 1), (1, 0), (1, 1), (2, 1))), ("w_high", ((2, 0),))):
            raw = placed([P, 512 * len(halves)], I32, name, at_w[halves[0]])
            for i, key in enumerate(halves):
                w_raw[key] = raw[:, 512 * i : 512 * (i + 1)]

        def load_w(g, b):
            nc.sync.dma_start(w_raw[g, b], w_words[g][0].rearrange("p r i -> p (r i)")[:, 2048 * b : 2048 * (b + 1)].bitcast(I32))

        def load_w_scales(eng, rows):
            for g, q in rows:
                row = 32 * q + 4 * (g + 1)
                eng.dma_start(ws_raw[g // 2][row : row + 4, :].bitcast(I32), w_scales[g][0, 4 * q : 4 * q + 4, :].bitcast(I32))

        rows = [(g, q) for q in range(4) for g in range(2)] + [(2, q) for q in range(4)]
        load_w(0, 0)
        words = tab_words[0].rearrange("p t i -> p (t i)").bitcast(I32)
        nc.sync.dma_start(tab[:, 0:TAB_EARLY], words[:, 0:TAB_EARLY])
        nc.sync.dma_start(sm_rows[30:32, :], sm.rearrange("(b m) -> b m", b=2))
        for r in range(4):
            nc.sync.dma_start(tab_plane[r:P:32, :].bitcast(I32), tab_scales[0, r:16:4, :].bitcast(I32))
        load_w_scales(nc.gpsimd, rows[0:1] + rows[8:10])
        load_w_scales(nc.sync, rows[1:2])
        for (lo, hi), behind in zip(TAB_PIECES, (rows[2:8], rows[10:12])):
            nc.sync.dma_start(tab[:, lo:hi], words[:, lo:hi])
            load_w_scales(nc.sync, behind)
        load_w(1, 0)
        load_w(2, 0)
        sm_t = placed([P, 2, 4], F32, "sm_t", at_sm)
        nc.sync.dma_start(sm_t[:], sm.rearrange("(b p t) -> p b t", b=2, t=4))
        for g in range(3):
            load_w(g, 1)

        gs = {}
        gw = {}

        late_planes = placed([P, 3 * HALF], U8, "late_planes", at_w[2, 0] + 256)
        late_words = placed([P, 3 * QUARTER], U32, "late_words", at_w[2, 0] + 1792)

        def gather_plane(half, g):
            gs[half, g] = late_planes[:, HALF * g : HALF * (g + 1)] if half else tile([P, HALF], U8, "gs%d" % g)[:]
            c0 = (J * g + HALF * half) // 16
            nc.vector.tensor_copy(gs[half, g], tab_plane[:].indirect(offsets[:, c0 : c0 + HALF // 16]))

        late = ((2, 0), (2, 1), (2, 2))

        def gather_words(q, g):
            if (q, g) in late:
                gw[q, g] = late_words[:, QUARTER * late.index((q, g)) : QUARTER * (late.index((q, g)) + 1)]
            else:
                gw[q, g] = keep.tile([P, QUARTER], U32, name="gw%d%d" % (q, g), tag="gw%d%d" % (q % 3, g), align_bytes=256)[:]
            c0 = (J * g + QUARTER * q) // 16
            nc.vector.tensor_copy(gw[q, g], tab[:].bitcast(U32).indirect(offsets[:, c0 : c0 + QUARTER // 16]))

        w = {}

        def sort_words(g, b, on):
            w[g, b] = tile([P, 512], U32, "w%d%d" % (g, b))
            dst = w[g, b][:].rearrange("p (t c i) -> p c t i", t=4, i=4)
            src = w_raw[g, b].bitcast(U32).rearrange("p (c i t) -> p c t i", t=4, i=4)
            if on == "scalar":
                nc.scalar.copy(dst, src)
            else:
                nc.gpsimd.tensor_copy(dst, src)

        ws = {}

        def sort_scales(i, b):
            ws[i, b] = tile([P, HALF], U8, "ws%d%d" % (i, b))
            nc.gpsimd.tensor_copy(ws[i, b][:].rearrange("p (t m) -> p t m", t=4), ws_raw[i][:, HALF * b : HALF * (b + 1)].rearrange("p (m t) -> p t m", t=4))

        for g in range(3):
            gather_plane(0, g)
        for q, g in ((0, 0), (0, 1), (0, 2), (1, 2), (1, 1), (1, 0)):
            gather_words(q, g)
        for g in range(3):
            sort_words(g, 0, "scalar")
        for i in range(2):
            for b in range(2):
                sort_scales(i, b)
        sort_words(0, 1, "gpsimd")
        sort_words(1, 1, "gpsimd")
        for g in range(3):
            gather_plane(1, g)
            gather_words(2, g)

        next_bank = [0]

        def bank(name, width=512, at=None):
            if at is None:
                at = next_bank[0] % 6
                next_bank[0] = next_bank[0] + 1
            return psum.tile([P, width], F32, name=name, tag="bank%d" % at)

        def first_layer(accs, q, b, j0, width, order, whole=(0, 1, 2)):
            per_bank = 4 // len(accs)
            s0 = QUARTER * (q % 2) + j0
            for g in order:
                for t in range(4):
                    e = t % per_bank
                    nc.tensor.matmul_mx(
                        out=accs[t // per_bank][:, e * width : (e + 1) * width],
                        lhsT=w[g, b][:, 128 * t : 128 * (t + 1)].bitcast(FP8X4),
                        lhsT_scale=ws[g // 2, b][4 * (g + 1) : P, 128 * t : 128 * (t + 1)],
                        rhs=gw[q, g][:, j0 : j0 + width].bitcast(FP8X4),
                        rhs_scale=gs[q // 2, g][:, s0 : s0 + width],
                        start=(g == whole[0] and e == 0),
                        stop=(g == whole[2] and e == per_bank - 1),
                    )

        def wide_unit(q, b, order=(0, 1, 2), cuts=1):
            shape, name = [P, 2, QUARTER, 2], "act%d%d" % (q, b)
            act = placed(shape, F32, name, at_act) if (q, b) == (0, 1) else tile(shape, F32, name)
            accs = [bank("a%d%d%d" % (q, b, u)) for u in range(2)]
            first_layer(accs, q, b, 0, QUARTER, order, order)
            step = QUARTER // cuts
            for lo in range(0, QUARTER, step):
                for u in range(2):
                    nc.scalar.activation(act[:, u, lo : lo + step, :], accs[u][:].rearrange("p (e j) -> p j e", e=2)[:, lo : lo + step, :], GELU)
            return act[:].rearrange("p u j e -> p j u e")

        def narrow_gelu(act, acc):
            nc.scalar.activation(act, acc[:].rearrange("p (t j) -> p j t", t=4), GELU)

        def pairs(act):
            return act.rearrange("p j (u e) -> p j u e", u=2)

        sm_bank = bank("sm_bank", at=7)
        for t in range(4):
            nc.tensor.transpose(sm_bank[:, P * t : P * (t + 1)], sm_rows[:, t:HALF:4], ident[:])
        factors = {"gpsimd": sm_t[:], "vector": sm_bank[:].rearrange("p (t c) -> p c t", t=4)}
        engines = {"gpsimd": nc.gpsimd, "vector": nc.vector}

        def smooth(on, act, b, lo, hi, hb):
            engines[on].tensor_tensor(
                hb.rearrange("p (j u e) -> p j u e", u=2, e=2),
                act[:, lo:hi, :, :],
                factors[on][:, b, :].rearrange("p (u e) -> p u e", u=2).unsqueeze(1).to_broadcast([P, hi - lo, 2, 2]),
                MULT,
            )

        def smooth_narrow(on, act, b, hb):
            places = act.shape[1]
            engines[on].tensor_tensor(hb.rearrange("p (j t) -> p j t", t=4), act, factors[on][:, b, :].unsqueeze(1).to_broadcast([P, places, 4]), MULT)

        def smooth_scalar(act, b, lo, hi, hb, name):
            hp = tile([P, 4, hi - lo], BF16, name)
            for t in range(4):
                nc.scalar.activation(hp[:, t, :], act[:, lo:hi, t // 2, t % 2], COPY, scale=sm_t[:, b, t : t + 1])
            nc.scalar.copy(hb.rearrange("p (c i t) -> p c t i", i=4, t=4), hp[:].rearrange("p t (c i) -> p c t i", i=4))

        codes = {key: tile([P, HALF], U32, "codes%s" % key) for key in ("00", "01")}
        planes = {"0%d" % b: placed([P, HALF], U8, "plane0%d" % b, at_act + HALF * b) for b in range(2)}
        codes["2"] = tile([P, HALF], U32, "codes2")
        codes["3"] = placed([P, HALF], U32, "codes3", at_last)
        for key in ("2", "3"):
            planes[key] = tile([P, HALF], U8, "plane%s" % key)

        def quantise(hb, key, c0):
            width = hb.shape[1] // 4
            nc.vector.quantize_mx(out=codes[key][:, c0 : c0 + width].bitcast(FP8X4), scales=planes[key][:, c0 : c0 + width], in_=hb)

        def second_pass(y, key, c0, width, b, nt, start, stop):
            nc.tensor.matmul_mx(
                out=y,
                lhsT=wd[:, 512 * b + 256 * nt : 512 * b + 256 * (nt + 1)].bitcast(FP4X4),
                lhsT_scale=wd_plane[:, 256 * b + 128 * nt : 256 * b + 128 * (nt + 1)],
                rhs=codes[key][:, c0 : c0 + width].bitcast(FP8X4),
                rhs_scale=planes[key][:, c0 : c0 + width],
                start=start,
                stop=stop,
            )

        out_v = out.rearrange("(nt p) j -> p nt j", p=P)

        def store(y, j0, width, on):
            res = tile([P, 2, width], F32, "res%d" % j0)
            if on == "scalar":
                nc.scalar.copy(res[:], y[:].rearrange("p (nt j) -> p nt j", nt=2))
            else:
                nc.vector.tensor_copy(res[:], y[:].rearrange("p (nt j) -> p nt j", nt=2))
            nc.sync.dma_start(out_v[:, :, j0 : j0 + width], res[:])

        idle = bank("idle")
        for g in WARM_PASSES:
            nc.tensor.matmul_mx(
                out=idle[:], lhsT=w[0, 0][:, 0:128].bitcast(FP8X4), lhsT_scale=gs[0, g][:, 0:128],
                rhs=w[0, 0][:].bitcast(FP8X4), rhs_scale=gs[0, g], start=True, stop=True,
            )
        next_bank[0] = 0

        hb_first = [placed([P, 4 * HALF], BF16, "hb_first%d" % b, at_hb + 4096 * b) for b in range(2)]

        def part(hb, i, count=1):
            return hb[:, 4 * EIGHTH * i : 4 * EIGHTH * (i + count)]

        first = {j0: bank("first%d" % j0) for j0 in (0, EIGHTH)}
        for g in range(2):
            for j0 in first:
                first_layer([first[j0]], 0, 0, j0, EIGHTH, (g,))
        for j0 in first:
            first_layer([first[j0]], 0, 0, j0, EIGHTH, (2,))
            act = tile([P, EIGHTH, 4], F32, "first_act%d" % j0)
            narrow_gelu(act[:], first[j0])
            smooth_narrow("gpsimd", act[:], 0, part(hb_first[0], j0 // EIGHTH))
        sort_words(2, 1, "scalar")
        act = wide_unit(1, 0, (2, 1, 0))
        smooth("gpsimd", act, 0, 0, EIGHTH, part(hb_first[0], 2))
        smooth_scalar(act, 0, EIGHTH, QUARTER, part(hb_first[0], 3), "hp10")
        act = wide_unit(0, 1, cuts=2)
        for lo in (0, EIGHTH):
            smooth("gpsimd", act, 1, lo, lo + EIGHTH, part(hb_first[1], lo // EIGHTH))
        wd = placed([P, 2 * 2 * N], U8, "wd", at_w[0, 1] + 256)
        nc.sync.dma_start(wd[:].bitcast(I32).rearrange("p (a c) -> p a c", a=2), wd_words.bitcast(I32).rearrange("a p c -> p a c"))
        wd_plane = placed([P, 2 * N], U8, "wd_plane", at_ws)
        nc.gpsimd.memset(wd_plane[:].bitcast(I32), 0)
        for q in range(4):
            nc.sync.dma_start(
                wd_plane[32 * q : 32 * q + 4, :].bitcast(I32).rearrange("p (a c) -> p a c", a=2),
                wd_scales[:, 4 * q : 4 * q + 4, :].bitcast(I32).rearrange("a r c -> r a c"),
            )
        for g in range(3):
            gather_words(3, g)
        act11 = wide_unit(1, 1)
        smooth_scalar(act11, 1, 0, EIGHTH, part(hb_first[1], 2), "hp11")
        smooth("vector", act11, 1, EIGHTH, QUARTER, part(hb_first[1], 3))
        for b in range(2):
            quantise(hb_first[b][:], "0%d" % b, 0)

        acts = [wide_unit(q, b) for q, b in ((2, 0), (2, 1), (3, 0))]
        for j0 in (0, EIGHTH):
            acc = bank("n%d" % j0)
            first_layer([acc], 3, 1, j0, EIGHTH, (0, 1, 2))
            act = tile([P, EIGHTH, 4], F32, "nact%d" % j0) if j0 else placed([P, EIGHTH, 4], F32, "nact0", at_last)
            narrow_gelu(act[:], acc)
            acts.append(act[:])
        ab = placed([P, 8 * EIGHTH], BF16, "ab", at_hb)
        cd = placed([P, 8 * EIGHTH], BF16, "cd", at_hb + 4096)
        smooth("vector", acts[0], 0, 0, QUARTER, ab[:])
        smooth("gpsimd", acts[1], 1, 0, EIGHTH, part(cd, 0))
        smooth("vector", acts[1], 1, EIGHTH, QUARTER, part(cd, 1))
        quantise(ab[:], "2", 0)
        quantise(cd[:], "2", QUARTER)
        ef = placed([P, 8 * EIGHTH], BF16, "ef", at_hb)
        gh = placed([P, 8 * EIGHTH], BF16, "gh", at_hb + 4096)
        smooth("vector", acts[2], 0, 0, QUARTER, ef[:])
        smooth_narrow("gpsimd", acts[3], 1, part(gh, 0))
        smooth_narrow("vector", acts[4], 1, part(gh, 1))
        quantise(ef[:], "3", 0)
        quantise(gh[:], "3", QUARTER)

        for q in range(3):
            y = bank("y%d" % q, at=(6, 4, 5)[q])
            for b in range(2):
                key, c0 = ("0%d" % b, QUARTER * q) if q < 2 else ("2", QUARTER * b)
                for nt in range(2):
                    second_pass(y[:, nt * QUARTER : (nt + 1) * QUARTER], key, c0, QUARTER, b, nt, b == 0 and nt == 0, b == 1 and nt == 1)
            store(y, QUARTER * q, QUARTER, "scalar")
        ys = [bank("ylast%d" % nt, QUARTER, at=nt) for nt in range(2)]
        for b in range(2):
            for nt in range(2):
                second_pass(ys[nt][:], "3", QUARTER * b, QUARTER, b, nt, b == 0, b == 1)
        for nt in range(2):
            res = tile([P, QUARTER], F32, "res_last%d" % nt)
            if nt == 0:
                nc.scalar.copy(res[:], ys[nt][:])
            else:
                nc.vector.tensor_copy(res[:], ys[nt][:])
            nc.sync.dma_start(out_v[:, nt, 3 * QUARTER : J], res[:])
